import numpy as np, ml_dtypes
CORES = [35,38,43,46]
N = 4
BF = ml_dtypes.bfloat16
def gentries(a):
    return np.ascontiguousarray(a.reshape(8, 16, -1).transpose(0, 2, 1)).reshape(8, -1)
def gtable(e):
    e = np.asarray(e); return np.ascontiguousarray(e.reshape(8, -1, 16).transpose(0, 2, 1)).reshape(128, -1).astype(np.int32)
V, G, BL, K, CAP, HO, RO = 3072, 512, 768, 1024, 256, 2, 3
W = V + G; CL = RO + 1; OWN = np.arange(V); LO = BL * (OWN // BL + 1)
def glists(a):
    return np.stack([gentries(x) for x in a]).astype(np.int64)
def pick(x, i):
    return np.take_along_axis(x, i[:, :, None, :], 3)
def reals(rng, top):
    return (0.5 + (top - 0.5) * rng.random((N, 8, 16, V))) * np.exp2(rng.integers(-1, 2, (N, 8, 1, V)))
def later(rng):
    r = rng.random((N, 8, V)); r = np.where(rng.random((N, 8, V)) < 0.5, r, r * r * r)
    return np.minimum(LO + ((W - LO) * r).astype(np.int64), W - 1)
def parts(rng):
    d = dict(a=rng.integers(-127, 128, (N, 8, 16, V)), b=rng.integers(-127, 128, (N, 8, 16, V)), h=reals(rng, 1.0), u=rng.integers(0, 256, (N, 8, 16, K)), v=rng.integers(0, 256, (N, 8, 16, K)))
    d["n0"] = later(rng); d["n1"] = later(rng); d["s"] = rng.integers(0, K, (N, 8, V))
    share = rng.permutation(np.array([0.1, 0.1, 0.2, 0.2, 0.35, 0.35, 0.5, 0.5])).reshape(1, 8, 1)
    d["f"] = np.where(rng.random((N, 8, K)) < share, rng.integers(V, W, (N, 8, K)), rng.integers(0, V, (N, 8, K)))
    d["th"] = rng.integers(60, 111, (N, 8, 1, RO)) + rng.integers(-15, 16, (N, 8, 16, RO))
    return d
def pack(d):
    o = {}
    for k, x, n in (("ta", "a", V), ("tb", "b", V), ("h0", "h", V), ("u0", "u", K), ("v0", "v", K)):
        o[k] = np.ascontiguousarray(d[x].reshape(N, 128, n)).astype(np.float32).astype(BF)
    for k, x in (("na", "n0"), ("nb", "n1"), ("sd", "s"), ("pf", "f")): o[k] = np.stack([gtable(e) for e in d[x]])
    o["th"] = np.ascontiguousarray(d["th"].reshape(N, 128, RO)).astype(np.int32)
    return o
def setup_inputs(rng):
    return pack(parts(rng))
def setup_inputs_spread(rng):
    d = parts(rng); d["h"] = reals(rng, 2.0)
    d["u"] = (256 * rng.random((N, 8, 16, K)) ** rng.integers(1, 5, (N, 8, 1, K))).astype(np.int64)
    d["u"] = np.minimum(d["u"], 255)
    d["th"] = np.clip(rng.choice(np.array([5, 40, 80, 120, 250]), (N, 8, 1, RO)) + rng.integers(-40, 41, (N, 8, 16, RO)), 0, 255)
    return pack(d)
def setup_inputs_ends(rng):
    d = parts(rng)
    def two(lo, hi, n):
        e = rng.integers(0, 2, (N, 8, 16, n)); r = rng.integers(0, 2, (N, 8, 1, n))
        return np.where(np.where(rng.random((N, 8, 1, n)) < 0.5, r, e) == 1, hi, lo)
    d["a"] = two(-127, 127, V); d["b"] = two(-127, 127, V); d["h"] = two(0.25, 4.0, V); d["u"] = two(0, 255, K); d["v"] = two(0, 255, K); d["th"] = two(0, 255, RO)
    for k in ("n0", "n1"): d[k] = np.where(rng.random((N, 8, V)) < 0.75, W - 1, LO)
    d["s"] = np.where(rng.random((N, 8, V)) < 0.5, 0, K - 1)
    d["f"] = np.where(rng.random((N, 8, K)) < 0.7, np.where(rng.random((N, 8, K)) < 0.5, 0, W - 1), rng.integers(0, W, (N, 8, K)))
    d["th"][:, 0] = 255; d["th"][:, 6:, :, 0] = 255
    for g, s, w in ((7, 127, 255), (6, -127, 0)):
        d["a"][:, g, :, 0] = s; d["a"][:, g, :, V - 1] = s; d["b"][:, g, :, 0] = s
        for p in (1, K - 1): d["u"][:, g, :, p] = w; d["v"][:, g, :, p] = 255; d["f"][:, g, p] = 0
    d["n1"][:, 6:, 0] = BL
    L = V - 1 - (V - RO) % CL; d["th"][:, 6:, :, RO - 1] = 255
    for g, s, w in ((7, 127, 255), (6, -127, 0)):
        d["a"][:, g, :, L] = 0; d["b"][:, g, :, L] = s
        d["u"][:, g, :, K - 2] = 255; d["v"][:, g, :, K - 2] = w; d["f"][:, g, K - 2] = L
    return pack(d)
def setup_inputs_corners(rng):
    d = parts(rng); rest = OWN[OWN % CL == RO]; far = V + np.arange(RO, G, CL)
    n = np.array([0, 1, CAP - 1, CAP, CAP + 1, K, RO * CAP - 1, CAP])
    for g in range(8):
        q = int(rng.integers(N))
        for r in range(N):
            k = int(n[g])
            if r != q: k = K if g == 6 else int(rng.choice(np.array([k, min(k + 1, K), K])))
            if g == 6: gh = rng.choice(far, k)
            else: gh = np.where(rng.random(k) < 0.5, rng.integers(V, W, k), rng.choice(np.array([V, W - 1]), k))
            d["f"][r, g] = rng.permutation(np.concatenate([gh, rng.choice(rest, K - k)]))
    d["s"][:, 2] = K - 1; d["s"][:, 4] = K - 1; d["s"][:, 4, 0] = 0; d["s"][:, 3] = rng.choice(np.array([0, 1, K - 2, K - 1]), (N, V))
    t = rng.integers(20, 101, (N, 8, 16, 1)); d["th"] = np.repeat(t, RO, axis=3)
    c = rng.choice(np.array([0, 1, 8, 9, 15, 16]), (N, 8, 1, V)); at = (np.argsort(rng.random((N, 8, 16, V)), axis=2) < c).astype(np.int64)
    e = t + 1 - at; x = pick(d["u"], d["s"]) - 128
    d["a"] = np.where(x - e >= -127, x - e, x + e)
    return pack(d)
def setup_inputs_calm(rng):
    d = parts(rng); rest = OWN[OWN % CL == RO]; far = V + np.arange(RO, G, CL)
    c = ((0, 1, 2, 3, 0, 0, 1, 2), (0, 0, 0, 0, 1, 2, 1, 1), (0, 1, 0, 0, 0, 1, 1, 0))
    d["f"][..., :16] = rng.choice(far, (N, 8, 16))
    for g in range(8):
        q = int(rng.integers(N)); w = rng.choice(rest, K); at = rng.permutation(K); j = c[0][g]
        w[at[:j]] = rng.choice(far, j)
        for t in range(1, RO):
            k = c[t][g]; e = rng.choice(OWN[OWN % CL == t], k); w[at[j:j + k]] = e; j += k
            d["n0"][q, g, e] = rng.choice(far, k); d["n1"][q, g, e] = rng.choice(far, k); d["th"][q, g, :, t] = 255
        d["f"][q, g] = w
    return pack(d)
def setup_inputs_chains(rng):
    d = parts(rng); nxt = LO + (OWN - LO) % CL
    d["n0"][:, :4] = nxt; d["n1"][:, 2:6] = nxt; d["th"][:, ::2] = 255; d["th"][:, 5] = 0
    d["f"] = np.where(rng.random((N, 8, K)) < 0.6, rng.integers(0, BL, (N, 8, K)), d["f"])
    z = rng.random((N, 8, 1, V)) < 0.33; d["a"] = np.where(z, 0, d["a"]); d["b"] = np.where(z, 0, d["b"])
    c = rng.choice(np.array([0, 8, 9, 16]), (N, 8, 1, K)); tie = (np.argsort(rng.random((N, 8, 16, K)), axis=2) < c).astype(np.int64)
    d["u"] = np.minimum(d["u"], 254); d["v"] = np.where(rng.random((N, 8, 1, K)) < 0.5, d["u"] + 1 - tie, d["v"])
    d["f"][:, 4] = 0; d["f"][:, 4, K - 1] = V - 1
    d["s"][:, 1] = 0; d["s"][:, 3] = K - 1; d["s"][:, 3, V - 1] = 0
    return pack(d)
def check_ranges(d):
    bad = []
    for k, lo, hi in (("ta", -127, 127), ("tb", -127, 127), ("u0", 0, 255), ("v0", 0, 255), ("na", BL, W - 1), ("nb", BL, W - 1), ("sd", 0, K - 1), ("pf", 0, W - 1), ("th", 0, 255)):
        x = np.asarray(d[k]).astype(np.float64)
        if not np.all((x >= lo) & (x <= hi) & (x == np.floor(x))): bad.append("range of " + k)
    y = np.asarray(d["h0"]).astype(np.float64)
    if not np.all((y >= 0.25) & (y <= 4)): bad.append("range of h0")
    for k in ("na", "nb"):
        if not np.all(glists(d[k]) >= LO): bad.append("blocks of " + k)
    return bad
def reference(ta, tb, h0, u0, v0, na, nb, sd, pf, th):
    a = ta.astype(np.float32).astype(np.int64).reshape(N, 8, 16, V); b = tb.astype(np.float32).astype(np.int64).reshape(N, 8, 16, V)
    u = u0.astype(np.float32).astype(np.int64).reshape(N, 8, 16, K); v = v0.astype(np.float32).astype(np.int64).reshape(N, 8, 16, K)
    h = h0.astype(np.float64).reshape(N, 8, 16, V); limit = th.astype(np.int64).reshape(N, 8, 16, RO)
    n0, n1, s, face = glists(na), glists(nb), glists(sd), glists(pf)
    dead = np.zeros((N, 8, W), bool); shift = np.zeros(8, np.int64)
    for t in range(RO):
        w = np.concatenate([h, np.roll(h, -1, axis=0)[..., :G]], axis=3)
        x = pick(u, (s + shift[None, :, None]) & (K - 1))
        count = np.add.reduce((np.abs(x - 128 - a) <= limit[..., t:t + 1]).astype(np.int64), axis=2)
        dead[..., :V] |= (OWN % CL == t) & (count >= 9)
        for hop in range(HO):
            go = np.take_along_axis(dead, face, 2); fi = np.minimum(face, V - 1)
            un = (u + pick(a, fi) * v) & 255; vn = (v + pick(b, fi) * un) & 255
            u = np.where(go[:, :, None, :], un, u); v = np.where(go[:, :, None, :], vn, v)
            count = np.add.reduce((u >= v).astype(np.int64), axis=2)
            to = np.where(count >= 9, np.take_along_axis(n0, fi, 2), np.take_along_axis(n1, fi, 2))
            face = np.where(go, to, face)
        on = face >= V
        m = np.minimum(np.min(np.add.reduce(on.astype(np.int64), axis=2), axis=0), CAP)
        nu, nv, nf = u.copy(), v.copy(), face.copy()
        for g in range(8):
            at = [np.flatnonzero(on[r, g])[:int(m[g])] for r in range(N)]
            for r in range(N):
                e = (r + 1) % N
                nu[e, g][:, at[e]] = u[r, g][:, at[r]]; nv[e, g][:, at[e]] = v[r, g][:, at[r]]; nf[e, g, at[e]] = face[r, g, at[r]] - V
        u, v, face = nu, nv, nf; shift = shift + m
        x = pick(u, (s + shift[None, :, None]) & (K - 1))
        w[..., :V] = 0.5 * (h + x * 0.015625 - 2.0)
        for k in range(V // BL - 1, -1, -1):
            c = slice(k * BL, (k + 1) * BL)
            y = (a[..., c] * pick(w, n0[..., c]) + b[..., c] * pick(w, n1[..., c])) * 0.00390625
            w[..., c] = np.where(dead[:, :, None, c], y, w[..., c])
        h = w[..., :V]
    z = ((u - 128) * (v - 128)) * 2.0 ** -13
    p = pick(w, face) * (0.5 * (1.0 + np.tanh(0.5 * z)))
    yh = np.add.reduce(h.reshape(N, 8, 16, V // BL, BL), axis=3)
    return {"yh": yh.reshape(N, 128, BL).astype(np.float32), "yw": (p[..., :K // 2] + p[..., K // 2:]).reshape(N, 128, K // 2).astype(np.float32)}

def check_inputs(d):
    bad = list(check_ranges(d))
    if not bad:
        for name, y in reference(**d).items():
            for q in range(N):
                v = np.abs(np.asarray(y[q], np.float64)); s = np.sqrt(np.mean(v * v))
                if v.max() > 8 * s or s < 2.0 ** -3: bad.append('%s of rank %d is uneven or too small' % (name, q))
    return bad

@@ -1,0 +1,748 @@
+import math
+import numpy
+from concourse.bass import DstId, RemoteDMATransfer
+from concourse.mybir import AluOpType, AxisListType, ActivationFunctionType
+
+F32, BF, I32, U16 = "float32", "bfloat16", "int32", "uint16"
+NV, NW, BL, K = 3072, 3584, 768, 1024
+VO = 1280
+UV = ("uv", "uv0", "uv", "uv0")
+MAGIC = 1.5 * 2.0 ** 31
+
+
+def _sb(n, d):
+    return ("sbuf", [128, n], d)
+
+
+SCRATCH = {
+    "ps": ("psum", [128, 4096], F32),
+    "a": _sb(NV, BF), "b": _sb(NV, BF), "h": _sb(NV, BF),
+    "uv": _sb(2 * VO, BF), "uv0": _sb(2 * VO, BF), "uw": _sb(2 * VO, BF), "mq": _sb(K, BF), "hc": _sb(512, BF), "idh": _sb(128, BF),
+    "nab": _sb(384, I32), "sdi": _sb(192, I32), "pfi": _sb(64, I32), "thi": _sb(4, I32),
+    "ci": _sb(4, I32), "cf": _sb(16, F32), "cb": _sb(8, BF), "kr": _sb(272, BF), "r16": _sb(128, BF),
+    "q1": _sb(144, BF), "wd": _sb(144, BF), "w0": _sb(144, BF), "w1": _sb(144, BF),
+    "blk": _sb(128, BF), "idb": _sb(128, BF), "id8": _sb(128, BF), "id256": _sb(128, BF), "bs": _sb(3 * BL, BF), "idf": _sb(128, F32),
+    "un": _sb(128, BF), "un0": _sb(128, BF), "i16": _sb(16, F32), "bm": _sb(16 * 144, BF),
+    "kw": _sb(64, F32), "fw": _sb(192, F32), "sf0": _sb(48, F32), "sf": _sb(48, F32),
+    "thf": _sb(8, F32), "shl": _sb(384, BF), "dn": _sb(384, F32), "dhl": _sb(768, BF),
+    "nnc": _sb(3 * BL, BF), "nnd": _sb(NW, BF), "ah": _sb(NW, BF), "bh": _sb(NW, BF), "ee": _sb(3 * BL, BF),
+    "sdf": _sb(288, F32), "si": _sb(240, I32), "sl": _sb(720, U16),
+    "dd": _sb(BL, F32), "c1": _sb(BL, BF), "c2": _sb(BL, BF),
+    "ff": _sb(128, F32), "fu": _sb(64, U16), "sg": _sb(64, F32), "t2": _sb(64, F32),
+    "ga": _sb(K, BF), "gb": _sb(K, BF), "gg": _sb(2 * K, BF), "idn": _sb(128, BF), "zr": _sb(256, F32),
+    "on": _sb(64, BF), "sc": _sb(64, BF), "cc": _sb(136, F32), "rk": _sb(72, F32), "fc": _sb(72, F32),
+    "junk": _sb(K, BF), "acc": _sb(16, F32), "cu": _sb(16, U16), "cx": _sb(16, F32),
+    "le": _sb(256, BF), "eq": _sb(256, BF), "atf": _sb(16, F32), "atu": _sb(16, U16), "asu": _sb(16, U16),
+    "e1": _sb(16, F32), "e2": _sb(16, F32), "e3": _sb(16, F32),
+    "cin": _sb(48, F32), "mm": _sb(12, F32), "ro": _sb(64, U16), "lv": _sb(64, F32), "lv0": _sb(64, F32),
+    "fk": _sb(64, F32), "gf": _sb(K, BF),
+    "snd": _sb(768, BF), "rcv": _sb(3 * 768, BF),
+    "gl0": _sb(512, BF), "gl": _sb(1024, F32),
+    "w": _sb(NW, F32), "x0": _sb(NV, BF), "x1": _sb(NV, BF), "x2": _sb(NV, BF), "us": _sb(K, BF),
+    "nl": _sb(6 * 48, U16), "h1": _sb(3 * 192, F32), "h2": _sb(3 * 192, F32), "p2": _sb(3 * 192, F32),
+    "uc": _sb(K, BF), "sig": _sb(VO, F32), "pa": _sb(512, F32), "hb": _sb(512, F32),
+    "oh": _sb(BL, F32), "ow": _sb(512, F32),
+}
+SEMAPHORES = ["cv", "cs", "cp", "cg"] + ["d%d" % i for i in range(16)] + ["l%d" % i for i in range(12)] + ["r%d" % i for i in range(12)]
+COUNTER = {"v": "cv", "s": "cs", "p": "cp", "g": "cg"}
+
+COST = {"cyc": 1.0, "pe": 0.52, "gat": 1.55, "sca": 3.8, "fix": 60.0, "lat": 120.0, "own": 120.0, "remote": 3200.0, "rissue": 900.0}
+OPT = {"xh": ["AAAA", "AAAA", "AAVV"], "corr": "BBB", "cmp": "SV", "dead": "SS", "ga": "SSSS", "gn": "SSSS", "ge": "SVSV", "pc": 0, "accv": 0, "split": 1, "passes": 5000, "noise": 4000.0, "span": 10000.0, "later": [0.0, 5e3, 1e4, 2e4, 4e4, 1e6], "seed": 1, "pull": 3.0, "warm": 150.0, "dbank": (4, 5)}
+
+
+def build(T, topo, core):
+    ALU, ACT = AluOpType, ActivationFunctionType
+    ops = []
+    fill = [False]
+    rank = T.rank_of(core)
+    n = len(T.cores)
+    cy = COST["cyc"]
+
+    def A(name, lo, hi, step=1):
+        ap = T[name][:, lo:hi] if step == 1 else T[name][:, lo:hi:step]
+        return {"ap": ap, "reg": [(name, lo, hi, step)], "n": (hi - lo + step - 1) // step, "d": SCRATCH[name][2], "ps": name == "ps", "ind": False}
+
+    def P(bank, lo, hi):
+        return A("ps", 512 * bank + lo, 512 * bank + hi)
+
+    def G(win, off):
+        return {"ap": win["ap"].indirect(off["ap"]), "reg": win["reg"], "oreg": off["reg"], "n": 16 * off["n"], "d": win["d"], "ps": False, "ind": True}
+
+    def add(eng, fn, dur, rd, wr, **kw):
+        r, w = [], []
+        for x in rd:
+            if isinstance(x, dict):
+                r += x["reg"] + x.get("oreg", [])
+        for x in wr:
+            w += x["reg"]
+            r += x.get("oreg", [])
+        op = {"eng": eng, "fn": fn, "dur": dur, "rd": r, "wr": w, "kind": "c", "fill": fill[0]}
+        op.update(kw)
+        ops.append(op)
+        return len(ops) - 1
+
+    def ap(x):
+        return x["ap"] if isinstance(x, dict) else x
+
+    def vcost(out, ins, two=False):
+        m = out["n"]
+        if out["ind"]:
+            c = COST["sca"]
+        elif ins[0]["ind"]:
+            c = COST["gat"]
+        elif two:
+            c = 1.0 if any(x["ps"] for x in ins) else 2.0
+        else:
+            c = 0.5 if all(x["d"] in (BF, U16) for x in ins + [out]) else 1.0
+        return COST["fix"] + max(64, m * c) * cy
+
+    def tt(out, i0, i1, op):
+        add("v", lambda q: q.tensor_tensor(out["ap"], i0["ap"], i1["ap"], op), vcost(out, [i0, i1], True), [i0, i1], [out])
+
+    def ts(out, i0, s1, op0, s2=None, op1=None):
+        if op1 is None:
+            fn = lambda q: q.tensor_scalar(out["ap"], i0["ap"], ap(s1), None, op0)
+        else:
+            fn = lambda q: q.tensor_scalar(out["ap"], i0["ap"], ap(s1), ap(s2), op0, op1)
+        add("v", fn, vcost(out, [i0]), [i0, s1, s2], [out])
+
+    def cp(out, i0):
+        add("v", lambda q: q.tensor_copy(out["ap"], i0["ap"]), vcost(out, [i0]), [i0], [out])
+
+    def ms(out, val):
+        add("v", lambda q: q.memset(out["ap"], val), vcost(out, [out]), [], [out])
+
+    def act(out, i0, func=None, bias=0.0, scale=1.0, acc=None, extra=0.0):
+        f = ACT.Identity if func is None else func
+        c = COST["gat"] if i0["ind"] else 1.0
+        if acc is None:
+            fn = lambda q: q.activation(out["ap"], i0["ap"], f, bias=ap(bias), scale=ap(scale))
+        else:
+            fn = lambda q: q.activation(out["ap"], i0["ap"], f, bias=ap(bias), scale=ap(scale), accum_out=acc["ap"])
+        add("s", fn, COST["fix"] + extra + max(64, i0["n"] * c) * cy, [i0, bias, scale], [out] + ([acc] if acc else []))
+
+    def mm(out, pairs, start=True, stop=True):
+        def fn(q):
+            last = None
+            for j, (l, r) in enumerate(pairs):
+                last = q.matmul(out["ap"], l["ap"], r["ap"], start and j == 0, stop and j == len(pairs) - 1)
+            return last
+        dur = 30.0 + sum(max(64, r["n"]) * (4 if r["d"] == F32 else 1) for l, r in pairs) * COST["pe"]
+        add("p", fn, dur, [x for pr in pairs for x in pr], [out])
+
+    def iota(out, pattern, base, cm):
+        if out["d"] == I32:
+            fn = lambda q: q.iota(out["ap"], pattern, base, cm)
+        else:
+            fn = lambda q: q.iota(out["ap"], pattern, base, cm, allow_small_or_imprecise_dtypes=True)
+        add("g", fn, 130.0 + 2 * out["n"] * cy, [], [out])
+
+    nd, nr, bus = [0], [0], [0.0]
+
+    def load(dst, src, eng, nbytes):
+        s = "d%d" % nd[0]
+        nd[0] += 1
+        bus[0] += nbytes * 0.22 - 60.0
+        j = add(eng, lambda q: q.dma_start(dst["ap"], src), 60.0, [], [dst], kind="dma", sem=s, cnt=16, lat=1900.0 + max(bus[0], 0.0))
+        if nd[0] > 1:
+            ops[j]["follow"] = j - 1
+
+    def store(dst, src, eng, nbytes):
+        s = "d%d" % nd[0]
+        nd[0] += 1
+        add(eng, lambda q: q.dma_start(dst, src["ap"]), 60.0, [src], [], kind="dma", sem=s, cnt=16, lat=1900.0 + nbytes * 0.22)
+
+    mask = -1
+    for c in T.cores:
+        if c != core:
+            mask &= topo.mask(core, c)
+    ne = bin(mask).count("1")
+
+    def send(src, dsts, lands, nbytes):
+        ls, rs = "l%d" % nr[0], "r%d" % nr[0]
+        nr[0] += 1
+
+        def fn(q):
+            if len(dsts) == 1:
+                rid, pid, _ = topo.addr(dsts[0][0])
+                return q.remote_dma(dsts[0][1]["ap"], src["ap"], T.sem[rs], T.sem[ls], pid, rid, mask)
+            ids = [DstId(rid=topo.addr(c)[0], pnc=topo.addr(c)[1]) for c, _ in dsts]
+            tr = RemoteDMATransfer(dst_ids=ids, dma_engine_mask=mask, remote_sem=T.sem[rs], srcs=[src["ap"]], dsts=[d["ap"] for _, d in dsts])
+            return q.remote_dma_fused([tr], local_sem=T.sem[ls])
+        lat = COST["remote"] - COST["rissue"] + nbytes * 0.8
+        j = add("g", fn, COST["rissue"], [src], [], kind="send", sem=ls, cnt=ne, lat=lat)
+        add(None, None, 0.0, [], lands, kind="recv", sem=rs, cnt=ne * len(lands), after=j, lat=0.0)
+
+    nxt, prv = T.cores[(rank + 1) % n], T.cores[(rank - 1) % n]
+
+    def sh(name, i, base=0):
+        return A(name, base + 15 - i, base + 143 - i)
+
+    def wrap(out, mat, src, lo, hi, more=()):
+        mm(out, [(sh(mat, i), A(src, lo + i, hi, 16)) for i in range(16)] + list(more))
+
+    load(A("sdi", 0, 192), T.sd[:], "y", 768)
+    load(A("uv", 0, K), T.u0[:], "y", 2048)
+    load(A("a", 0, NV), T.ta[:], "y", 6144)
+    load(A("thi", 0, 3), T.th[:], "y", 200)
+    load(A("nab", 0, 192), T.na[:], "y", 768)
+    load(A("nab", 192, 384), T.nb[:], "y", 768)
+    load(A("pfi", 0, 64), T.pf[:], "y", 256)
+    load(A("uv", VO, VO + K), T.v0[:], "y", 2048)
+    load(A("b", 0, NV), T.tb[:], "y", 6144)
+    load(A("h", 0, NV), T.h0[:], "y", 6144)
+
+    iota(A("ci", 0, 1), [[0, 1]], 0, 1)
+    iota(A("kr", 0, 272), [[1, 272]], 0, 0)
+    iota(A("r16", 0, 128), [[16, 8], [0, 16]], 0, 0)
+    iota(A("sf0", 0, 48), [[0, 4], [64, 12]], 0, 0)
+    rows = len(ops) - 1
+    for j in range(rows - 2, rows + 1):
+        ops[j]["follow"] = j - 1
+    ts(A("ci", 1, 2), A("ci", 0, 1), 15, ALU.bitwise_and)
+    ts(A("ci", 2, 3), A("ci", 0, 1), 112, ALU.bitwise_and)
+    cp(A("cf", 0, 3), A("ci", 0, 3))
+    pc, lane, g16 = A("cf", 0, 1), A("cf", 1, 2), A("cf", 2, 3)
+    ts(A("q1", 0, 144), A("kr", 0, 144), -15.0, ALU.add, g16, ALU.is_equal)
+    ts(A("i16", 0, 16), A("kr", 0, 16), lane, ALU.is_equal)
+    masks = len(ops) - 1
+    for t in range(3):
+        for q in range(4):
+            i = 4 * q + t
+            if t == 0 and q % 2 == 0:
+                ts(A("bm", 144 * i, 144 * i + 144), A("q1", 0, 144), A("i16", i, i + 1), ALU.mult)
+            else:
+                act(A("bm", 144 * i, 144 * i + 144), A("q1", 0, 144), scale=A("i16", i, i + 1))
+    ts(A("blk", 0, 128), A("r16", 0, 128), g16, ALU.is_equal)
+    ts(A("idb", 0, 128), A("kr", 0, 128), pc, ALU.is_equal)
+    act(A("idf", 0, 128), A("idb", 0, 128))
+    act(A("id8", 0, 128), A("idb", 0, 128), scale=0.125)
+    act(A("id256", 0, 128), A("idb", 0, 128), scale=1.0 / 256)
+    ts(A("un0", 0, 128), A("kr", 0, 128), pc, ALU.is_lt, -1.0, ALU.mult)
+    tt(A("un", 0, 128), A("un0", 0, 128), A("blk", 0, 128), ALU.mult)
+    low = A("cb", 0, 1)
+    act(low, lane, ACT.Sigmoid, bias=7.5 * 512, scale=-512.0, extra=1300.0)
+    act(A("cf", 3, 4), low, scale=2.0)
+    act(A("cf", 4, 5), low, bias=2.0, scale=-2.0)
+    act(A("cf", 5, 6), low, bias=-2.0, scale=4.0)
+    act(A("cf", 6, 7), lane, scale=4.0)
+    act(A("idn", 0, 128), A("idb", 0, 128), scale=-1.0)
+    act(A("idh", 0, 128), A("idb", 0, 128), scale=127.5)
+    for lo in (0, VO):
+        ts(A("uv", lo, lo + K), A("uv", lo, lo + K), -127.5, ALU.add)
+    act(A("wd", 0, 144), A("q1", 0, 144), scale=A("cf", 5, 6))
+    act(A("w0", 0, 144), A("q1", 0, 144), scale=A("cf", 3, 4))
+    act(A("w1", 0, 144), A("q1", 0, 144), scale=A("cf", 4, 5))
+    act(A("sf", 0, 48), A("sf0", 0, 48), bias=A("cf", 6, 7))
+    act(A("fw", 0, 192), A("kr", 0, 192), bias=lane, scale=16.0)
+    act(A("kw", 0, 16), A("fw", 0, 16), bias=0.5)
+    act(A("kw", 16, 32), A("fw", 0, 16), bias=1.0)
+    act(A("kw", 32, 48), A("fw", 0, 16), bias=1024.0)
+    idb, idf, blk = A("idb", 0, 128), A("idf", 0, 128), A("blk", 0, 128)
+    for name in ("ah", "bh"):
+        for c in range(4):
+            ms(A(name, 896 * c, 896 * c + 896), 0.0)
+            if name != "ah" or c > 0:
+                ops[-1]["follow"] = masks
+    iota(A("nnd", 0, NW), [[0, NW]], 0, 0)
+    ops[-1]["follow"] = rows
+    ms(A("hc", 0, 512), 127.5)
+    ms(A("ff", 0, 32), 0.0)
+    ms(A("ff", 96, 128), 0.0)
+    ms(A("sig", K, VO), 0.0)
+    for name in ("uv", "uv0"):
+        ms(A(name, K, VO), 0.0)
+        ms(A(name, VO + K, 2 * VO), 0.0)
+    ms(A("cc", 128, 136), 4096.0)
+    ms(A("rk", 64, 72), 0.0)
+    ms(A("fc", 64, 72), 0.0)
+    if OPT["cmp"] == "SV":
+        cp(A("thf", 0, 3), A("thi", 0, 3))
+    else:
+        ts(A("thf", 4, 7), A("thi", 0, 3), 0.5, ALU.add)
+
+    cp(A("shl", 0, 192), A("sdi", 0, 192))
+    tt(A("shl", 192, 384), A("sdi", 0, 192), A("shl", 0, 192), ALU.subtract)
+    tt(A("dn", 0, 192), A("nab", 0, 192), A("fw", 0, 192), ALU.subtract)
+    tt(A("dn", 192, 384), A("nab", 192, 384), A("fw", 0, 192), ALU.subtract)
+    act(A("dhl", 0, 384), A("dn", 0, 384))
+    tt(A("dhl", 384, 768), A("dn", 0, 384), A("dhl", 0, 384), ALU.subtract)
+    cp(A("ff", 32, 96), A("pfi", 0, 64))
+    cp(A("fu", 0, 64), A("pfi", 0, 64))
+    cp(A("sdf", 48, 240), A("sdi", 0, 192))
+
+    def class_lists(t):
+        bank = 4 if t == 0 else 6
+        prs = []
+        for i in range(16):
+            src = 4 * (i % 4) + t
+            for part in (0, 192):
+                prs.append((sh("bm", i, 144 * src), A("shl", part + i // 4, part + 192, 4)))
+        mm(P(bank, 0, 48), prs)
+        if t == 0:
+            cp(A("sl", 672, 720), P(bank, 0, 48))
+        else:
+            act(A("sdf", 240 * t - 240, 240 * t - 192), P(bank, 0, 48))
+        b0 = 0 if t == 0 else 6
+        for q in range(4):
+            i = 4 * q + t
+            o = P(b0 + (q // 2 if t == 0 or OPT["pc"] == 0 else 0), 192 * (q % 2), 192 * (q % 2) + 192)
+            mm(o, [(sh("bm", l, 144 * i), A("dhl", c0, c0 + 192)) for l, c0 in ((0, 0), (1, 384), (8, 192), (9, 576))])
+            act(A("nnc", BL * t + q, BL * t + BL, 4), o, scale=0.5)
+
+    for t in range(3):
+        fill[0] = t > 0
+        class_lists(t)
+    fill[0] = False
+
+    send(A("h", 0, 512), [(prv, A("gl0", 0, 512))], [A("gl0", 0, 512)], 1024)
+
+    first = [False]
+
+    def collapse(t):
+        act(A("bs", BL * t, BL * t + BL), A("b", t, NV, 4), scale=1.0 / 256)
+        for c in range(2):
+            lo, hi = 384 * c, 384 * c + 384
+            o = (672, 0, 432)[t] + 24 * c
+            cls = lambda name: A(name, 4 * lo + t, 4 * hi, 4)
+            dd, c1, c2, d = A("dd", lo, hi), A("c1", lo, hi), A("c2", lo, hi), P(OPT["dbank"][c], 128, 512)
+            tt(dd, G(A(UV[t], 0, K), A("sl", o, o + 24)), cls("a"), ALU.subtract)
+            act(c2, dd, ACT.Abs, bias=-0.5)
+            if OPT["cmp"] == "SV":
+                ts(c1, c2, A("thf", t, t + 1), ALU.is_le)
+            else:
+                act(c1, c2, ACT.Sign, bias=A("thf", 4 + t, 5 + t), scale=-1.0)
+            mm(d, [(blk, c1)])
+            thr = 8.5 if OPT["cmp"] == "SV" else 1.0
+            if OPT["dead"][c] == "S":
+                act(d, d, ACT.Sigmoid, bias=-512.0 * thr, scale=512.0, extra=1300.0 if first[0] else 0.0)
+                first[0] = False
+            else:
+                ts(d, d, thr, ALU.is_ge)
+            tt(cls("ah"), d, cls("a"), ALU.mult)
+            tt(cls("bh"), d, A("bs", BL * t + lo, BL * t + hi), ALU.mult)
+            tt(cls("nnd"), d, A("nnc", BL * t + lo, BL * t + hi), ALU.mult)
+            act(A("ee", BL * t + lo, BL * t + hi), d, bias=1.0, scale=-1.0)
+
+    def hop(t, k, c):
+        lo, hi = 512 * c, 512 * c + 512
+        off = A("fu", 32 * c, 32 * c + 32)
+        gn, ge = A("gg", 512 + lo, 512 + hi), A("gg", 3 * lo, 3 * lo + 512)
+        pa, pb = P(2 * c, 0, 512), P(2 * c + 1, 0, 512)
+        ga, gb, mq = A("ga", lo, hi), A("gb", lo, hi), A("mq", lo, hi)
+        src, dst = (UV[t], "uw") if k == 0 else ("uw", UV[t + 1])
+        ub, vb = A(src, lo, hi), A(src, VO + lo, VO + hi)
+        un, vn = A(dst, lo, hi), A(dst, VO + lo, VO + hi)
+        how = {x: OPT[x][2 * k + c] for x in ("ga", "gn", "ge")}
+        copy = {"S": act, "V": cp}
+        copy[how["ga"]](ga, G(A("ah", 0, NW), off))
+        act(gb, G(A("bh", 0, NW), off), scale=256.0)
+        copy[how["gn"]](gn, G(A("nnd", 0, NW), off))
+        f = A("ff", 32 * c + 32, 32 * c + 64)
+        wb, w0 = 4 + c, 0
+        yield
+        pm, pd, pn = P(wb, w0 + 32 - 32 * c, w0 + 64 - 32 * c), P(wb, w0 + 64, w0 + 96), P(wb, w0 + 32 * c, w0 + 32 * c + 32)
+        wrap(pd, "wd", "gg", 512 + lo, 512 + hi)
+        mm(pb, [(idb, vb), (idb, A("hc", 0, 512))])
+        mm(pa, [(idb, ub)], True, False)
+        tt(pa, pb, ga, ALU.mult)
+        mm(pa, [(idb, ub)], False, True)
+        mm(pb, [(idb, vb)], True, False)
+        ts(mq, pa, MAGIC, ALU.add, -MAGIC, ALU.add)
+        if OPT["pc"] == 0:
+            tt(pa, pa, mq, ALU.subtract)
+            tt(pb, pa, gb, ALU.mult)
+            act(un, pa)
+        else:
+            yield
+            pc = P(7, 0, 512)
+            mm(pc, [(idb, gb)])
+            tt(un, pa, mq, ALU.subtract)
+            tt(pb, pc, un, ALU.mult)
+            yield
+        mm(pb, [(idb, vb), (A("idh", 0, 128), gb)], False, True)
+        ts(mq, pb, MAGIC, ALU.add, -MAGIC, ALU.add)
+        tt(vn, pb, mq, ALU.subtract)
+        if how["ge"] == "V":
+            tt(ge, pa if OPT["pc"] == 0 else un, vn, ALU.is_ge)
+        else:
+            mm(pa, [(idb, un), (A("idn", 0, 128), vn)])
+            act(ge, pa, ACT.Sign, bias=0.5)
+        mm(P(wb, w0, w0 + 64), [(idf, A("ff", 64 * c, 64 * c + 64))], True, False)
+        mm(P(wb, w0, w0 + 64), [(sh("q1", i), A("gg", 2 * lo + i, 2 * lo + K, 16)) for i in range(16)], False, True)
+        sg, t2 = A("sg", 32 * c, 32 * c + 32), A("t2", 32 * c, 32 * c + 32)
+        ts(sg, pn, 8.5 if how["ge"] == "V" else 1.0, ALU.is_ge, -0.5, ALU.add)
+        tt(t2, pd, sg, ALU.mult)
+        tt(f, pm, t2, ALU.add)
+        if k == 0:
+            cp(off, f)
+
+    def moves(t):
+        f, on, sc = A("ff", 32, 96), A("on", 0, 64), A("sc", 0, 64)
+        ts(on, f, 3071.5, ALU.is_ge)
+        add("v", lambda q: q.tensor_tensor_scan(sc["ap"], on["ap"], on["ap"], 0.0, ALU.add, ALU.max), COST["fix"] + 64 * cy, [on], [sc])
+        mm(P(4, 0, 64), [(blk, sc)])
+        mm(P(5, 0, 2), [(blk, A("sc", 62, 64))])
+        mm(P(5, 64, 128), [(blk, sc), (A("un", 0, 128), on)])
+        slot = lambda r: A("cin", 16 * t + 4 * r, 16 * t + 4 * r + 1)
+        ts(slot(rank), P(5, 1, 2), 256.0, ALU.min)
+        incl = A("cc", 64, 128)
+        cp(incl, P(5, 64, 128))
+        others = [r for r in range(n) if r != rank]
+        send(slot(rank), [(T.cores[r], slot(rank)) for r in others], [slot(r) for r in others], 100)
+        nv = OPT["accv"]
+        if nv:
+            mm(P(0, 0, 64), [(blk, sc)])
+        for c in range(16):
+            jk, acc = A("junk", 64 * c, 64 * c + 64), A("acc", c, c + 1)
+            if c < nv:
+                ts(jk, P(0, 0, 64), A("kw", c, c + 1), ALU.is_le)
+                add("v", lambda q, jk=jk, acc=acc: q.tensor_reduce(acc["ap"], jk["ap"], AxisListType.X, ALU.add), COST["fix"] + 64 * cy, [jk], [acc])
+            else:
+                act(jk, P(4, 0, 64), ACT.Sign, bias=A("kw", c, c + 1), scale=-1.0, acc=acc, extra=20.0)
+        cu = A("cu", 0, 16)
+        if nv:
+            cp(A("cu", 0, nv), A("acc", 0, nv))
+            act(A("cx", 0, nv), A("acc", 0, nv), scale=16.0)
+        ts(A("cu", nv, 16), A("acc", nv, 16), 0.5, ALU.mult, 32.0, ALU.add)
+        act(A("cx", nv, 16), A("acc", nv, 16), bias=512.0, scale=8.0)
+        tt(A("le", 0, 256), G(A("cc", 64, 136), cu), A("kr", 0, 256), ALU.is_le)
+        mm(P(5, 0, 16), [(idf, A("cx", 0, 16))], True, False)
+        mm(P(5, 0, 16), [(sh("q1", i), A("le", i, 256, 16)) for i in range(16)], False, True)
+        atu = A("atu", 0, 16)
+        cp(atu, P(5, 0, 16))
+        uv = UV[t + 1]
+        act(A("snd", 0, 256), G(A(uv, 0, VO), atu))
+        cp(A("snd", 256, 512), G(A(uv, VO, 2 * VO), atu))
+        act(A("atf", 0, 16), P(5, 0, 16))
+        rk = A("rk", 0, 64)
+        act(A("lv0", 0, 64), on, bias=4096.0, scale=-4096.0)
+        tt(rk, incl, A("lv0", 0, 64), ALU.add)
+        act(A("fc", 0, 64), f, bias=-3328.0)
+        act(A("fk", 0, 64), f, bias=256.0, scale=-1.0)
+        if t == 2:
+            ts(A("uc", 0, K), A(uv, 0, K), -0.5, ALU.add)
+            for c in range(2):
+                z = P(2 + c, 0, 512)
+                act(z, A(uv, VO + 512 * c, VO + 512 * c + 512), bias=-0.5)
+                tt(z, z, A("uc", 512 * c, 512 * c + 512), ALU.mult)
+                act(A("sig", 512 * c, 512 * c + 512), z, ACT.Sigmoid, scale=2.0 ** -13, extra=1300.0 if first[0] else 0.0)
+                first[0] = False
+        tt(A("eq", 0, 256), G(A("rk", 0, 72), cu), A("kr", 1, 257), ALU.is_equal)
+        tt(A("snd", 512, 768), G(A("fc", 0, 72), cu), A("eq", 0, 256), ALU.mult)
+        r0 = 768 * t
+        for lo, hi in ((0, 256), (256, 768)) if OPT["split"] else ((0, 768),):
+            send(A("snd", lo, hi), [(nxt, A("rcv", r0 + lo, r0 + hi))], [A("rcv", r0 + lo, r0 + hi)], 2 * (hi - lo))
+        m = A("mm", 4 * t, 4 * t + 1)
+        cin = A("cin", 16 * t, 16 * t + 13, 4)
+        add("v", lambda q: q.tensor_reduce(m["ap"], cin["ap"], AxisListType.X, ALU.min), COST["fix"] + 64 * cy, [cin], [m])
+        shift = A("mm", 4 * t + 1, 4 * t + 2)
+        if t == 0:
+            shift = m
+        else:
+            act(shift, m, bias=A("mm", 4 * t - 4 + min(t - 1, 1), 4 * t - 3 + min(t - 1, 1)))
+        ts(A("e1", 0, 16), A("kw", 16, 32), m, ALU.subtract, 2048.0, ALU.mult)
+        tt(A("e2", 0, 16), A("e1", 0, 16), A("kw", 32, 48), ALU.min)
+        tt(A("e3", 0, 16), A("e2", 0, 16), A("atf", 0, 16), ALU.max)
+        asu = A("asu", 0, 16)
+        cp(asu, A("e3", 0, 16))
+        lo, hi = ((0, 240), (48, 288), (48, 240))[t]
+        si = A("si", 0, hi - lo)
+        ts(si, A("sdf", lo, hi), shift, ALU.add)
+        ts(si, si, 1023, ALU.bitwise_and)
+        cp(A("sl", 240 * t, 240 * t + hi - lo), si)
+        ts(A("ro", 0, 64), incl, -1.0, ALU.add, 255.0, ALU.min)
+        lv = A("lv", 0, 64)
+        ts(lv, rk, m, ALU.is_le)
+        cp(G(A(uv, 0, VO), asu), A("rcv", r0, r0 + 256))
+        if t < 2:
+            cp(G(A(uv, VO, 2 * VO), asu), A("rcv", r0 + 256, r0 + 512))
+        else:
+            z = P(2, 0, 256)
+            act(z, A("rcv", r0, r0 + 256), bias=-0.5 * 2.0 ** -13, scale=2.0 ** -13)
+            ts(A("uc", 0, 256), A("rcv", r0 + 256, r0 + 512), -0.5, ALU.add)
+            tt(A("zr", 0, 256), z, A("uc", 0, 256), ALU.mult)
+            o = G(A("sig", 0, VO), asu)
+            add("s", lambda q: q.activation(o["ap"], T["zr"][:, 0:256], ACT.Sigmoid), COST["fix"] + 256 * COST["sca"] * cy, [A("zr", 0, 256)], [o])
+            act(P(5, 0, 512), A("sig", 512, K))
+        for c in range(2):
+            act(A("gf", 512 * c, 512 * c + 512), G(A("rcv", r0 + 512, r0 + 768), A("ro", 32 * c, 32 * c + 32)))
+        pf = P(0 if t < 2 else 4, 0, 64)
+        mm(pf, [(idf, A("fk", 0, 64))], True, False)
+        mm(pf, [(sh("q1", i), A("gf", i, K, 16)) for i in range(16)], False, True)
+        tt(A("t2", 0, 64), pf, lv, ALU.mult)
+        tt(f, A("t2", 0, 64), f, ALU.add)
+        cp(A("fu", 0, 64), f)
+
+    def follower_lists(t):
+        for j, mat in ((0, "w0"), (1, "w1")):
+            o = P(6 + j, 0, 48) if OPT["pc"] == 0 else P(6, 64 * j, 64 * j + 48)
+            mm(o, [(sh(mat, i), A("nnd", 4 * i + t, NV, 64)) for i in range(16)] + [(idf, A("sf", 0, 48))])
+            ts(A("nl", 144 * j + 48 * t, 144 * j + 48 * t + 48), o, float(t), ALU.add)
+
+    def heights(t):
+        s = 2.0 ** (t - 9)
+        if t == 0:
+            act(A("w", NV, NW), A("gl0", 0, 512), scale=0.25)
+        else:
+            act(A("w", NV, NW), A("gl", 512 * t - 512, 512 * t), scale=2.0)
+        if "V" in OPT["xh"][t]:
+            ts(A("us", 0, K), A(UV[t + 1], 0, K), -0.5, ALU.add, s, ALU.mult)
+        xs = "x%d" % t
+        base = (48, 240, 480)[t]
+        for b in range(3, -1, -1):
+            how = OPT["xh"][t][b]
+            for c in range(2):
+                lo, hi = BL * b + 384 * c, BL * b + 384 * c + 384
+                off = A("sl", base + lo // 16, base + hi // 16)
+                if how == "V":
+                    tt(A("w", lo, hi), G(A("us", 0, K), off), A("w", lo, hi), ALU.add)
+                    continue
+                act(A(xs, lo, hi), G(A(UV[t + 1], 0, K), off), bias=-0.5 * s, scale=s)
+                o = P(3 + c if t == 2 else 6 + c * (1 - OPT["pc"]), 0, 384)
+                if how == "P":
+                    mm(o, [(idb, A(xs, lo, hi))])
+                    tt(A("w", lo, hi), o, A("w", lo, hi), ALU.add)
+                else:
+                    mm(o, [(A("id8", 0, 128), A("h", lo, hi))] + [(idb, A("x%d" % j, lo, hi)) for j in range(t + 1)])
+                    if how == "A":
+                        act(A("w", lo, hi), o)
+                    else:
+                        cp(A("w", lo, hi), o)
+            win = A("w", BL * b, NW)
+            adds = []
+            for c in range(t + 1):
+                bank = 6 + c if t < 2 else c
+                lo, hi = BL * b + c, BL * b + BL
+                l0 = A("nl", 48 * c + 12 * b, 48 * c + 12 * b + 12)
+                l1 = A("nl", 144 + 48 * c + 12 * b, 144 + 48 * c + 12 * b + 12)
+                h1, h2, p2 = (A(x, 192 * c, 192 * c + 192) for x in ("h1", "h2", "p2"))
+                pa = P(bank, 0, 192) if t == 2 or OPT["pc"] == 0 else P(6, 192 * c, 192 * c + 192)
+                mm(pa, [(A("id256", 0, 128), A("ah", lo, hi, 4)), (idb, A("ee", BL * c + 192 * b, BL * c + 192 * b + 192))])
+                act(h1, G(win, l0))
+                if OPT["corr"][t] == "A":
+                    pb = P(bank, 192, 384)
+                    mm(pb, [(idb, A("bh", lo, hi, 4))])
+                    act(h2, G(win, l1))
+                    tt(p2, pb, h2, ALU.mult)
+                else:
+                    tt(p2, G(win, l1), A("bh", lo, hi, 4), ALU.mult)
+                tt(pa, pa, h1, ALU.mult)
+                adds.append((A("w", lo, hi, 4), pa, p2))
+            for o, pa, p2 in adds:
+                tt(o, pa, p2, ALU.add)
+        if t < 2:
+            gl = A("gl", 512 * t, 512 * t + 512)
+            send(A("w", 0, 512), [(prv, gl)], [gl], 2048)
+
+    def outputs():
+        for bank, lo, hi in ((6, 0, 512), (7, 512, BL)):
+            mm(P(bank, 0, hi - lo), [(idf, A("w", BL * b + lo, BL * b + hi)) for b in (3, 2, 1)])
+        win = A("w", 0, NW)
+        act(A("hb", 0, 512), G(win, A("fu", 32, 64)))
+        tt(A("pa", 0, 512), G(win, A("fu", 0, 32)), A("sig", 0, 512), ALU.mult)
+        z = P(5, 0, 512)
+        tt(z, z, A("hb", 0, 512), ALU.mult)
+        tt(A("ow", 0, 512), z, A("pa", 0, 512), ALU.add)
+        tt(A("oh", 0, BL), P(6, 0, BL), A("w", 0, BL), ALU.add)
+        store(T.yw[:], A("ow", 0, 512), "y", 2048)
+        store(T.yh[:], A("oh", 0, BL), "y", 3072)
+
+    for t in range(3):
+        collapse(t)
+        fill[0] = True
+        follower_lists(t)
+        fill[0] = False
+        for k in range(2):
+            halves = [hop(t, k, 0), hop(t, k, 1)]
+            for _ in range(4):
+                for x in halves:
+                    next(x, None)
+        moves(t)
+        if t < 2:
+            fill[0] = True
+            heights(t)
+            fill[0] = False
+    heights(2)
+    outputs()
+    return ops
+
+
+def depend(ops):
+    hist = {}
+    for j, op in enumerate(ops):
+        wait, order = set(), set()
+        if op["kind"] == "recv":
+            order.add(op["after"])
+        if "follow" in op:
+            order.add(op["follow"])
+        acc = [(r, False) for r in op["rd"]] + [(r, True) for r in op["wr"]]
+        for (name, lo, hi, st), wr in acc:
+            for lo2, hi2, st2, i, wr2 in hist.get(name, []):
+                o = ops[i]
+                same = o["eng"] == op["eng"] and o["kind"] == "c" and op["kind"] == "c"
+                if name == "ps" and not same:
+                    if lo // 512 <= (hi2 - 1) // 512 and lo2 // 512 <= (hi - 1) // 512:
+                        wait.add(i)
+                elif lo < hi2 and lo2 < hi and (wr or wr2) and (lo - lo2) % math.gcd(st, st2) == 0:
+                    wait.add(i)
+                elif name == "ps" and op["eng"] == "p" and lo // 512 == lo2 // 512:
+                    order.add(i)
+        for (name, lo, hi, st), wr in acc:
+            hist.setdefault(name, []).append((lo, hi, st, j, wr))
+        if op["kind"] == "recv":
+            wait = set()
+        op["wait"], op["order"] = wait, order - wait
+
+
+def graph(ops):
+    pred = []
+    for op in ops:
+        p = {i: 0.0 for i in op["order"]}
+        if op["kind"] == "recv":
+            p[op["after"]] = ops[op["after"]]["lat"]
+        for i in op["wait"]:
+            near = ops[i]["eng"] == op["eng"]
+            p[i] = ops[i].get("lat", 0.0) + (COST["own"] if near else COST["lat"])
+        pred.append(p)
+    far = []
+    for j, p in enumerate(pred):
+        reach = {}
+        for i in sorted(p, reverse=True):
+            if reach.get(i, -1.0) >= p[i]:
+                del p[i]
+                continue
+            reach[i] = p[i]
+            for h, x in far[i].items():
+                reach[h] = max(reach.get(h, -1.0), x + ops[i]["dur"] + p[i])
+        far.append(reach)
+    return pred
+
+
+def place(eng, dur, pred, succ, pri, rel):
+    n = len(eng)
+    left = [len(p) for p in pred]
+    ready = [j for j in range(n) if left[j] == 0]
+    start, can = [0.0] * n, list(rel)
+    busy = {e: ([], []) for e in "vspgy"}
+    urgent = lambda x: pri[x]
+    while ready:
+        j = max(ready, key=urgent)
+        ready.remove(j)
+        t, d = can[j], dur[j]
+        if eng[j] is not None:
+            a, b = busy[eng[j]]
+            m = len(a)
+            lo, hi = 0, m
+            while lo < hi:
+                mid = (lo + hi) // 2
+                if b[mid] > t:
+                    hi = mid
+                else:
+                    lo = mid + 1
+            while lo < m and t + d > a[lo] + 1e-6:
+                t = b[lo]
+                lo += 1
+            a.insert(lo, t)
+            b.insert(lo, t + d)
+        start[j] = t
+        t += d
+        for s, x in succ[j].items():
+            if can[s] < t + x:
+                can[s] = t + x
+            left[s] -= 1
+            if left[s] == 0:
+                ready.append(s)
+    return start
+
+
+def schedule(ops):
+    n = len(ops)
+    pred = graph(ops)
+    succ = [{} for _ in range(n)]
+    for j in range(n):
+        for i, d in pred[j].items():
+            succ[i][j] = d
+    eng, dur = [o["eng"] for o in ops], [o["dur"] + 1e-3 for o in ops]
+    tail, zero = [o.get("lat", 0.0) for o in ops], [0.0] * n
+    pri = [0.0] * n
+    for j in range(n - 1, -1, -1):
+        pri[j] = dur[j] + max([pri[s] + d for s, d in succ[j].items()] + [tail[j]])
+    best = None
+    rng = numpy.random.default_rng(OPT["seed"])
+    chain = pri
+    later = OPT["later"]
+    cur = None
+    main = [j for j in range(n) if not ops[j]["fill"]]
+    for it in range(OPT["passes"]):
+        if it < len(later):
+            pri = [chain[j] - (later[it] if ops[j]["fill"] else 0.0) for j in range(n)]
+        else:
+            shake = (rng.random(n) * OPT["noise"] * float(rng.random()) ** 2).tolist()
+            lo = float(rng.random()) * max(cur[1]) - 0.5 * OPT["span"]
+            pri = [(shake[j] if lo <= cur[1][j] < lo + OPT["span"] else 0.0) - cur[1][j] for j in range(n)]
+        start = place(eng, dur, pred, succ, pri, zero)
+        for _ in range(3 if it < len(later) else 1):
+            back = place(eng, dur, succ, pred, [start[j] + dur[j] for j in range(n)], tail)
+            start = place(eng, dur, pred, succ, [back[j] + dur[j] for j in range(n)], zero)
+        end = max(start[j] + dur[j] + tail[j] for j in range(n)) + OPT["pull"] * sum(start[j] for j in main) / len(main)
+        if best is None or end < best[0]:
+            best = (end, start)
+        if cur is None or end <= cur[0] + OPT["warm"] * (1.0 - it / OPT["passes"]) * (it >= len(later)):
+            cur = (end, start)
+    start = best[1]
+    seq = sorted(range(n), key=lambda j: (start[j], j))
+    order = {e: [j for j in seq if eng[j] == e] for e in "vspgy"}
+    return order, start, [start[j] + dur[j] + tail[j] for j in range(n)]
+
+
+PLAN = {}
+
+
+def rank_program(g, core, T, topo):
+    if T.rank_of(core) is None:
+        return
+    ops = build(T, topo, core)
+    depend(ops)
+    if "order" not in PLAN:
+        PLAN["order"] = schedule(ops)
+    order, start, _ = PLAN["order"]
+    queue = {"v": g.vector, "s": g.scalar, "p": g.tensor, "g": g, "y": g.sync}
+    total = {}
+    for e in "vspg":
+        k = 0
+        for j in order[e]:
+            if ops[j]["kind"] == "c":
+                k += 1
+                ops[j]["sem"], ops[j]["cnt"] = COUNTER[e], k
+    for op in ops:
+        total[op["sem"]] = max(total.get(op["sem"], 0), op["cnt"])
+    known = {e: {} for e in "vspgy"}
+    for j in sorted(range(len(ops)), key=lambda x: (start[x], x)):
+        op = ops[j]
+        if op["eng"] is None:
+            op["clock"] = {}
+            continue
+        seen = known[op["eng"]]
+        op["waits"] = []
+        for i in sorted(op["wait"], key=lambda x: -start[x]):
+            o = ops[i]
+            if seen.get(o["sem"], 0) < o["cnt"]:
+                op["waits"].append((o["sem"], o["cnt"]))
+                seen[o["sem"]] = o["cnt"]
+                for s, c in o["clock"].items():
+                    seen[s] = max(seen.get(s, 0), c)
+        op["clock"] = dict(seen)
+    for e in "yvspg":
+        q = queue[e]
+        for j in order[e]:
+            op = ops[j]
+            for s, c in op["waits"]:
+                q.wait_ge(T.sem[s], c)
+            ins = op["fn"](q)
+            if op["kind"] == "c":
+                ins.then_inc(T.sem[op["sem"]], 1)
+            elif op["kind"] == "dma":
+                ins.then_inc(T.sem[op["sem"]], 16)
+    for s in sorted(total):
+        g.wait_ge(T.sem[s], total[s])

@@ -5,7 +5,9 @@ from concourse.mybir import AluOpType, AxisListType, ActivationFunctionType
 
 F32, BF, I32, U16 = "float32", "bfloat16", "int32", "uint16"
 NV, NW, BL, K = 3072, 3584, 768, 1024
-VO = 1280
+NZ = NV + 32
+ZC = 1280
+VO = 1296
 UV = ("uv", "uv0", "uv", "uv0")
 MAGIC = 1.5 * 2.0 ** 31
 
@@ -17,37 +19,49 @@ def _sb(n, d):
 SCRATCH = {
     "ps": ("psum", [128, 4096], F32),
     "a": _sb(NV, BF), "b": _sb(NV, BF), "h": _sb(NV, BF),
-    "uv": _sb(2 * VO, BF), "uv0": _sb(2 * VO, BF), "uw": _sb(2 * VO, BF), "mq": _sb(K, BF), "hc": _sb(512, BF), "idh": _sb(128, BF),
+    "uv": _sb(2 * VO, BF), "uv0": _sb(2 * VO, BF), "uw": _sb(2 * VO, BF), "us": _sb(VO, BF), "md": _sb(72, F32), "gs": _sb(384, F32), "gr": _sb(384, F32), "mqt": _sb(K, F32), "idk": _sb(128, BF), "zz": _sb(NZ // 4, BF),
+    "mqu": _sb(K, BF), "mqv": _sb(K, F32), "hc": _sb(512, BF), "one": _sb(256, BF), "un4": _sb(128, BF), "lz": _sb(128, BF), "st": _sb(128, BF), "ro": _sb(64, U16), "hh": _sb(512, BF),
     "nab": _sb(384, I32), "sdi": _sb(192, I32), "pfi": _sb(64, I32), "thi": _sb(4, I32),
     "ci": _sb(4, I32), "cf": _sb(16, F32), "cb": _sb(8, BF), "kr": _sb(272, BF), "r16": _sb(128, BF),
     "q1": _sb(144, BF), "wd": _sb(144, BF), "w0": _sb(144, BF), "w1": _sb(144, BF),
-    "blk": _sb(128, BF), "idb": _sb(128, BF), "id8": _sb(128, BF), "id256": _sb(128, BF), "bs": _sb(3 * BL, BF), "idf": _sb(128, F32),
+    "blk": _sb(128, BF), "idb": _sb(128, BF), "idn": _sb(128, BF), "idh": _sb(128, BF), "id256": _sb(128, BF), "id512": _sb(128, BF), "idf": _sb(128, F32),
     "un": _sb(128, BF), "un0": _sb(128, BF), "i16": _sb(16, F32), "bm": _sb(16 * 144, BF),
-    "kw": _sb(64, F32), "fw": _sb(192, F32), "sf0": _sb(48, F32), "sf": _sb(48, F32),
-    "thf": _sb(8, F32), "shl": _sb(384, BF), "dn": _sb(384, F32), "dhl": _sb(768, BF),
-    "nnc": _sb(3 * BL, BF), "nnd": _sb(NW, BF), "ah": _sb(NW, BF), "bh": _sb(NW, BF), "ee": _sb(3 * BL, BF),
-    "sdf": _sb(288, F32), "si": _sb(240, I32), "sl": _sb(720, U16),
-    "dd": _sb(BL, F32), "c1": _sb(BL, BF), "c2": _sb(BL, BF),
+    "kw": _sb(64, F32), "fw": _sb(16, F32), "sf0": _sb(48, F32), "sf": _sb(48, F32),
+    "thf": _sb(8, F32), "shl": _sb(384, BF), "dhl": _sb(768, BF),
+    "nnd": _sb(NZ, BF), "ah": _sb(NZ, BF), "bh": _sb(NZ, BF), "dm": _sb(3 * BL, BF),
+    "sdf": _sb(384, F32), "si": _sb(192, I32), "sl": _sb(624, U16),
+    "dd": _sb(BL, F32), "xs": _sb(BL, BF), "c1": _sb(BL, BF), "c2": _sb(BL, BF),
     "ff": _sb(128, F32), "fu": _sb(64, U16), "sg": _sb(64, F32), "t2": _sb(64, F32),
-    "ga": _sb(K, BF), "gb": _sb(K, BF), "gg": _sb(2 * K, BF), "idn": _sb(128, BF), "zr": _sb(256, F32),
+    "ga": _sb(K, BF), "gb": _sb(K, BF), "gg": _sb(2 * K, BF),
     "on": _sb(64, BF), "sc": _sb(64, BF), "cc": _sb(136, F32), "rk": _sb(72, F32), "fc": _sb(72, F32),
     "junk": _sb(K, BF), "acc": _sb(16, F32), "cu": _sb(16, U16), "cx": _sb(16, F32),
     "le": _sb(256, BF), "eq": _sb(256, BF), "atf": _sb(16, F32), "atu": _sb(16, U16), "asu": _sb(16, U16),
     "e1": _sb(16, F32), "e2": _sb(16, F32), "e3": _sb(16, F32),
-    "cin": _sb(48, F32), "mm": _sb(12, F32), "ro": _sb(64, U16), "lv": _sb(64, F32), "lv0": _sb(64, F32),
-    "fk": _sb(64, F32), "gf": _sb(K, BF),
+    "cin": _sb(48, F32), "mm": _sb(12, F32), "lv": _sb(64, F32), "lv0": _sb(64, F32),
+    "fk": _sb(64, F32), "gf": _sb(VO, BF),
     "snd": _sb(768, BF), "rcv": _sb(3 * 768, BF),
     "gl0": _sb(512, BF), "gl": _sb(1024, F32),
-    "w": _sb(NW, F32), "x0": _sb(NV, BF), "x1": _sb(NV, BF), "x2": _sb(NV, BF), "us": _sb(K, BF),
-    "nl": _sb(6 * 48, U16), "h1": _sb(3 * 192, F32), "h2": _sb(3 * 192, F32), "p2": _sb(3 * 192, F32),
-    "uc": _sb(K, BF), "sig": _sb(VO, F32), "pa": _sb(512, F32), "hb": _sb(512, F32),
+    "w": _sb(NW, F32), "x": _sb(NV, BF),
+    "nl": _sb(6 * 48, U16), "h1": _sb(3 * 192, F32), "p2": _sb(3 * 192, F32),
+    "zt": _sb(K + 16, F32), "sig": _sb(VO, F32), "pa": _sb(512, F32), "hb": _sb(512, F32),
     "oh": _sb(BL, F32), "ow": _sb(512, F32),
 }
-SEMAPHORES = ["cv", "cs", "cp", "cg"] + ["d%d" % i for i in range(16)] + ["l%d" % i for i in range(12)] + ["r%d" % i for i in range(12)]
+SEMAPHORES = ["cv", "cs", "cp", "cg"] + ["d%d" % i for i in range(40)] + ["l%d" % i for i in range(20)] + ["r%d" % i for i in range(20)]
 COUNTER = {"v": "cv", "s": "cs", "p": "cp", "g": "cg"}
 
-COST = {"cyc": 1.0, "pe": 0.52, "gat": 1.55, "sca": 3.8, "fix": 60.0, "lat": 120.0, "own": 120.0, "remote": 3200.0, "rissue": 900.0}
-OPT = {"xh": ["AAAA", "AAAA", "AAVV"], "corr": "BBB", "cmp": "SV", "dead": "SS", "ga": "SSSS", "gn": "SSSS", "ge": "SVSV", "pc": 0, "accv": 0, "split": 1, "passes": 5000, "noise": 4000.0, "span": 10000.0, "later": [0.0, 5e3, 1e4, 2e4, 4e4, 1e6], "seed": 1, "pull": 3.0, "warm": 150.0, "dbank": (4, 5)}
+COST = {"cyc": 1.0, "pe": 0.52, "gat": 1.55, "sca": 3.8, "fix": 60.0, "lat": 120.0, "own": 120.0, "remote": 1800.0, "rows": 800.0, "link": 1.4, "rissue": 900.0,
+        "gissue": 900.0, "glat": 3000.0}
+OPT = {
+    "corr": [["M"] * 4, ["MM"] * 4, ["BBB"] * 4], "cmp": "VVV", "sg": "S", "on": "V", "incl": "S",
+    "hop": ["SVSV", "SVSV", "SSSV"],
+    "ga": "SSSS", "gb": "SSSS", "gn": "SSSS",
+    "stag": [(("m2", 0, 1), ("vn", 0, 0)), (("m2", 1, 1), ("vn", 1, 0))],
+    "cuts": [(0, 256, 512, 768), (0, 256, 512, 768), (0, 256, 768)], "gs": "SS", "dcuts": [(4, 2, 0), (4, 2, 0)], "pd": 1, "early": 1,
+    "direct": [(1, 0), (2, 0)], "xparts": [2, 2], "nn": "S", "qu": ["VVVV"] * 3, "blank": ["ah", "bh"], "x0": "V", "xs": "SS", "xc": ["SSSS", "SSSS"],
+    "xl": ["DD", "DD", "VV", "VV"], "pre3": [1, 1, 0], "dead": "SS", "oh": "P", "accv": [6, 6, 3], "gf": "VVS", "sv": "S", "zero": "gVVg",
+    "sweeps": 8, "wide": 24000.0, "tries": 300, "near": 0.5, "cool": 100.0,
+    "raw": "VVSS",
+    "aim": 0.85, "reach": 2000.0, "every": 10, "passes": 9000, "noise": 4000.0, "span": 10000.0, "later": [0.0, 5e3, 1e4, 2e4, 4e4, 1e6], "seed": 1, "pull": 3.0, "warm": 250.0}
 
 
 def build(T, topo, core):
@@ -76,7 +90,7 @@ def build(T, topo, core):
         for x in wr:
             w += x["reg"]
             r += x.get("oreg", [])
-        op = {"eng": eng, "fn": fn, "dur": dur, "rd": r, "wr": w, "kind": "c", "fill": fill[0]}
+        op = {"eng": eng, "fn": fn, "dur": dur * COST.get(eng, 1.0), "rd": r, "wr": w, "kind": "c", "fill": fill[0]}
         op.update(kw)
         ops.append(op)
         return len(ops) - 1
@@ -121,6 +135,14 @@ def build(T, topo, core):
             fn = lambda q: q.activation(out["ap"], i0["ap"], f, bias=ap(bias), scale=ap(scale), accum_out=acc["ap"])
         add("s", fn, COST["fix"] + extra + max(64, i0["n"] * c) * cy, [i0, bias, scale], [out] + ([acc] if acc else []))
 
+    def lin(how, out, i0, bias=0.0, scale=1.0):
+        if how == "S":
+            act(out, i0, bias=bias, scale=scale)
+        elif bias == 0.0 and scale == 1.0:
+            cp(out, i0)
+        else:
+            ts(out, i0, scale, ALU.mult, bias, ALU.add)
+
     def mm(out, pairs, start=True, stop=True):
         def fn(q):
             last = None
@@ -137,7 +159,13 @@ def build(T, topo, core):
             fn = lambda q: q.iota(out["ap"], pattern, base, cm, allow_small_or_imprecise_dtypes=True)
         add("g", fn, 130.0 + 2 * out["n"] * cy, [], [out])
 
-    nd, nr, bus = [0], [0], [0.0]
+    def zero(how, out):
+        if how == "g":
+            iota(out, [[0, out["n"]]], 0, 0)
+        else:
+            ms(out, 0.0)
+
+    nd, nr, bus = [0], [0], [0.0, 0]
 
     def load(dst, src, eng, nbytes):
         s = "d%d" % nd[0]
@@ -145,33 +173,46 @@ def build(T, topo, core):
         bus[0] += nbytes * 0.22 - 60.0
         j = add(eng, lambda q: q.dma_start(dst["ap"], src), 60.0, [], [dst], kind="dma", sem=s, cnt=16, lat=1900.0 + max(bus[0], 0.0))
         if nd[0] > 1:
-            ops[j]["follow"] = j - 1
+            ops[j]["follow"] = bus[1]
+        bus[1] = j
 
     def store(dst, src, eng, nbytes):
         s = "d%d" % nd[0]
         nd[0] += 1
-        add(eng, lambda q: q.dma_start(dst, src["ap"]), 60.0, [src], [], kind="dma", sem=s, cnt=16, lat=1900.0 + nbytes * 0.22)
+        add(eng, lambda q: q.dma_start(dst["ap"], src["ap"]), 60.0, [src], [dst], kind="dma", sem=s, cnt=16, lat=1900.0 + nbytes * 0.22)
 
-    mask = -1
-    for c in T.cores:
-        if c != core:
-            mask &= topo.mask(core, c)
-    ne = bin(mask).count("1")
+    def dadd(dst, src):
+        s = "d%d" % nd[0]
+        nd[0] += 1
+        add("g", lambda q: q.dma_start(dst["ap"], src["ap"], accum_op=ALU.add), COST["gissue"], [src, dst], [dst], kind="dma", sem=s, cnt=16,
+            lat=COST["glat"] + dst["n"] * 4 * 0.3)
 
-    def send(src, dsts, lands, nbytes):
+    def engines(a, b, wide=False):
+        far = -1
+        for c in T.cores:
+            if c != a:
+                far &= topo.mask(a, c)
+        return topo.mask(a, b) if wide else (topo.mask(a, b) & ~far) or far
+
+    def send(src, dsts, froms, lands, nbytes, line, wide=False):
         ls, rs = "l%d" % nr[0], "r%d" % nr[0]
         nr[0] += 1
+        masks = sorted({engines(core, c, wide) for c, _ in dsts})
 
         def fn(q):
             if len(dsts) == 1:
                 rid, pid, _ = topo.addr(dsts[0][0])
-                return q.remote_dma(dsts[0][1]["ap"], src["ap"], T.sem[rs], T.sem[ls], pid, rid, mask)
-            ids = [DstId(rid=topo.addr(c)[0], pnc=topo.addr(c)[1]) for c, _ in dsts]
-            tr = RemoteDMATransfer(dst_ids=ids, dma_engine_mask=mask, remote_sem=T.sem[rs], srcs=[src["ap"]], dsts=[d["ap"] for _, d in dsts])
-            return q.remote_dma_fused([tr], local_sem=T.sem[ls])
-        lat = COST["remote"] - COST["rissue"] + nbytes * 0.8
-        j = add("g", fn, COST["rissue"], [src], [], kind="send", sem=ls, cnt=ne, lat=lat)
-        add(None, None, 0.0, [], lands, kind="recv", sem=rs, cnt=ne * len(lands), after=j, lat=0.0)
+                return q.remote_dma(dsts[0][1]["ap"], src["ap"], T.sem[rs], T.sem[ls], pid, rid, masks[0])
+            trs = []
+            for m in masks:
+                to = [(c, d) for c, d in dsts if engines(core, c, wide) == m]
+                trs.append(RemoteDMATransfer(dst_ids=[DstId(rid=topo.addr(c)[0], pnc=topo.addr(c)[1]) for c, _ in to], dma_engine_mask=m,
+                                             remote_sem=T.sem[rs], srcs=[src["ap"]], dsts=[d["ap"] for _, d in to]))
+            return q.remote_dma_fused(trs, local_sem=T.sem[ls])
+        rows = COST["rows"] * min(len(dsts), 2) + nbytes * COST["link"]
+        left = sum(bin(m).count("1") for m in masks)
+        j = add("g", fn, COST["rissue"], [src], [], kind="send", sem=ls, cnt=left, lat=COST["remote"] + rows, lead=COST["remote"])
+        add(line, None, rows, [], lands, kind="recv", sem=rs, cnt=sum(bin(engines(c, core, wide)).count("1") for c in froms), after=j, lat=0.0)
 
     nxt, prv = T.cores[(rank + 1) % n], T.cores[(rank - 1) % n]
 
@@ -188,8 +229,20 @@ def build(T, topo, core):
     load(A("nab", 0, 192), T.na[:], "y", 768)
     load(A("nab", 192, 384), T.nb[:], "y", 768)
     load(A("pfi", 0, 64), T.pf[:], "y", 256)
+    zz = A("zz", 0, NZ // 4)
+
+    def blank(name):
+        if name in OPT["blank"]:
+            for c in range(4):
+                load(A(name, c * NZ // 4, (c + 1) * NZ // 4), zz["ap"], "y", NZ // 2)
+                ops[-1]["rd"] = zz["reg"]
+
+    ms(zz if OPT["blank"] else A("zz", 0, 384), 0.0)
+    blank("ah")
     load(A("uv", VO, VO + K), T.v0[:], "y", 2048)
     load(A("b", 0, NV), T.tb[:], "y", 6144)
+    blank("bh")
+    blank("nnd")
     load(A("h", 0, NV), T.h0[:], "y", 6144)
 
     iota(A("ci", 0, 1), [[0, 1]], 0, 1)
@@ -204,195 +257,291 @@ def build(T, topo, core):
     cp(A("cf", 0, 3), A("ci", 0, 3))
     pc, lane, g16 = A("cf", 0, 1), A("cf", 1, 2), A("cf", 2, 3)
     ts(A("q1", 0, 144), A("kr", 0, 144), -15.0, ALU.add, g16, ALU.is_equal)
-    ts(A("i16", 0, 16), A("kr", 0, 16), lane, ALU.is_equal)
-    masks = len(ops) - 1
-    for t in range(3):
+    ts(A("i16", 0, 16), A("kr", 0, 16), lane, ALU.is_equal, 0.5, ALU.mult)
+    for t in range(4):
+        fill[0] = t > 0
         for q in range(4):
             i = 4 * q + t
             if t == 0 and q % 2 == 0:
                 ts(A("bm", 144 * i, 144 * i + 144), A("q1", 0, 144), A("i16", i, i + 1), ALU.mult)
             else:
                 act(A("bm", 144 * i, 144 * i + 144), A("q1", 0, 144), scale=A("i16", i, i + 1))
+    fill[0] = False
     ts(A("blk", 0, 128), A("r16", 0, 128), g16, ALU.is_equal)
     ts(A("idb", 0, 128), A("kr", 0, 128), pc, ALU.is_equal)
-    act(A("idf", 0, 128), A("idb", 0, 128))
-    act(A("id8", 0, 128), A("idb", 0, 128), scale=0.125)
-    act(A("id256", 0, 128), A("idb", 0, 128), scale=1.0 / 256)
+    idb, idf, idn, idh, blk = (A(x, 0, 128) for x in ("idb", "idf", "idn", "idh", "blk"))
+    id256, id512, hc = A("id256", 0, 128), A("id512", 0, 128), A("hc", 0, 512)
+    act(idf, idb)
+    act(id256, idb, scale=1.0 / 256)
+    act(id512, idb, scale=1.0 / 512)
     ts(A("un0", 0, 128), A("kr", 0, 128), pc, ALU.is_lt, -1.0, ALU.mult)
-    tt(A("un", 0, 128), A("un0", 0, 128), A("blk", 0, 128), ALU.mult)
+    mm(P(5, 256, 384), [(idb, blk)])
+    tt(A("un", 0, 128), P(5, 256, 384), A("un0", 0, 128), ALU.mult)
     low = A("cb", 0, 1)
     act(low, lane, ACT.Sigmoid, bias=7.5 * 512, scale=-512.0, extra=1300.0)
+    table = len(ops) - 1
     act(A("cf", 3, 4), low, scale=2.0)
     act(A("cf", 4, 5), low, bias=2.0, scale=-2.0)
-    act(A("cf", 5, 6), low, bias=-2.0, scale=4.0)
+    half = 1.0 if OPT["sg"] == "V" else 0.5
+    act(A("cf", 5, 6), low, bias=-2.0 * half, scale=4.0 * half)
     act(A("cf", 6, 7), lane, scale=4.0)
-    act(A("idn", 0, 128), A("idb", 0, 128), scale=-1.0)
-    act(A("idh", 0, 128), A("idb", 0, 128), scale=127.5)
-    for lo in (0, VO):
-        ts(A("uv", lo, lo + K), A("uv", lo, lo + K), -127.5, ALU.add)
+    act(idn, idb, scale=-1.0)
+    act(idh, idb, scale=127.5)
     act(A("wd", 0, 144), A("q1", 0, 144), scale=A("cf", 5, 6))
     act(A("w0", 0, 144), A("q1", 0, 144), scale=A("cf", 3, 4))
     act(A("w1", 0, 144), A("q1", 0, 144), scale=A("cf", 4, 5))
     act(A("sf", 0, 48), A("sf0", 0, 48), bias=A("cf", 6, 7))
-    act(A("fw", 0, 192), A("kr", 0, 192), bias=lane, scale=16.0)
+    act(A("fw", 0, 16), A("kr", 0, 16), bias=lane, scale=16.0)
     act(A("kw", 0, 16), A("fw", 0, 16), bias=0.5)
     act(A("kw", 16, 32), A("fw", 0, 16), bias=1.0)
     act(A("kw", 32, 48), A("fw", 0, 16), bias=1024.0)
-    idb, idf, blk = A("idb", 0, 128), A("idf", 0, 128), A("blk", 0, 128)
-    for name in ("ah", "bh"):
-        for c in range(4):
-            ms(A(name, 896 * c, 896 * c + 896), 0.0)
-            if name != "ah" or c > 0:
-                ops[-1]["follow"] = masks
-    iota(A("nnd", 0, NW), [[0, NW]], 0, 0)
-    ops[-1]["follow"] = rows
-    ms(A("hc", 0, 512), 127.5)
+    for name, how in (("nnd", "ggg"), ("ah", OPT["zero"][1] * 3), ("bh", OPT["zero"][2] + OPT["zero"][3] * 2)):
+        if name in OPT["blank"]:
+            continue
+        for c in range(1, 4):
+            zero(how[c - 1], A(name, c, NV, 4))
+            if how[c - 1] == "g":
+                ops[-1]["follow"] = rows
+                rows = len(ops) - 1
+        ms(A(name, NV, NZ), 0.0)
+    ms(hc, 127.5)
     ms(A("ff", 0, 32), 0.0)
     ms(A("ff", 96, 128), 0.0)
-    ms(A("sig", K, VO), 0.0)
-    for name in ("uv", "uv0"):
-        ms(A(name, K, VO), 0.0)
-        ms(A(name, VO + K, 2 * VO), 0.0)
+    fill[0] = True
+    ms(A("one", 0, 256), 1.0)
+    ts(A("un4", 0, 128), idb, -4096.0, ALU.mult)
+    tt(A("un4", 0, 128), A("un4", 0, 128), A("un", 0, 128), ALU.add)
+    act(A("lz", 0, 128), idb, scale=A("i16", 0, 1))
+    act(A("lz", 0, 128), A("lz", 0, 128), scale=2.0)
+    ts(A("st", 0, 128), A("kr", 0, 128), -1.0, ALU.add, pc, ALU.is_equal)
+    tt(A("st", 0, 128), A("st", 0, 128), blk, ALU.mult)
+    tt(A("st", 0, 128), A("st", 0, 128), idb, ALU.subtract)
+    ms(A("hh", 0, 512), -0.5)
+    for name in ("uv0", "uv"):
+        ms(A(name, ZC, VO), 0.5)
+    for out in (A("uv0", K, ZC), A("uv0", VO + K, 2 * VO), A("gf", 0, VO), A("uv", K, ZC), A("uv", VO + K, 2 * VO), A("us", K, VO), A("sig", K, VO)):
+        zero("g", out)
+        ops[-1]["follow"] = rows
+        rows = len(ops) - 1
+    fill[0] = False
     ms(A("cc", 128, 136), 4096.0)
-    ms(A("rk", 64, 72), 0.0)
     ms(A("fc", 64, 72), 0.0)
-    if OPT["cmp"] == "SV":
+    if "V" in OPT["cmp"]:
         cp(A("thf", 0, 3), A("thi", 0, 3))
-    else:
+    if "S" in OPT["cmp"]:
         ts(A("thf", 4, 7), A("thi", 0, 3), 0.5, ALU.add)
 
     cp(A("shl", 0, 192), A("sdi", 0, 192))
     tt(A("shl", 192, 384), A("sdi", 0, 192), A("shl", 0, 192), ALU.subtract)
-    tt(A("dn", 0, 192), A("nab", 0, 192), A("fw", 0, 192), ALU.subtract)
-    tt(A("dn", 192, 384), A("nab", 192, 384), A("fw", 0, 192), ALU.subtract)
-    act(A("dhl", 0, 384), A("dn", 0, 384))
-    tt(A("dhl", 384, 768), A("dn", 0, 384), A("dhl", 0, 384), ALU.subtract)
+    if OPT["nn"] == "V":
+        act(P(5, 0, 192), A("kr", 0, 192), bias=lane, scale=16.0)
+    else:
+        act(A("cf", 7, 8), lane, bias=-4112.5)
+        act(P(5, 0, 192), A("kr", 0, 192), bias=A("cf", 7, 8), scale=16.0)
+        act(A("idk", 0, 128), idb, scale=4096.0)
+        tt(A("cf", 9, 11), A("i16", 0, 2), A("i16", 8, 10), ALU.add)
+        act(A("cf", 9, 10), A("cf", 9, 10), bias=-4096.0, scale=-4128.0)
+        act(A("cf", 8, 9), A("cf", 10, 11), bias=A("cf", 9, 10), scale=15.5)
+    for j in range(2):
+        tt(P(6, 192 * j, 192 * j + 192), A("nab", 192 * j, 192 * j + 192), P(5, 0, 192), ALU.subtract)
+    act(A("dhl", 0, 384), P(6, 0, 384))
+    tt(A("dhl", 384, 768), P(6, 0, 384), A("dhl", 0, 384), ALU.subtract)
     cp(A("ff", 32, 96), A("pfi", 0, 64))
-    cp(A("fu", 0, 64), A("pfi", 0, 64))
-    cp(A("sdf", 48, 240), A("sdi", 0, 192))
+    ts(A("fu", 0, 64), A("pfi", 0, 64), float(NV), ALU.min)
 
-    def class_lists(t):
-        bank = 4 if t == 0 else 6
+    for t in range(4):
+        fill[0] = t > 0
+        o = P(4, 0, 48) if t == 0 else P(7, 0, 48)
         prs = []
         for i in range(16):
             src = 4 * (i % 4) + t
             for part in (0, 192):
                 prs.append((sh("bm", i, 144 * src), A("shl", part + i // 4, part + 192, 4)))
-        mm(P(bank, 0, 48), prs)
+        mm(o, prs)
         if t == 0:
-            cp(A("sl", 672, 720), P(bank, 0, 48))
-        else:
-            act(A("sdf", 240 * t - 240, 240 * t - 192), P(bank, 0, 48))
-        b0 = 0 if t == 0 else 6
-        for q in range(4):
-            i = 4 * q + t
-            o = P(b0 + (q // 2 if t == 0 or OPT["pc"] == 0 else 0), 192 * (q % 2), 192 * (q % 2) + 192)
-            mm(o, [(sh("bm", l, 144 * i), A("dhl", c0, c0 + 192)) for l, c0 in ((0, 0), (1, 384), (8, 192), (9, 576))])
-            act(A("nnc", BL * t + q, BL * t + BL, 4), o, scale=0.5)
-
-    for t in range(3):
-        fill[0] = t > 0
-        class_lists(t)
+            ts(A("sl", 576, 624), o, 2.0, ALU.mult)
+        act(A("sdf", 48 * t, 48 * t + 48), o, scale=2.0)
+    cp(A("sdf", 192, 384), A("sdi", 0, 192))
+    for b in range(4):
+        act(A("w", BL * b, BL * b + BL), A("h", BL * b, BL * b + BL), scale=0.125)
     fill[0] = False
 
-    send(A("h", 0, 512), [(prv, A("gl0", 0, 512))], [A("gl0", 0, 512)], 1024)
+    send(A("h", 0, 512), [(prv, A("gl0", 0, 512))], [nxt], [A("gl0", 0, 512)], 1024, "k", True)
 
-    first = [False]
+    def prefill(t):
+        for name, mat, c0 in (("a", idb, 0), ("b", id256, BL)):
+            cut = 512 - c0 % 512
+            for lo, hi in ((0, cut), (cut, BL)):
+                mm(A("ps", c0 + lo, c0 + hi), [(mat, A(name, 4 * lo + t, 4 * hi, 4))])
+        for q in range(4):
+            i = 4 * q + t
+            own = OPT["nn"] == "V"
+            if not own and q % 2 == 0:
+                mm(P(3 if q < 2 else 6, 0, 384), [(idb, A("zz", 0, 384))], True, False)
+            mm(rowsof(q), [(sh("bm", l, 144 * i), A("dhl", c0, c0 + 192)) for l, c0 in ((0, 0), (1, 384), (8, 192), (9, 576))], own, own)
+
+    def rowsof(q):
+        return P(3 if q < 2 else 6, 192 * (q % 2), 192 * (q % 2) + 192)
 
     def collapse(t):
-        act(A("bs", BL * t, BL * t + BL), A("b", t, NV, 4), scale=1.0 / 256)
         for c in range(2):
             lo, hi = 384 * c, 384 * c + 384
-            o = (672, 0, 432)[t] + 24 * c
             cls = lambda name: A(name, 4 * lo + t, 4 * hi, 4)
-            dd, c1, c2, d = A("dd", lo, hi), A("c1", lo, hi), A("c2", lo, hi), P(OPT["dbank"][c], 128, 512)
-            tt(dd, G(A(UV[t], 0, K), A("sl", o, o + 24)), cls("a"), ALU.subtract)
-            act(c2, dd, ACT.Abs, bias=-0.5)
-            if OPT["cmp"] == "SV":
+            c1, c2, d, dm = A("c1", lo, hi), A("c2", lo, hi), P(4 + c, 128, 512), A("dm", BL * t + lo, BL * t + hi)
+            if t == 0:
+                off = A("sl", 576 + 24 * c, 600 + 24 * c)
+                if OPT["x0"] == "V":
+                    tt(A("dd", lo, hi), G(A(UV[0], 0, K), off), cls("a"), ALU.subtract)
+                    act(c2, A("dd", lo, hi), ACT.Abs, bias=-128.0)
+                else:
+                    act(A("xs", lo, hi), G(A(UV[0], 0, K), off), bias=-128.0)
+                    mm(d, [(idb, cls("a")), (idn, A("xs", lo, hi))])
+                    act(c2, d, ACT.Abs)
+            else:
+                s = 2.0 ** (t - 10)
+                o = 192 * (t - 1) + 48 * t + 24 * c
+                lin(OPT["xs"][c], cls("x"), G(A(UV[t], 0, K), A("sl", o, o + 24)), bias=-0.5 * s, scale=s)
+                if (t, c) in OPT["direct"]:
+                    ops[-1]["fill"] = True
+                    tt(A("dd", lo, hi), G(A(UV[t], 0, K), A("sl", o, o + 24)), cls("a"), ALU.subtract)
+                    act(c2, A("dd", lo, hi), ACT.Abs, bias=-0.5)
+                else:
+                    mm(d, [(id512 if t == 1 else id256, cls("a"))], True, False)
+                    mm(d, [(idn, cls("x"))], False)
+                    act(c2, d, ACT.Abs, scale=1.0 / s)
+            if OPT["cmp"][t] == "V":
                 ts(c1, c2, A("thf", t, t + 1), ALU.is_le)
             else:
                 act(c1, c2, ACT.Sign, bias=A("thf", 4 + t, 5 + t), scale=-1.0)
+            thr = 8.5 if OPT["cmp"][t] == "V" else 1.0
             mm(d, [(blk, c1)])
-            thr = 8.5 if OPT["cmp"] == "SV" else 1.0
             if OPT["dead"][c] == "S":
-                act(d, d, ACT.Sigmoid, bias=-512.0 * thr, scale=512.0, extra=1300.0 if first[0] else 0.0)
-                first[0] = False
+                act(dm, d, ACT.Sigmoid, bias=-512.0 * thr, scale=512.0)
+                ops[-1]["follow"] = table
             else:
-                ts(d, d, thr, ALU.is_ge)
-            tt(cls("ah"), d, cls("a"), ALU.mult)
-            tt(cls("bh"), d, A("bs", BL * t + lo, BL * t + hi), ALU.mult)
-            tt(cls("nnd"), d, A("nnc", BL * t + lo, BL * t + hi), ALU.mult)
-            act(A("ee", BL * t + lo, BL * t + hi), d, bias=1.0, scale=-1.0)
+                ts(dm, d, thr, ALU.is_ge)
+            tt(cls("ah"), A("ps", lo, hi), dm, ALU.mult)
+            tt(cls("bh"), A("ps", BL + lo, BL + hi), dm, ALU.mult)
+        for q in range(4):
+            dq = A("dm", BL * t + q, BL * t + BL, 4)
+            if OPT["nn"] == "V":
+                tt(A("nnd", 4 * q + t, NV, 16), rowsof(q), dq, ALU.mult)
+            else:
+                mm(rowsof(q), [(A("idk", 0, 128), dq)], False, q % 2 == 1)
+        if OPT["nn"] == "S":
+            for q in range(4):
+                act(A("nnd", 4 * q + t, NV, 16), rowsof(q), ACT.Relu, bias=A("cf", 8, 9))
+
+    marks = {}
 
     def hop(t, k, c):
         lo, hi = 512 * c, 512 * c + 512
         off = A("fu", 32 * c, 32 * c + 32)
         gn, ge = A("gg", 512 + lo, 512 + hi), A("gg", 3 * lo, 3 * lo + 512)
-        pa, pb = P(2 * c, 0, 512), P(2 * c + 1, 0, 512)
-        ga, gb, mq = A("ga", lo, hi), A("gb", lo, hi), A("mq", lo, hi)
+        pa, pb, pv = P(2 * c, 0, 512), P(2 * c + 1, 0, 512), P(4 + c, 0, 512)
+        ga, gb, mqu, mqv = (A(x, lo, hi) for x in ("ga", "gb", "mqu", "mqv"))
         src, dst = (UV[t], "uw") if k == 0 else ("uw", UV[t + 1])
         ub, vb = A(src, lo, hi), A(src, VO + lo, VO + hi)
         un, vn = A(dst, lo, hi), A(dst, VO + lo, VO + hi)
-        how = {x: OPT[x][2 * k + c] for x in ("ga", "gn", "ge")}
-        copy = {"S": act, "V": cp}
-        copy[how["ga"]](ga, G(A("ah", 0, NW), off))
-        act(gb, G(A("bh", 0, NW), off), scale=256.0)
-        copy[how["gn"]](gn, G(A("nnd", 0, NW), off))
+        raw, last, end = t == 0 and k == 0, k == 1, t == 2 and k == 1
+        how = OPT["hop"][t][2 * k + c]
+
+        def mark(name):
+            marks[name, k, c] = len(ops) - 1
+            for late, early in OPT["stag"]:
+                if late == (name, k, c) and early in marks:
+                    ops[-1]["follow"] = marks[early]
+        lin(OPT["ga"][2 * k + c], ga, G(A("ah", 0, NZ), off))
+        lin(OPT["gb"][2 * k + c], gb, G(A("bh", 0, NZ), off), scale=256.0)
+        lin(OPT["gn"][2 * k + c], gn, G(A("nnd", 0, NZ), off))
         f = A("ff", 32 * c + 32, 32 * c + 64)
-        wb, w0 = 4 + c, 0
-        yield
-        pm, pd, pn = P(wb, w0 + 32 - 32 * c, w0 + 64 - 32 * c), P(wb, w0 + 64, w0 + 96), P(wb, w0 + 32 * c, w0 + 32 * c + 32)
-        wrap(pd, "wd", "gg", 512 + lo, 512 + hi)
-        mm(pb, [(idb, vb), (idb, A("hc", 0, 512))])
-        mm(pa, [(idb, ub)], True, False)
-        tt(pa, pb, ga, ALU.mult)
-        mm(pa, [(idb, ub)], False, True)
-        mm(pb, [(idb, vb)], True, False)
-        ts(mq, pa, MAGIC, ALU.add, -MAGIC, ALU.add)
-        if OPT["pc"] == 0:
-            tt(pa, pa, mq, ALU.subtract)
-            tt(pb, pa, gb, ALU.mult)
-            act(un, pa)
+        wb = 4 + c
+        pm, pd, pn = P(wb, 32 - 32 * c, 64 - 32 * c), P(wb, 64, 96), P(wb, 32 * c, 32 * c + 32)
+        less = []
+        if raw:
+            mm(pv, [(idb, vb)])
+            ub, vb = A("uv0", lo, hi), A("uv0", VO + lo, VO + hi)
+            lin(OPT["raw"][c], ub, A(src, lo, hi), bias=-127.5)
+            lin(OPT["raw"][2 + c], vb, A(src, VO + lo, VO + hi), bias=-127.5)
         else:
-            yield
-            pc = P(7, 0, 512)
-            mm(pc, [(idb, gb)])
-            tt(un, pa, mq, ALU.subtract)
-            tt(pb, pc, un, ALU.mult)
-            yield
-        mm(pb, [(idb, vb), (A("idh", 0, 128), gb)], False, True)
-        ts(mq, pb, MAGIC, ALU.add, -MAGIC, ALU.add)
-        tt(vn, pb, mq, ALU.subtract)
-        if how["ge"] == "V":
-            tt(ge, pa if OPT["pc"] == 0 else un, vn, ALU.is_ge)
+            mm(pv, [(idb, vb), (idb, hc)])
+        mm(pa, [(idb, hc)], True, False)
+        mm(pb, [(idb, hc)], True, False)
+        tt(pa, pv, ga, ALU.mult)
+        mark("m1")
+        if not OPT["pd"]:
+            wrap(pd, "wd", "gg", 512 + lo, 512 + hi)
+        elif c == 1:
+            wrap(P(5, 64, 128), "wd", "gg", 512, 1536)
+        mm(pa, [(idb, ub)] + less, False)
+        tt(pb, pa, gb, ALU.mult)
+        mark("m2")
+        mm(pb, [(idb, vb), (idh, gb)] + less, False)
+        if OPT["qu"][t][2 * k + c] == "V":
+            ts(mqu, pa, MAGIC, ALU.add, -MAGIC, ALU.add)
         else:
-            mm(pa, [(idb, un), (A("idn", 0, 128), vn)])
+            act(A("mqt", lo, hi), pa, bias=MAGIC)
+            act(mqu, A("mqt", lo, hi), bias=-MAGIC)
+        mark("qu")
+        if how == "V":
+            tt(pa, pa, mqu, ALU.subtract)
+            if end:
+                act(A("us", lo, hi), pa, bias=-0.5 * 2.0 ** -7, scale=2.0 ** -7)
+            else:
+                act(un, pa)
+        else:
+            tt(un, pa, mqu, ALU.subtract)
+            if end:
+                ts(A("us", lo, hi), un, -0.5, ALU.add, 2.0 ** -7, ALU.mult)
+        ts(mqv, pb, MAGIC, ALU.add, -MAGIC, ALU.add)
+        mark("qv")
+        tt(vn, pb, mqv, ALU.subtract)
+        mark("vn")
+        if how == "V":
+            tt(ge, pa, vn, ALU.is_ge)
+        else:
+            mm(pa, [(idb, un)], True, False)
+            mm(pa, [(idn, vn)], False)
             act(ge, pa, ACT.Sign, bias=0.5)
-        mm(P(wb, w0, w0 + 64), [(idf, A("ff", 64 * c, 64 * c + 64))], True, False)
-        mm(P(wb, w0, w0 + 64), [(sh("q1", i), A("gg", 2 * lo + i, 2 * lo + K, 16)) for i in range(16)], False, True)
+        if end:
+            mm(pb, [(idb, vn), (idb, A("hh", 0, 512))])
+            tt(A("zt", lo, hi), pb, A("us", lo, hi), ALU.mult)
+            act(A("sig", lo, hi), A("zt", lo, hi), ACT.Sigmoid, scale=2.0 ** -6)
+        yield
+        if OPT["pd"]:
+            pd = P(5, 64 + 32 * c, 96 + 32 * c)
+        mm(P(wb, 0, 64), [(idf, A("ff", 64 * c, 64 * c + 64))], True, False)
+        mm(P(wb, 0, 64), [(sh("q1", i), A("gg", 2 * lo + i, 2 * lo + K, 16)) for i in range(16)], False, True)
         sg, t2 = A("sg", 32 * c, 32 * c + 32), A("t2", 32 * c, 32 * c + 32)
-        ts(sg, pn, 8.5 if how["ge"] == "V" else 1.0, ALU.is_ge, -0.5, ALU.add)
+        thr = 8.5 if how == "V" else 1.0
+        if OPT["sg"] == "V":
+            ts(sg, pn, thr, ALU.is_ge, -0.5, ALU.add)
+        else:
+            act(sg, pn, ACT.Sign, bias=-thr)
         tt(t2, pd, sg, ALU.mult)
         tt(f, pm, t2, ALU.add)
         if k == 0:
-            cp(off, f)
+            ts(off, f, float(NV), ALU.min)
 
     def moves(t):
         f, on, sc = A("ff", 32, 96), A("on", 0, 64), A("sc", 0, 64)
-        ts(on, f, 3071.5, ALU.is_ge)
+        if OPT["on"] == "V":
+            ts(on, f, 3071.5, ALU.is_ge)
+        else:
+            act(on, f, ACT.Sigmoid, bias=-3071.5 * 512, scale=512.0)
         add("v", lambda q: q.tensor_tensor_scan(sc["ap"], on["ap"], on["ap"], 0.0, ALU.add, ALU.max), COST["fix"] + 64 * cy, [on], [sc])
+        nv = OPT["accv"][t]
         mm(P(4, 0, 64), [(blk, sc)])
-        mm(P(5, 0, 2), [(blk, A("sc", 62, 64))])
+        mm(P(0, 0, 64), [(blk, sc)])
+        rk = P(2, 0, 64)
         mm(P(5, 64, 128), [(blk, sc), (A("un", 0, 128), on)])
+        mm(rk, [(blk, sc), (A("un4", 0, 128), on)])
         slot = lambda r: A("cin", 16 * t + 4 * r, 16 * t + 4 * r + 1)
-        ts(slot(rank), P(5, 1, 2), 256.0, ALU.min)
+        ts(slot(rank), P(0, 63, 64), 256.0, ALU.min)
         incl = A("cc", 64, 128)
-        cp(incl, P(5, 64, 128))
+        lin(OPT["incl"], incl, P(5, 64, 128))
         others = [r for r in range(n) if r != rank]
-        send(slot(rank), [(T.cores[r], slot(rank)) for r in others], [slot(r) for r in others], 100)
-        nv = OPT["accv"]
-        if nv:
-            mm(P(0, 0, 64), [(blk, sc)])
+        send(slot(rank), [(T.cores[r], slot(rank)) for r in others], [T.cores[r] for r in others], [slot(r) for r in others], 4, "l")
         for c in range(16):
             jk, acc = A("junk", 64 * c, 64 * c + 64), A("acc", c, c + 1)
             if c < nv:
@@ -412,27 +561,23 @@ def build(T, topo, core):
         atu = A("atu", 0, 16)
         cp(atu, P(5, 0, 16))
         uv = UV[t + 1]
-        act(A("snd", 0, 256), G(A(uv, 0, VO), atu))
-        cp(A("snd", 256, 512), G(A(uv, VO, 2 * VO), atu))
-        act(A("atf", 0, 16), P(5, 0, 16))
-        rk = A("rk", 0, 64)
-        act(A("lv0", 0, 64), on, bias=4096.0, scale=-4096.0)
-        tt(rk, incl, A("lv0", 0, 64), ALU.add)
+        utab = A(uv if t < 2 else "us", 0, VO)
+        act(A("snd", 0, 256), G(utab, atu))
+        if t < 2:
+            lin(OPT["sv"], A("snd", 512, 768), G(A(uv, VO, 2 * VO), atu))
+        else:
+            lin(OPT["sv"], A("snd", 512, 768), G(A(uv, VO, 2 * VO), atu), bias=-0.5 * 2.0 ** -6, scale=2.0 ** -6)
         act(A("fc", 0, 64), f, bias=-3328.0)
         act(A("fk", 0, 64), f, bias=256.0, scale=-1.0)
-        if t == 2:
-            ts(A("uc", 0, K), A(uv, 0, K), -0.5, ALU.add)
-            for c in range(2):
-                z = P(2 + c, 0, 512)
-                act(z, A(uv, VO + 512 * c, VO + 512 * c + 512), bias=-0.5)
-                tt(z, z, A("uc", 512 * c, 512 * c + 512), ALU.mult)
-                act(A("sig", 512 * c, 512 * c + 512), z, ACT.Sigmoid, scale=2.0 ** -13, extra=1300.0 if first[0] else 0.0)
-                first[0] = False
-        tt(A("eq", 0, 256), G(A("rk", 0, 72), cu), A("kr", 1, 257), ALU.is_equal)
-        tt(A("snd", 512, 768), G(A("fc", 0, 72), cu), A("eq", 0, 256), ALU.mult)
+        eq = P(4, 256, 512)
+        mm(eq, [(A("lz", 0, 128), A("one", 0, 256))], True, False)
+        mm(eq, [(A("st", 0, 128), A("le", 0, 256))], False)
+        act(A("eq", 0, 256), G(A("fc", 0, 72), cu))
+        tt(A("snd", 256, 512), eq, A("eq", 0, 256), ALU.mult)
         r0 = 768 * t
-        for lo, hi in ((0, 256), (256, 768)) if OPT["split"] else ((0, 768),):
-            send(A("snd", lo, hi), [(nxt, A("rcv", r0 + lo, r0 + hi))], [A("rcv", r0 + lo, r0 + hi)], 2 * (hi - lo))
+        cuts = OPT["cuts"][t]
+        for lo, hi in zip(cuts, cuts[1:]):
+            send(A("snd", lo, hi), [(nxt, A("rcv", r0 + lo, r0 + hi))], [prv], [A("rcv", r0 + lo, r0 + hi)], 2 * (hi - lo), "l")
         m = A("mm", 4 * t, 4 * t + 1)
         cin = A("cin", 16 * t, 16 * t + 13, 4)
         add("v", lambda q: q.tensor_reduce(m["ap"], cin["ap"], AxisListType.X, ALU.min), COST["fix"] + 64 * cy, [cin], [m])
@@ -443,127 +588,241 @@ def build(T, topo, core):
             act(shift, m, bias=A("mm", 4 * t - 4 + min(t - 1, 1), 4 * t - 3 + min(t - 1, 1)))
         ts(A("e1", 0, 16), A("kw", 16, 32), m, ALU.subtract, 2048.0, ALU.mult)
         tt(A("e2", 0, 16), A("e1", 0, 16), A("kw", 32, 48), ALU.min)
-        tt(A("e3", 0, 16), A("e2", 0, 16), A("atf", 0, 16), ALU.max)
+        tt(A("e3", 0, 16), P(5, 0, 16), A("e2", 0, 16), ALU.max)
         asu = A("asu", 0, 16)
         cp(asu, A("e3", 0, 16))
-        lo, hi = ((0, 240), (48, 288), (48, 240))[t]
-        si = A("si", 0, hi - lo)
-        ts(si, A("sdf", lo, hi), shift, ALU.add)
+        lo = 0 if t < 2 else 192
+        si = A("si", 0, 192)
+        ts(si, A("sdf", lo, lo + 192), shift, ALU.add)
         ts(si, si, 1023, ALU.bitwise_and)
-        cp(A("sl", 240 * t, 240 * t + hi - lo), si)
-        ts(A("ro", 0, 64), incl, -1.0, ALU.add, 255.0, ALU.min)
+        if OPT["pre3"][t]:
+            for lo, hi, o in [(144, 192, 24)] if t == 2 else [(48 * c + 36, 48 * c + 48, 12 * c) for c in range(t + 1)]:
+                tt(A("si", lo, hi), A("si", lo, hi), A("md", o, o + hi - lo), ALU.max)
+        cp(A("sl", 192 * t, 192 * t + 192), si)
         lv = A("lv", 0, 64)
-        ts(lv, rk, m, ALU.is_le)
-        cp(G(A(uv, 0, VO), asu), A("rcv", r0, r0 + 256))
+        ts(lv, rk, 4096.0, ALU.add, m, ALU.is_le)
         if t < 2:
-            cp(G(A(uv, VO, 2 * VO), asu), A("rcv", r0 + 256, r0 + 512))
+            prefill(t + 1)
+        cp(G(utab, asu), A("rcv", r0, r0 + 256))
+        if t == 2:
+            yield
+        faces = A("rcv", r0 + 256, r0 + 512)
+        if OPT["gf"][t] == "V":
+            cp(G(A("gf", 0, VO), asu), faces)
         else:
-            z = P(2, 0, 256)
-            act(z, A("rcv", r0, r0 + 256), bias=-0.5 * 2.0 ** -13, scale=2.0 ** -13)
-            ts(A("uc", 0, 256), A("rcv", r0 + 256, r0 + 512), -0.5, ALU.add)
-            tt(A("zr", 0, 256), z, A("uc", 0, 256), ALU.mult)
-            o = G(A("sig", 0, VO), asu)
-            add("s", lambda q: q.activation(o["ap"], T["zr"][:, 0:256], ACT.Sigmoid), COST["fix"] + 256 * COST["sca"] * cy, [A("zr", 0, 256)], [o])
+            ts(A("ro", 0, 64), incl, -1.0, ALU.add, 255.0, ALU.min)
+            for c in range(2):
+                act(A("gf", 512 * c, 512 * c + 512), G(faces, A("ro", 32 * c, 32 * c + 32)))
+        if t < 2:
+            cp(G(A(uv, VO, 2 * VO), asu), A("rcv", r0 + 512, r0 + 768))
+        else:
+            o, z = G(A("sig", 0, VO), asu), A("zt", 0, 256)
+            mm(P(5, 0, 256), [(idb, A("rcv", r0 + 512, r0 + 768))])
+            tt(z, P(5, 0, 256), A("rcv", r0, r0 + 256), ALU.mult)
+            add("s", lambda q: q.activation(o["ap"], z["ap"], ACT.Sigmoid), COST["fix"] + 256 * COST["sca"] * cy, [z], [o])
             act(P(5, 0, 512), A("sig", 512, K))
-        for c in range(2):
-            act(A("gf", 512 * c, 512 * c + 512), G(A("rcv", r0 + 512, r0 + 768), A("ro", 32 * c, 32 * c + 32)))
-        pf = P(0 if t < 2 else 4, 0, 64)
+        pf = (P(3, 384, 448) if OPT["nn"] == "V" else P(7, 384, 448)) if t < 2 else P(4, 256, 320)
         mm(pf, [(idf, A("fk", 0, 64))], True, False)
         mm(pf, [(sh("q1", i), A("gf", i, K, 16)) for i in range(16)], False, True)
         tt(A("t2", 0, 64), pf, lv, ALU.mult)
         tt(f, A("t2", 0, 64), f, ALU.add)
-        cp(A("fu", 0, 64), f)
+        if t < 2:
+            ts(A("fu", 0, 64), f, float(NV), ALU.min)
+        else:
+            cp(A("fu", 0, 64), f)
 
     def follower_lists(t):
         for j, mat in ((0, "w0"), (1, "w1")):
-            o = P(6 + j, 0, 48) if OPT["pc"] == 0 else P(6, 64 * j, 64 * j + 48)
+            o = P(7, 64 * j, 64 * j + 48)
             mm(o, [(sh(mat, i), A("nnd", 4 * i + t, NV, 64)) for i in range(16)] + [(idf, A("sf", 0, 48))])
             ts(A("nl", 144 * j + 48 * t, 144 * j + 48 * t + 48), o, float(t), ALU.add)
+        if t < 2 and any(OPT["pre3"][t:2]):
+            o = P(7, 128, 140)
+            wrap(o, "q1", "dm", BL * t + 576, BL * t + BL)
+            act(A("md", 12 * t, 12 * t + 12), o, scale=ZC / 16.0)
+        if t < 2 and OPT["pre3"][t]:
+            ghosts(t)
+            correct(t, 3)
+        if t == 2 and OPT["pre3"][t]:
+            o = P(7, 128, 176)
+            mm(o, [(sh("q1", i), A("dm", BL * (i % 4) + 576 + i // 4, BL * (i % 4) + BL, 4)) for i in range(16) if i % 4 < 3])
+            act(A("md", 24, 72), o, scale=ZC / 16.0)
 
-    def heights(t):
-        s = 2.0 ** (t - 9)
+    def ghosts(t):
         if t == 0:
             act(A("w", NV, NW), A("gl0", 0, 512), scale=0.25)
         else:
             act(A("w", NV, NW), A("gl", 512 * t - 512, 512 * t), scale=2.0)
-        if "V" in OPT["xh"][t]:
-            ts(A("us", 0, K), A(UV[t + 1], 0, K), -0.5, ALU.add, s, ALU.mult)
-        xs = "x%d" % t
-        base = (48, 240, 480)[t]
+            for c in range(t if OPT["gs"] else 0):
+                o = 128 * (t - 1 + c)
+                lin(OPT["gs"][c], A("w", NV + c, NW, 4), A("gr", o, o + 128), scale=2.0)
+
+    def live(b):
+        for c in range(2):
+            how = OPT["xl"][b][c]
+            lo, hi = BL * b + 384 * c, BL * b + 384 * c + 384
+            g = G(A("us", 0, VO), A("sl", 384 + lo // 16, 384 + hi // 16))
+            if how == "V":
+                tt(A("w", lo, hi), g, A("w", lo, hi), ALU.add)
+                continue
+            act(A("x", lo, hi), g)
+            if how == "A":
+                o = P(6 + b % 2, 0, 384) if OPT["oh"] == "D" or OPT["early"] else P(3 + b % 2, 128, 512)
+                mm(o, [(idf, A("w", lo, hi))], True, False)
+                mm(o, [(idb, A("x", lo, hi))], False, True)
+                act(A("w", lo, hi), o)
+        if OPT["xl"][b] == "DD":
+            dadd(A("w", BL * b, BL * b + BL), A("x", BL * b, BL * b + BL))
+
+    yh = {"ap": T.yh[:], "reg": [("yh", 0, BL, 1)], "n": BL}
+
+    def total(b):
+        src = A("w", BL * b, BL * b + BL)
+        if OPT["oh"] == "D":
+            if b == 3:
+                store(yh, src, "y", 3072)
+            else:
+                dadd(yh, src)
+        elif b > 0 or OPT["oh"] == "P":
+            for bank, lo, hi in ((7, 512, BL), (6, 0, 512)):
+                mm(P(bank, 0, hi - lo), [(idf, A("w", BL * b + lo, BL * b + hi))], b == 3, b == (0 if OPT["oh"] == "P" else 1))
+
+    def heights(t):
+        s = 2.0 ** (t - 9)
+        if not OPT["pre3"][t]:
+            ghosts(t)
+        parts = OPT["xparts"][t]
+        for k in range(parts - 1, -1, -1):
+            m = 48 // parts
+            for c in range(4):
+                if c != t + 1:
+                    o = 192 * t + 48 * c + m * k
+                    lin(OPT["xc"][t][c], A("x", 64 * m * k + c, 64 * m * (k + 1), 4), G(A(UV[t + 1], 0, VO), A("sl", o, o + m)), bias=-0.5 * s, scale=s)
+        cuts = OPT["dcuts"][t]
+        for hi, lo in zip(cuts, cuts[1:]):
+            dadd(A("w", BL * lo, BL * hi), A("x", BL * lo, BL * hi))
+        gl = A("gl", 512 * t, 512 * t + 512)
+        if OPT["gs"]:
+            send(A("w", 0, 512), [(prv, gl)], [nxt], [gl], 2048, "k")
+        for b in range(2 if OPT["pre3"][t] else 3, -1, -1):
+            correct(t, b)
+        if OPT["gs"]:
+            gr = A("gr", 128 * t, 256 * t + 128)
+            send(A("gs", 128 * t, 256 * t + 128), [(prv, gr)], [nxt], [gr], 512 * (t + 1), "k")
+        else:
+            send(A("w", 0, 512), [(prv, gl)], [nxt], [gl], 2048, "k")
+
+    def factors():
         for b in range(3, -1, -1):
-            how = OPT["xh"][t][b]
-            for c in range(2):
-                lo, hi = BL * b + 384 * c, BL * b + 384 * c + 384
-                off = A("sl", base + lo // 16, base + hi // 16)
-                if how == "V":
-                    tt(A("w", lo, hi), G(A("us", 0, K), off), A("w", lo, hi), ALU.add)
-                    continue
-                act(A(xs, lo, hi), G(A(UV[t + 1], 0, K), off), bias=-0.5 * s, scale=s)
-                o = P(3 + c if t == 2 else 6 + c * (1 - OPT["pc"]), 0, 384)
-                if how == "P":
-                    mm(o, [(idb, A(xs, lo, hi))])
-                    tt(A("w", lo, hi), o, A("w", lo, hi), ALU.add)
-                else:
-                    mm(o, [(A("id8", 0, 128), A("h", lo, hi))] + [(idb, A("x%d" % j, lo, hi)) for j in range(t + 1)])
-                    if how == "A":
-                        act(A("w", lo, hi), o)
-                    else:
-                        cp(A("w", lo, hi), o)
+            for c in range(3):
+                i = 192 * (3 * (3 - b) + c)
+                cut = min(192, 512 - i % 512)
+                for lo, hi in ((0, cut), (cut, 192)):
+                    if lo < hi:
+                        d0 = BL * c + 192 * b
+                        mm(A("ps", i + lo, i + hi), [(id256, A("ah", BL * b + 4 * lo + c, BL * b + 4 * hi, 4)), (idn, A("dm", d0 + lo, d0 + hi)), (idb, A("one", lo, hi))])
+
+    def correct(t, b):
+        if True:
             win = A("w", BL * b, NW)
-            adds = []
+            m = 128 if b == 0 and t < 2 else 192
+            adds, work = [], []
+            hows = OPT["corr"][t][b]
             for c in range(t + 1):
-                bank = 6 + c if t < 2 else c
-                lo, hi = BL * b + c, BL * b + BL
-                l0 = A("nl", 48 * c + 12 * b, 48 * c + 12 * b + 12)
-                l1 = A("nl", 144 + 48 * c + 12 * b, 144 + 48 * c + 12 * b + 12)
-                h1, h2, p2 = (A(x, 192 * c, 192 * c + 192) for x in ("h1", "h2", "p2"))
-                pa = P(bank, 0, 192) if t == 2 or OPT["pc"] == 0 else P(6, 192 * c, 192 * c + 192)
-                mm(pa, [(A("id256", 0, 128), A("ah", lo, hi, 4)), (idb, A("ee", BL * c + 192 * b, BL * c + 192 * b + 192))])
-                act(h1, G(win, l0))
-                if OPT["corr"][t] == "A":
-                    pb = P(bank, 192, 384)
-                    mm(pb, [(idb, A("bh", lo, hi, 4))])
-                    act(h2, G(win, l1))
-                    tt(p2, pb, h2, ALU.mult)
+                lo, hi = BL * b + c, BL * b + 4 * m
+                l0 = A("nl", 48 * c + 12 * b, 48 * c + 12 * b + m // 16)
+                l1 = A("nl", 144 + 48 * c + 12 * b, 144 + 48 * c + 12 * b + m // 16)
+                h1, p2 = (A(x, m * c, m * c + m) for x in ("h1", "p2"))
+                if t == 2 and OPT["early"]:
+                    i = 192 * (3 * (3 - b) + c)
+                    pa = pr = A("ps", i, i + 192)
+                elif t == 2:
+                    pa, pr = P(c // 2, m * (c % 2), m * (c % 2) + m), P(2 + c, 0, m)
+                elif "P" in hows or "M" in hows or b == 0 and OPT["gs"]:
+                    pa, pr = P(6, m * c, m * c + m), P(7, m * c, m * c + m)
                 else:
-                    tt(p2, G(win, l1), A("bh", lo, hi, 4), ALU.mult)
-                tt(pa, pa, h1, ALU.mult)
-                adds.append((A("w", lo, hi, 4), pa, p2))
-            for o, pa, p2 in adds:
-                tt(o, pa, p2, ALU.add)
-        if t < 2:
-            gl = A("gl", 512 * t, 512 * t + 512)
-            send(A("w", 0, 512), [(prv, gl)], [gl], 2048)
+                    pa, pr = P(6 + c, 0, m), None
+                d0 = BL * c + 192 * b
+                if t < 2 or not OPT["early"]:
+                    mm(pa, [(id256, A("ah", lo, hi, 4)), (idn, A("dm", d0, d0 + m)), (idb, A("one", 0, m))])
+                act(h1, G(win, l0))
+                tt(p2, G(win, l1), A("bh", lo, hi, 4), ALU.mult)
+                work.append((hows[c], A("w", lo, hi, 4), pa, pr, h1, p2))
+            k = m * (t + 1)
+            if t < 2 and b == 0 and OPT["gs"]:
+                tt(P(6, 0, k), P(6, 0, k), A("h1", 0, k), ALU.mult)
+                tt(A("gs", 128 * t, 128 * t + k), P(6, 0, k), A("p2", 0, k), ALU.add)
+            elif t < 2 and "M" in hows:
+                tt(P(6, 0, k), P(6, 0, k), A("h1", 0, k), ALU.mult)
+                for how, o, pa, pr, h1, p2 in work:
+                    tt(o, pa, p2, ALU.add)
+            elif t < 2 and "P" in hows:
+                mm(P(7, 0, k), [(idb, A("hc", 0, k))], True, False)
+                tt(P(7, 0, k), P(6, 0, k), A("h1", 0, k), ALU.mult)
+                mm(P(7, 0, k), [(idf, A("p2", 0, k))], False)
+                for how, o, pa, pr, h1, p2 in work:
+                    act(o, pr)
+            else:
+                for how, o, pa, pr, h1, p2 in work:
+                    if how == "P":
+                        mm(pr, [(idb, A("hc", 0, m))], True, False)
+                        tt(pr, pa, h1, ALU.mult)
+                        mm(pr, [(idf, p2)], False)
+                    elif t == 2:
+                        tt(pr, pa, h1, ALU.mult)
+                    else:
+                        tt(pa, pa, h1, ALU.mult)
+                        pr = pa
+                    adds.append((how, o, pr, p2))
+                for how, o, pr, p2 in adds:
+                    if how == "P":
+                        act(o, pr)
+                    else:
+                        tt(o, pr, p2, ALU.add)
 
     def outputs():
-        for bank, lo, hi in ((6, 0, 512), (7, 512, BL)):
-            mm(P(bank, 0, hi - lo), [(idf, A("w", BL * b + lo, BL * b + hi)) for b in (3, 2, 1)])
         win = A("w", 0, NW)
         act(A("hb", 0, 512), G(win, A("fu", 32, 64)))
         tt(A("pa", 0, 512), G(win, A("fu", 0, 32)), A("sig", 0, 512), ALU.mult)
         z = P(5, 0, 512)
         tt(z, z, A("hb", 0, 512), ALU.mult)
         tt(A("ow", 0, 512), z, A("pa", 0, 512), ALU.add)
-        tt(A("oh", 0, BL), P(6, 0, BL), A("w", 0, BL), ALU.add)
-        store(T.yw[:], A("ow", 0, 512), "y", 2048)
-        store(T.yh[:], A("oh", 0, BL), "y", 3072)
+        if OPT["oh"] == "P":
+            act(A("oh", 512, BL), P(7, 0, 256))
+            act(A("oh", 0, 512), P(6, 0, 512))
+        elif OPT["oh"] == "V":
+            tt(A("oh", 0, BL), P(6, 0, BL), A("w", 0, BL), ALU.add)
+        store({"ap": T.yw[:], "reg": [("yw", 0, 512, 1)]}, A("ow", 0, 512), "y", 2048)
+        if OPT["oh"] != "D":
+            store(yh, A("oh", 0, BL), "y", 3072)
 
+    prefill(0)
     for t in range(3):
         collapse(t)
         fill[0] = True
+        if t > 0:
+            heights(t - 1)
         follower_lists(t)
         fill[0] = False
         for k in range(2):
-            halves = [hop(t, k, 0), hop(t, k, 1)]
-            for _ in range(4):
+            halves = [hop(t, k, c) for c in range(2)]
+            for _ in range(2):
                 for x in halves:
                     next(x, None)
-        moves(t)
-        if t < 2:
-            fill[0] = True
-            heights(t)
-            fill[0] = False
-    heights(2)
+        rest = moves(t)
+        next(rest, None)
+    ghosts(2)
+    if OPT["early"]:
+        factors()
+    if OPT["pre3"][2]:
+        correct(2, 3)
+    for b in range(3, -1, -1):
+        live(b)
+    next(rest, None)
+    for b in range(3, -1, -1):
+        if b < 3 or not OPT["pre3"][2]:
+            correct(2, b)
+        total(b)
     outputs()
     return ops
 
@@ -600,7 +859,7 @@ def graph(ops):
     for op in ops:
         p = {i: 0.0 for i in op["order"]}
         if op["kind"] == "recv":
-            p[op["after"]] = ops[op["after"]]["lat"]
+            p[op["after"]] = ops[op["after"]]["lead"]
         for i in op["wait"]:
             near = ops[i]["eng"] == op["eng"]
             p[i] = ops[i].get("lat", 0.0) + (COST["own"] if near else COST["lat"])
@@ -622,13 +881,11 @@ def graph(ops):
 def place(eng, dur, pred, succ, pri, rel):
     n = len(eng)
     left = [len(p) for p in pred]
-    ready = [j for j in range(n) if left[j] == 0]
+    ready = sorted((pri[j], j) for j in range(n) if left[j] == 0)
     start, can = [0.0] * n, list(rel)
-    busy = {e: ([], []) for e in "vspgy"}
-    urgent = lambda x: pri[x]
+    busy = {e: ([], []) for e in "vspgylk"}
     while ready:
-        j = max(ready, key=urgent)
-        ready.remove(j)
+        j = ready.pop()[1]
         t, d = can[j], dur[j]
         if eng[j] is not None:
             a, b = busy[eng[j]]
@@ -652,7 +909,12 @@ def place(eng, dur, pred, succ, pri, rel):
                 can[s] = t + x
             left[s] -= 1
             if left[s] == 0:
-                ready.append(s)
+                x = (pri[s], s)
+                if not ready or x >= ready[-1]:
+                    ready.append(x)
+                else:
+                    ready.append(x)
+                    ready.sort()
     return start
 
 
@@ -664,36 +926,99 @@ def schedule(ops):
         for i, d in pred[j].items():
             succ[i][j] = d
     eng, dur = [o["eng"] for o in ops], [o["dur"] + 1e-3 for o in ops]
-    tail, zero = [o.get("lat", 0.0) for o in ops], [0.0] * n
-    pri = [0.0] * n
+    tail = [o.get("lat", 0.0) for o in ops]
+    chain = [0.0] * n
     for j in range(n - 1, -1, -1):
-        pri[j] = dur[j] + max([pri[s] + d for s, d in succ[j].items()] + [tail[j]])
-    best = None
+        chain[j] = dur[j] + max([chain[s] + d for s, d in succ[j].items()] + [tail[j]])
     rng = numpy.random.default_rng(OPT["seed"])
-    chain = pri
-    later = OPT["later"]
-    cur = None
+    seeds = [[chain[j] - (x if ops[j]["fill"] else 0.0) for j in range(n)] for x in OPT["later"]]
     main = [j for j in range(n) if not ops[j]["fill"]]
-    for it in range(OPT["passes"]):
-        if it < len(later):
-            pri = [chain[j] - (later[it] if ops[j]["fill"] else 0.0) for j in range(n)]
+    start = anneal(eng, dur, pred, succ, [0.0] * n, tail, seeds, main, OPT["passes"], OPT["pull"], OPT["warm"], rng)
+    for _ in range(OPT["sweeps"]):
+        lo = -float(rng.random()) * OPT["wide"]
+        while lo < max(start):
+            seq = sorted(range(n), key=lambda j: (start[j], j))
+            rest, behind, free = [0.0] * n, {}, {}
+            for j in reversed(seq):
+                rest[j] = dur[j] + max([rest[s] + d for s, d in succ[j].items()] + [tail[j], behind.get(eng[j], 0.0)])
+                if start[j] >= lo + OPT["wide"]:
+                    behind[eng[j]] = rest[j]
+            part = [j for j in seq if lo <= start[j] < lo + OPT["wide"]]
+            for j in seq:
+                if start[j] < lo:
+                    free[eng[j]] = start[j] + dur[j]
+            at = {j: k for k, j in enumerate(part)}
+            if len(part) > 1:
+                rel = [max([start[i] + dur[i] + d for i, d in pred[j].items() if i not in at] + [free.get(eng[j], 0.0)]) for j in part]
+                end = [max([rest[s] + d for s, d in succ[j].items() if s not in at] + [tail[j], behind.get(eng[j], 0.0)]) for j in part]
+                new = anneal([eng[j] for j in part], [dur[j] for j in part], [{at[i]: d for i, d in pred[j].items() if i in at} for j in part],
+                             [{at[i]: d for i, d in succ[j].items() if i in at} for j in part], rel, end, [[-start[j] for j in part]],
+                             [k for k, j in enumerate(part) if not ops[j]["fill"]] or [0], OPT["tries"], OPT["near"], OPT["cool"], rng)
+                seq = [j for j in seq if start[j] < lo] + sorted(part, key=lambda j: (new[at[j]], j)) + [j for j in seq if start[j] >= lo + OPT["wide"]]
+                free = {}
+                for j in seq:
+                    start[j] = max([start[i] + dur[i] + d for i, d in pred[j].items()] + [free.get(eng[j], 0.0)])
+                    free[eng[j]] = start[j] + dur[j]
+            lo += 0.5 * OPT["wide"]
+    seq = sorted(range(n), key=lambda j: (start[j], j))
+    order = {e: [j for j in seq if eng[j] == e] for e in "vspgylk"}
+    return order, start, [start[j] + dur[j] + tail[j] for j in range(n)]
+
+
+def anneal(eng, dur, pred, succ, zero, tail, seeds, main, passes, pull, warm, rng):
+    n = len(eng)
+    best = cur = None
+
+    def queued(start):
+        ends = {(eng[j], round(start[j] + dur[j])): j for j in range(n)}
+        j = max(range(n), key=lambda x: start[x] + dur[x] + tail[x])
+        pairs = []
+        while j is not None:
+            by = [i for i, d in pred[j].items() if abs(start[i] + dur[i] + d - start[j]) < 0.5]
+            if by:
+                j = by[int(rng.integers(len(by)))]
+            else:
+                i = ends.get((eng[j], round(start[j])))
+                if i is not None:
+                    pairs.append((i, j))
+                j = i
+        return pairs
+
+    for it in range(passes):
+        if it >= len(seeds) and cur[2] is None:
+            cur[2] = queued(cur[1])
+        if it < len(seeds):
+            pri = seeds[it]
+        elif cur[2] and float(rng.random()) < OPT["aim"]:
+            pri = [-x for x in cur[1]]
+            for _ in range(int(rng.integers(1, 3))):
+                a, b = cur[2][int(rng.integers(len(cur[2])))]
+                gain = (cur[1][b] - cur[1][a] + 1.0) * (1.0 + 3.0 * float(rng.random()) ** 2)
+                if float(rng.random()) < 0.5:
+                    todo, edge, sign = [b], pred, 1.0
+                else:
+                    todo, edge, sign = [a], succ, -1.0
+                seen, t0 = set(todo), cur[1][todo[0]]
+                for j in todo:
+                    pri[j] += sign * gain
+                    for i in edge[j]:
+                        if i not in seen and abs(cur[1][i] - t0) < OPT["reach"]:
+                            seen.add(i)
+                            todo.append(i)
         else:
             shake = (rng.random(n) * OPT["noise"] * float(rng.random()) ** 2).tolist()
-            lo = float(rng.random()) * max(cur[1]) - 0.5 * OPT["span"]
+            lo = min(cur[1]) + float(rng.random()) * (max(cur[1]) - min(cur[1])) - 0.5 * OPT["span"]
             pri = [(shake[j] if lo <= cur[1][j] < lo + OPT["span"] else 0.0) - cur[1][j] for j in range(n)]
         start = place(eng, dur, pred, succ, pri, zero)
-        for _ in range(3 if it < len(later) else 1):
+        for _ in range(3 if it < len(seeds) > 1 else int(it % OPT["every"] == 1)):
             back = place(eng, dur, succ, pred, [start[j] + dur[j] for j in range(n)], tail)
             start = place(eng, dur, pred, succ, [back[j] + dur[j] for j in range(n)], zero)
-        end = max(start[j] + dur[j] + tail[j] for j in range(n)) + OPT["pull"] * sum(start[j] for j in main) / len(main)
+        end = max(start[j] + dur[j] + tail[j] for j in range(n)) + pull * sum(start[j] for j in main) / len(main)
         if best is None or end < best[0]:
             best = (end, start)
-        if cur is None or end <= cur[0] + OPT["warm"] * (1.0 - it / OPT["passes"]) * (it >= len(later)):
-            cur = (end, start)
-    start = best[1]
-    seq = sorted(range(n), key=lambda j: (start[j], j))
-    order = {e: [j for j in seq if eng[j] == e] for e in "vspgy"}
-    return order, start, [start[j] + dur[j] + tail[j] for j in range(n)]
+        if cur is None or end <= cur[0] + warm * (1.0 - it / passes) * (it >= len(seeds)):
+            cur = [end, start, None]
+    return best[1]
 
 
 PLAN = {}
@@ -720,7 +1045,7 @@ def rank_program(g, core, T, topo):
     known = {e: {} for e in "vspgy"}
     for j in sorted(range(len(ops)), key=lambda x: (start[x], x)):
         op = ops[j]
-        if op["eng"] is None:
+        if op["kind"] == "recv":
             op["clock"] = {}
             continue
         seen = known[op["eng"]]

@@ -6,10 +6,13 @@ from concourse.mybir import AluOpType, AxisListType, ActivationFunctionType
 F32, BF, I32, U16 = "float32", "bfloat16", "int32", "uint16"
 NV, NW, BL, K = 3072, 3584, 768, 1024
 NZ = NV + 32
-ZC = 1280
-VO = 1296
+ZC = K
+SPARE = K + 16
+VO = SPARE + 256
 UV = ("uv", "uv0", "uv", "uv0")
-MAGIC = 1.5 * 2.0 ** 31
+BIG = 2.0 ** 21
+EDGE = NV - 0.5
+HALF = 127.5 / 256
 
 
 def _sb(n, d):
@@ -18,49 +21,51 @@ def _sb(n, d):
 
 SCRATCH = {
     "ps": ("psum", [128, 4096], F32),
-    "a": _sb(NV, BF), "b": _sb(NV, BF), "h": _sb(NV, BF),
-    "uv": _sb(2 * VO, BF), "uv0": _sb(2 * VO, BF), "uw": _sb(2 * VO, BF), "us": _sb(VO, BF), "md": _sb(72, F32), "gs": _sb(384, F32), "gr": _sb(384, F32), "mqt": _sb(K, F32), "idk": _sb(128, BF), "zz": _sb(NZ // 4, BF),
-    "mqu": _sb(K, BF), "mqv": _sb(K, F32), "hc": _sb(512, BF), "one": _sb(256, BF), "un4": _sb(128, BF), "lz": _sb(128, BF), "st": _sb(128, BF), "ro": _sb(64, U16), "hh": _sb(512, BF),
+    "a": _sb(NV, BF), "b": _sb(NV, BF), "zz": _sb(NZ // 4, BF),
+    "uv": _sb(2 * VO, BF), "uv0": _sb(2 * VO, BF), "uw": _sb(2 * VO, BF), "us": _sb(VO, BF),
+    "md": _sb(72, BF), "id512": _sb(128, BF), "gs": _sb(384, F32), "gr": _sb(384, F32), "gl": _sb(1024, F32),
+    "mqu": _sb(K, I32), "mqv": _sb(K, I32), "one": _sb(512, BF),
     "nab": _sb(384, I32), "sdi": _sb(192, I32), "pfi": _sb(64, I32), "thi": _sb(4, I32),
-    "ci": _sb(4, I32), "cf": _sb(16, F32), "cb": _sb(8, BF), "kr": _sb(272, BF), "r16": _sb(128, BF),
+    "ci": _sb(4, I32), "cf": _sb(24, F32), "cb": _sb(8, BF), "kr": _sb(272, BF), "r16": _sb(128, BF),
     "q1": _sb(144, BF), "wd": _sb(144, BF), "w0": _sb(144, BF), "w1": _sb(144, BF),
-    "blk": _sb(128, BF), "idb": _sb(128, BF), "idn": _sb(128, BF), "idh": _sb(128, BF), "id256": _sb(128, BF), "id512": _sb(128, BF), "idf": _sb(128, F32),
-    "un": _sb(128, BF), "un0": _sb(128, BF), "i16": _sb(16, F32), "bm": _sb(16 * 144, BF),
-    "kw": _sb(64, F32), "fw": _sb(16, F32), "sf0": _sb(48, F32), "sf": _sb(48, F32),
-    "thf": _sb(8, F32), "shl": _sb(384, BF), "dhl": _sb(768, BF),
+    "blk": _sb(128, BF), "blm": _sb(128, BF), "idb": _sb(128, BF), "idn": _sb(128, BF), "idh": _sb(128, BF), "id256": _sb(128, BF),
+    "idk": _sb(128, BF), "id64": _sb(128, BF), "id32": _sb(128, BF), "idf": _sb(128, F32),
+    "tri": _sb(128, BF), "tr4": _sb(128, BF), "st": _sb(256, BF), "su": _sb(256, BF),
+    "i16": _sb(16, F32), "bm": _sb(16 * 144, BF),
+    "kw": _sb(32, F32), "fw": _sb(16, F32), "sf0": _sb(48, F32), "sf": _sb(48, F32), "kt": _sb(K, BF), "jt": _sb(512, BF),
+    "thf": _sb(8, F32), "shl": _sb(192, "float16"), "dhl": _sb(768, BF),
     "nnd": _sb(NZ, BF), "ah": _sb(NZ, BF), "bh": _sb(NZ, BF), "dm": _sb(3 * BL, BF),
-    "sdf": _sb(384, F32), "si": _sb(192, I32), "sl": _sb(624, U16),
+    "sdf": _sb(384, F32), "si": _sb(192, BF), "sl": _sb(624, U16),
     "dd": _sb(BL, F32), "xs": _sb(BL, BF), "c1": _sb(BL, BF), "c2": _sb(BL, BF),
     "ff": _sb(128, F32), "fu": _sb(64, U16), "sg": _sb(64, F32), "t2": _sb(64, F32),
     "ga": _sb(K, BF), "gb": _sb(K, BF), "gg": _sb(2 * K, BF),
-    "on": _sb(64, BF), "sc": _sb(64, BF), "cc": _sb(136, F32), "rk": _sb(72, F32), "fc": _sb(72, F32),
-    "junk": _sb(K, BF), "acc": _sb(16, F32), "cu": _sb(16, U16), "cx": _sb(16, F32),
-    "le": _sb(256, BF), "eq": _sb(256, BF), "atf": _sb(16, F32), "atu": _sb(16, U16), "asu": _sb(16, U16),
+    "on": _sb(64, BF), "sc": _sb(80, BF), "cc": _sb(64, F32), "fc": _sb(64, F32),
+    "sk": _sb(K, F32), "ek": _sb(16, F32), "rr": _sb(16, BF), "cu": _sb(16, U16), "ro": _sb(4, U16), "hs": _sb(272, F32),
+    "le": _sb(256, BF), "eq": _sb(256, BF), "atu": _sb(16, U16), "asu": _sb(16, U16),
     "e1": _sb(16, F32), "e2": _sb(16, F32), "e3": _sb(16, F32),
-    "cin": _sb(48, F32), "mm": _sb(12, F32), "lv": _sb(64, F32), "lv0": _sb(64, F32),
-    "fk": _sb(64, F32), "gf": _sb(VO, BF),
-    "snd": _sb(768, BF), "rcv": _sb(3 * 768, BF),
-    "gl0": _sb(512, BF), "gl": _sb(1024, F32),
+    "cin": _sb(60, F32), "mm": _sb(12, F32), "lv": _sb(64, F32), "fk": _sb(64, F32), "fl": _sb(64, F32),
+    "snd": _sb(768, BF), "rcv": _sb(3 * 768, BF), "ru": _sb(6 * K, BF), "ra": _sb(48, U16),
     "w": _sb(NW, F32), "x": _sb(NV, BF),
     "nl": _sb(6 * 48, U16), "h1": _sb(3 * 192, F32), "p2": _sb(3 * 192, F32),
-    "zt": _sb(K + 16, F32), "sig": _sb(VO, F32), "pa": _sb(512, F32), "hb": _sb(512, F32),
+    "zt": _sb(K + 16, F32), "sig": _sb(VO, F32), "sa": _sb(512, F32), "pa": _sb(512, F32), "hb": _sb(512, F32),
     "oh": _sb(BL, F32), "ow": _sb(512, F32),
 }
-SEMAPHORES = ["cv", "cs", "cp", "cg"] + ["d%d" % i for i in range(40)] + ["l%d" % i for i in range(20)] + ["r%d" % i for i in range(20)]
+SEMAPHORES = ["cv", "cs", "cp", "cg"] + ["d%d" % i for i in range(48)] + ["l%d" % i for i in range(32)] + ["r%d" % i for i in range(32)]
 COUNTER = {"v": "cv", "s": "cs", "p": "cp", "g": "cg"}
 
-COST = {"cyc": 1.0, "pe": 0.52, "gat": 1.55, "sca": 3.8, "fix": 60.0, "lat": 120.0, "own": 120.0, "remote": 1800.0, "rows": 800.0, "link": 1.4, "rissue": 900.0,
+COST = {"cyc": 0.95, "pe": 0.49, "mm": 3.0, "gat": 1.55, "sca": 3.8, "fix": 60.0, "lat": 120.0, "own": 120.0, "remote": 1800.0, "rows": 800.0, "link": 1.4, "rissue": 900.0,
         "gissue": 900.0, "glat": 3000.0}
 OPT = {
-    "corr": [["M"] * 4, ["MM"] * 4, ["BBB"] * 4], "cmp": "VVV", "sg": "S", "on": "V", "incl": "S",
-    "hop": ["SVSV", "SVSV", "SSSV"],
+    "corr": [["M"] * 4, ["MM"] * 4, ["BBB"] * 4], "cmp": "VVV",
+    "hop": ["SVSV", "SVSV", "SSSS"],
     "ga": "SSSS", "gb": "SSSS", "gn": "SSSS",
     "stag": [(("m2", 0, 1), ("vn", 0, 0)), (("m2", 1, 1), ("vn", 1, 0))],
-    "cuts": [(0, 256, 512, 768), (0, 256, 512, 768), (0, 256, 768)], "gs": "SS", "dcuts": [(4, 2, 0), (4, 2, 0)], "pd": 1, "early": 1,
-    "direct": [(1, 0), (2, 0)], "xparts": [2, 2], "nn": "S", "qu": ["VVVV"] * 3, "blank": ["ah", "bh"], "x0": "V", "xs": "SS", "xc": ["SSSS", "SSSS"],
-    "xl": ["DD", "DD", "VV", "VV"], "pre3": [1, 1, 0], "dead": "SS", "oh": "P", "accv": [6, 6, 3], "gf": "VVS", "sv": "S", "zero": "gVVg",
+    "early": ["u", "u", "u"], "parts": ["uvf", "uvf", "uvf"], "accs": [4, 4, 4], "last": ["MB", "MP", "MP", "MP"], "turn": (0, 1, 2), "sums": (3, 0, 1, 2), "rest": 2,
+    "cuts": [(256, 512, 768), (256, 512, 768), (256, 768)], "dcuts": [(4, 2, 0), (4, 2, 0)],
+    "loads": ["b", "na", "nb", "pf", "v", "bh", "nnd"], "direct": [(), (), ()],
+    "xparts": [2, 2], "x0": "VV", "xs": ["VS", "SS"], "xc": ["SSSS", "SSSS"], "gr": "S", "us": "SS",
+    "xl": ["DD", "DD", "VV", "VV"], "pre3": [1, 1, 0], "dead": "SS", "oh": "P", "sv": "S", "su": "S", "bm0": "VSVS",
     "sweeps": 8, "wide": 24000.0, "tries": 300, "near": 0.5, "cool": 100.0,
-    "raw": "VVSS",
     "aim": 0.85, "reach": 2000.0, "every": 10, "passes": 9000, "noise": 4000.0, "span": 10000.0, "later": [0.0, 5e3, 1e4, 2e4, 4e4, 1e6], "seed": 1, "pull": 3.0, "warm": 250.0}
 
 
@@ -126,14 +131,15 @@ def build(T, topo, core):
     def ms(out, val):
         add("v", lambda q: q.memset(out["ap"], val), vcost(out, [out]), [], [out])
 
-    def act(out, i0, func=None, bias=0.0, scale=1.0, acc=None, extra=0.0):
+    def scan(out, d0, d1, first, op0, op1):
+        add("v", lambda q: q.tensor_tensor_scan(out["ap"], d0["ap"], d1["ap"], ap(first), op0, op1), vcost(out, [d0, d1]), [d0, d1, first], [out])
+
+    def act(out, i0, func=None, bias=0.0, scale=1.0, extra=0.0, acc=None):
         f = ACT.Identity if func is None else func
         c = COST["gat"] if i0["ind"] else 1.0
-        if acc is None:
-            fn = lambda q: q.activation(out["ap"], i0["ap"], f, bias=ap(bias), scale=ap(scale))
-        else:
-            fn = lambda q: q.activation(out["ap"], i0["ap"], f, bias=ap(bias), scale=ap(scale), accum_out=acc["ap"])
-        add("s", fn, COST["fix"] + extra + max(64, i0["n"] * c) * cy, [i0, bias, scale], [out] + ([acc] if acc else []))
+        more = {"accum_out": acc["ap"]} if acc else {}
+        add("s", lambda q: q.activation(out["ap"], i0["ap"], f, bias=ap(bias), scale=ap(scale), **more),
+            COST["fix"] + extra + (20.0 if acc else 0.0) + max(64, i0["n"] * c) * cy, [i0, bias, scale], [out] + ([acc] if acc else []))
 
     def lin(how, out, i0, bias=0.0, scale=1.0):
         if how == "S":
@@ -143,48 +149,57 @@ def build(T, topo, core):
         else:
             ts(out, i0, scale, ALU.mult, bias, ALU.add)
 
-    def mm(out, pairs, start=True, stop=True):
+    def mms(items):
         def fn(q):
             last = None
-            for j, (l, r) in enumerate(pairs):
-                last = q.matmul(out["ap"], l["ap"], r["ap"], start and j == 0, stop and j == len(pairs) - 1)
+            for o, l, r, a, z in items:
+                last = q.matmul(o["ap"], l["ap"], r["ap"], a, z)
             return last
-        dur = 30.0 + sum(max(64, r["n"]) * (4 if r["d"] == F32 else 1) for l, r in pairs) * COST["pe"]
-        add("p", fn, dur, [x for pr in pairs for x in pr], [out])
+        dur = 30.0 + sum(COST["mm"] + max(64, r["n"]) * (4 if r["d"] == F32 else 1) * COST["pe"] for o, l, r, a, z in items)
+        add("p", fn, dur, [x for it in items for x in it[1:3]], [it[0] for it in items])
+
+    def mm(out, pairs, start=True, stop=True):
+        mms([(out, l, r, start and j == 0, stop and j == len(pairs) - 1) for j, (l, r) in enumerate(pairs)])
+
+    line = [None]
+
+    def gp(fn, dur, rd, out):
+        j = add("g", fn, dur, rd, [out])
+        if line[0] is not None:
+            ops[j]["follow"] = line[0]
+        line[0] = j
 
     def iota(out, pattern, base, cm):
         if out["d"] == I32:
             fn = lambda q: q.iota(out["ap"], pattern, base, cm)
         else:
             fn = lambda q: q.iota(out["ap"], pattern, base, cm, allow_small_or_imprecise_dtypes=True)
-        add("g", fn, 130.0 + 2 * out["n"] * cy, [], [out])
+        gp(fn, 130.0 + 2 * out["n"] * cy, [], out)
 
-    def zero(how, out):
-        if how == "g":
-            iota(out, [[0, out["n"]]], 0, 0)
-        else:
-            ms(out, 0.0)
+    def pick(out, i0, test, other, base, sign):
+        gp(lambda q: q.affine_select(out["ap"], i0["ap"], [[sign, out["n"]]], test, other, base, -sign), 170.0 + 2 * out["n"] * cy, [i0], out)
+
+    def diag(name, c):
+        pick(A(name, 0, 128), A("zz", 0, 128), ALU.not_equal, c, 0, 1)
 
     nd, nr, bus = [0], [0], [0.0, 0]
 
-    def load(dst, src, eng, nbytes):
-        s = "d%d" % nd[0]
+    def sem():
         nd[0] += 1
+        return "d%d" % (nd[0] - 1)
+
+    def load(dst, src, nbytes):
         bus[0] += nbytes * 0.22 - 60.0
-        j = add(eng, lambda q: q.dma_start(dst["ap"], src), 60.0, [], [dst], kind="dma", sem=s, cnt=16, lat=1900.0 + max(bus[0], 0.0))
-        if nd[0] > 1:
+        j = add("y", lambda q: q.dma_start(dst["ap"], src), 60.0, [], [dst], kind="dma", sem=sem(), cnt=16, lat=1900.0 + max(bus[0], 0.0))
+        if j > 0:
             ops[j]["follow"] = bus[1]
         bus[1] = j
 
-    def store(dst, src, eng, nbytes):
-        s = "d%d" % nd[0]
-        nd[0] += 1
-        add(eng, lambda q: q.dma_start(dst["ap"], src["ap"]), 60.0, [src], [dst], kind="dma", sem=s, cnt=16, lat=1900.0 + nbytes * 0.22)
+    def copy(dst, src, nbytes):
+        add("y", lambda q: q.dma_start(dst["ap"], src["ap"]), 60.0, [src], [dst], kind="dma", sem=sem(), cnt=16, lat=1900.0 + nbytes * 0.22)
 
     def dadd(dst, src):
-        s = "d%d" % nd[0]
-        nd[0] += 1
-        add("g", lambda q: q.dma_start(dst["ap"], src["ap"], accum_op=ALU.add), COST["gissue"], [src, dst], [dst], kind="dma", sem=s, cnt=16,
+        add("g", lambda q: q.dma_start(dst["ap"], src["ap"], accum_op=ALU.add), COST["gissue"], [src, dst], [dst], kind="dma", sem=sem(), cnt=16,
             lat=COST["glat"] + dst["n"] * 4 * 0.3)
 
     def engines(a, b, wide=False):
@@ -194,194 +209,172 @@ def build(T, topo, core):
                 far &= topo.mask(a, c)
         return topo.mask(a, b) if wide else (topo.mask(a, b) & ~far) or far
 
-    def send(src, dsts, froms, lands, nbytes, line, wide=False):
+    def send(src, dsts, froms, lands, nbytes, lane, twice=False):
         ls, rs = "l%d" % nr[0], "r%d" % nr[0]
         nr[0] += 1
-        masks = sorted({engines(core, c, wide) for c, _ in dsts})
+        masks = sorted({engines(core, c) for c, _ in dsts})
 
         def fn(q):
-            if len(dsts) == 1:
+            if len(dsts) == 1 and not twice:
                 rid, pid, _ = topo.addr(dsts[0][0])
                 return q.remote_dma(dsts[0][1]["ap"], src["ap"], T.sem[rs], T.sem[ls], pid, rid, masks[0])
             trs = []
             for m in masks:
-                to = [(c, d) for c, d in dsts if engines(core, c, wide) == m]
-                trs.append(RemoteDMATransfer(dst_ids=[DstId(rid=topo.addr(c)[0], pnc=topo.addr(c)[1]) for c, _ in to], dma_engine_mask=m,
-                                             remote_sem=T.sem[rs], srcs=[src["ap"]], dsts=[d["ap"] for _, d in to]))
+                to = [(c, d) for c, d in dsts if engines(core, c) == m]
+                trs.append(RemoteDMATransfer(dst_ids=[DstId(rid=topo.addr(c)[0], pnc=topo.addr(c)[1]) for c, _ in to], dma_engine_mask=m, remote_sem=T.sem[rs],
+                                             srcs=[src["ap"]] * (2 if twice else 1), dsts=[d["ap"] for _, d in to], alu_op=1 if twice else 0))
             return q.remote_dma_fused(trs, local_sem=T.sem[ls])
         rows = COST["rows"] * min(len(dsts), 2) + nbytes * COST["link"]
         left = sum(bin(m).count("1") for m in masks)
         j = add("g", fn, COST["rissue"], [src], [], kind="send", sem=ls, cnt=left, lat=COST["remote"] + rows, lead=COST["remote"])
-        add(line, None, rows, [], lands, kind="recv", sem=rs, cnt=sum(bin(engines(c, core, wide)).count("1") for c in froms), after=j, lat=0.0)
+        add(lane, None, rows, [], lands, kind="recv", sem=rs, cnt=sum(bin(engines(c, core)).count("1") for c in froms), after=j, lat=0.0)
 
     nxt, prv = T.cores[(rank + 1) % n], T.cores[(rank - 1) % n]
 
     def sh(name, i, base=0):
         return A(name, base + 15 - i, base + 143 - i)
 
-    def wrap(out, mat, src, lo, hi, more=()):
-        mm(out, [(sh(mat, i), A(src, lo + i, hi, 16)) for i in range(16)] + list(more))
+    def wrap(out, mat, src, lo, hi, start=True):
+        mm(out, [(sh(mat, i), A(src, lo + i, hi, 16)) for i in range(16)], start)
 
-    load(A("sdi", 0, 192), T.sd[:], "y", 768)
-    load(A("uv", 0, K), T.u0[:], "y", 2048)
-    load(A("a", 0, NV), T.ta[:], "y", 6144)
-    load(A("thi", 0, 3), T.th[:], "y", 200)
-    load(A("nab", 0, 192), T.na[:], "y", 768)
-    load(A("nab", 192, 384), T.nb[:], "y", 768)
-    load(A("pfi", 0, 64), T.pf[:], "y", 256)
+    load(A("sdi", 0, 192), T.sd[:], 768)
+    load(A("uv", 0, K), T.u0[:], 2048)
+    for c in range(2):
+        load(A("a", 1536 * c, 1536 * c + 1536), T.ta[:, 1536 * c:1536 * c + 1536], 3072)
+    load(A("thi", 0, 3), T.th[:], 200)
     zz = A("zz", 0, NZ // 4)
-
-    def blank(name):
-        if name in OPT["blank"]:
+    ms(zz, 0.0)
+    later = {"na": (A("nab", 0, 192), T.na, 768), "nb": (A("nab", 192, 384), T.nb, 768), "pf": (A("pfi", 0, 64), T.pf, 256),
+             "v": (A("uv", VO, VO + K), T.v0, 2048), "b": (A("b", 0, NV), T.tb, 6144)}
+    for name in OPT["loads"]:
+        if name in later:
+            load(later[name][0], later[name][1][:], later[name][2])
+        else:
             for c in range(4):
-                load(A(name, c * NZ // 4, (c + 1) * NZ // 4), zz["ap"], "y", NZ // 2)
+                load(A(name, c * NZ // 4, (c + 1) * NZ // 4), zz["ap"], NZ // 2)
                 ops[-1]["rd"] = zz["reg"]
-
-    ms(zz if OPT["blank"] else A("zz", 0, 384), 0.0)
-    blank("ah")
-    load(A("uv", VO, VO + K), T.v0[:], "y", 2048)
-    load(A("b", 0, NV), T.tb[:], "y", 6144)
-    blank("bh")
-    blank("nnd")
-    load(A("h", 0, NV), T.h0[:], "y", 6144)
+    landed = [("landed", 0, 1, 1)]
+    ops[-1]["wr"] = ops[-1]["wr"] + landed
 
     iota(A("ci", 0, 1), [[0, 1]], 0, 1)
     iota(A("kr", 0, 272), [[1, 272]], 0, 0)
     iota(A("r16", 0, 128), [[16, 8], [0, 16]], 0, 0)
-    iota(A("sf0", 0, 48), [[0, 4], [64, 12]], 0, 0)
-    rows = len(ops) - 1
-    for j in range(rows - 2, rows + 1):
-        ops[j]["follow"] = j - 1
     ts(A("ci", 1, 2), A("ci", 0, 1), 15, ALU.bitwise_and)
     ts(A("ci", 2, 3), A("ci", 0, 1), 112, ALU.bitwise_and)
     cp(A("cf", 0, 3), A("ci", 0, 3))
-    pc, lane, g16 = A("cf", 0, 1), A("cf", 1, 2), A("cf", 2, 3)
-    ts(A("q1", 0, 144), A("kr", 0, 144), -15.0, ALU.add, g16, ALU.is_equal)
+    col = lambda i: A("cf", i, i + 1)
+    pc, lane, g16 = col(0), col(1), col(2)
+    q1 = A("q1", 0, 144)
+    ts(q1, A("kr", 0, 144), -15.0, ALU.add, g16, ALU.is_equal)
     ts(A("i16", 0, 16), A("kr", 0, 16), lane, ALU.is_equal, 0.5, ALU.mult)
-    for t in range(4):
-        fill[0] = t > 0
-        for q in range(4):
-            i = 4 * q + t
-            if t == 0 and q % 2 == 0:
-                ts(A("bm", 144 * i, 144 * i + 144), A("q1", 0, 144), A("i16", i, i + 1), ALU.mult)
-            else:
-                act(A("bm", 144 * i, 144 * i + 144), A("q1", 0, 144), scale=A("i16", i, i + 1))
-    fill[0] = False
-    ts(A("blk", 0, 128), A("r16", 0, 128), g16, ALU.is_equal)
-    ts(A("idb", 0, 128), A("kr", 0, 128), pc, ALU.is_equal)
-    idb, idf, idn, idh, blk = (A(x, 0, 128) for x in ("idb", "idf", "idn", "idh", "blk"))
-    id256, id512, hc = A("id256", 0, 128), A("id512", 0, 128), A("hc", 0, 512)
-    act(idf, idb)
+    for q in range(4):
+        if OPT["bm0"][q] == "V":
+            ts(A("bm", 576 * q, 576 * q + 144), q1, A("i16", 4 * q, 4 * q + 1), ALU.mult)
+        else:
+            act(A("bm", 576 * q, 576 * q + 144), q1, scale=A("i16", 4 * q, 4 * q + 1))
+    idb, idf, idn, idh, idk, id256, blk = (A(x, 0, 128) for x in ("idb", "idf", "idn", "idh", "idk", "id256", "blk"))
+    ts(blk, A("r16", 0, 128), g16, ALU.is_equal)
+    ts(idb, A("kr", 0, 128), pc, ALU.is_equal)
     act(id256, idb, scale=1.0 / 256)
-    act(id512, idb, scale=1.0 / 512)
-    ts(A("un0", 0, 128), A("kr", 0, 128), pc, ALU.is_lt, -1.0, ALU.mult)
-    mm(P(5, 256, 384), [(idb, blk)])
-    tt(A("un", 0, 128), P(5, 256, 384), A("un0", 0, 128), ALU.mult)
+    for name in ("ah", "bh", "nnd"):
+        if name not in OPT["loads"]:
+            for c in range(1, 4):
+                iota(A(name, c, NV, 4), [[0, BL]], 0, 0)
+            ms(A(name, NV, NZ), 0.0)
+    diag("idk", 4096.0)
+    diag("idn", -1.0)
+    act(idf, idb)
     low = A("cb", 0, 1)
     act(low, lane, ACT.Sigmoid, bias=7.5 * 512, scale=-512.0, extra=1300.0)
     table = len(ops) - 1
-    act(A("cf", 3, 4), low, scale=2.0)
-    act(A("cf", 4, 5), low, bias=2.0, scale=-2.0)
-    half = 1.0 if OPT["sg"] == "V" else 0.5
-    act(A("cf", 5, 6), low, bias=-2.0 * half, scale=4.0 * half)
-    act(A("cf", 6, 7), lane, scale=4.0)
-    act(idn, idb, scale=-1.0)
-    act(idh, idb, scale=127.5)
-    act(A("wd", 0, 144), A("q1", 0, 144), scale=A("cf", 5, 6))
-    act(A("w0", 0, 144), A("q1", 0, 144), scale=A("cf", 3, 4))
-    act(A("w1", 0, 144), A("q1", 0, 144), scale=A("cf", 4, 5))
-    act(A("sf", 0, 48), A("sf0", 0, 48), bias=A("cf", 6, 7))
-    act(A("fw", 0, 16), A("kr", 0, 16), bias=lane, scale=16.0)
-    act(A("kw", 0, 16), A("fw", 0, 16), bias=0.5)
-    act(A("kw", 16, 32), A("fw", 0, 16), bias=1.0)
-    act(A("kw", 32, 48), A("fw", 0, 16), bias=1024.0)
-    for name, how in (("nnd", "ggg"), ("ah", OPT["zero"][1] * 3), ("bh", OPT["zero"][2] + OPT["zero"][3] * 2)):
-        if name in OPT["blank"]:
-            continue
-        for c in range(1, 4):
-            zero(how[c - 1], A(name, c, NV, 4))
-            if how[c - 1] == "g":
-                ops[-1]["follow"] = rows
-                rows = len(ops) - 1
-        ms(A(name, NV, NZ), 0.0)
-    ms(hc, 127.5)
+    act(col(5), low, bias=-1.0, scale=2.0)
+    act(A("wd", 0, 144), q1, scale=col(5))
     ms(A("ff", 0, 32), 0.0)
     ms(A("ff", 96, 128), 0.0)
-    fill[0] = True
-    ms(A("one", 0, 256), 1.0)
-    ts(A("un4", 0, 128), idb, -4096.0, ALU.mult)
-    tt(A("un4", 0, 128), A("un4", 0, 128), A("un", 0, 128), ALU.add)
-    act(A("lz", 0, 128), idb, scale=A("i16", 0, 1))
-    act(A("lz", 0, 128), A("lz", 0, 128), scale=2.0)
-    ts(A("st", 0, 128), A("kr", 0, 128), -1.0, ALU.add, pc, ALU.is_equal)
-    tt(A("st", 0, 128), A("st", 0, 128), blk, ALU.mult)
-    tt(A("st", 0, 128), A("st", 0, 128), idb, ALU.subtract)
-    ms(A("hh", 0, 512), -0.5)
-    for name in ("uv0", "uv"):
-        ms(A(name, ZC, VO), 0.5)
-    for out in (A("uv0", K, ZC), A("uv0", VO + K, 2 * VO), A("gf", 0, VO), A("uv", K, ZC), A("uv", VO + K, 2 * VO), A("us", K, VO), A("sig", K, VO)):
-        zero("g", out)
-        ops[-1]["follow"] = rows
-        rows = len(ops) - 1
-    fill[0] = False
-    ms(A("cc", 128, 136), 4096.0)
-    ms(A("fc", 64, 72), 0.0)
     if "V" in OPT["cmp"]:
         cp(A("thf", 0, 3), A("thi", 0, 3))
     if "S" in OPT["cmp"]:
         ts(A("thf", 4, 7), A("thi", 0, 3), 0.5, ALU.add)
 
     cp(A("shl", 0, 192), A("sdi", 0, 192))
-    tt(A("shl", 192, 384), A("sdi", 0, 192), A("shl", 0, 192), ALU.subtract)
-    if OPT["nn"] == "V":
-        act(P(5, 0, 192), A("kr", 0, 192), bias=lane, scale=16.0)
-    else:
-        act(A("cf", 7, 8), lane, bias=-4112.5)
-        act(P(5, 0, 192), A("kr", 0, 192), bias=A("cf", 7, 8), scale=16.0)
-        act(A("idk", 0, 128), idb, scale=4096.0)
-        tt(A("cf", 9, 11), A("i16", 0, 2), A("i16", 8, 10), ALU.add)
-        act(A("cf", 9, 10), A("cf", 9, 10), bias=-4096.0, scale=-4128.0)
-        act(A("cf", 8, 9), A("cf", 10, 11), bias=A("cf", 9, 10), scale=15.5)
+    act(col(7), lane, bias=-4112.5)
+    act(P(5, 0, 192), A("kr", 0, 192), bias=col(7), scale=16.0)
+    tt(A("cf", 9, 11), A("i16", 0, 2), A("i16", 8, 10), ALU.add)
+    act(col(9), col(9), bias=-4096.0, scale=-4128.0)
+    act(col(8), col(10), bias=col(9), scale=15.5)
     for j in range(2):
         tt(P(6, 192 * j, 192 * j + 192), A("nab", 192 * j, 192 * j + 192), P(5, 0, 192), ALU.subtract)
     act(A("dhl", 0, 384), P(6, 0, 384))
     tt(A("dhl", 384, 768), P(6, 0, 384), A("dhl", 0, 384), ALU.subtract)
-    cp(A("ff", 32, 96), A("pfi", 0, 64))
+    ts(A("ff", 32, 96), A("pfi", 0, 64), -EDGE, ALU.add)
     ts(A("fu", 0, 64), A("pfi", 0, 64), float(NV), ALU.min)
 
-    for t in range(4):
-        fill[0] = t > 0
+    fill[0] = True
+    iota(A("kt", 0, K), [[2048, 16], [0, 64]], 0, 0)
+    iota(A("jt", 0, 512), [[0, 8], [1, 64]], 0, 0)
+    pick(A("tri", 0, 128), blk, ALU.is_ge, 0.0, 0, 1)
+    pick(A("tr4", 0, 128), A("tri", 0, 128), ALU.not_equal, -4096.0, 0, 1)
+    pick(A("w0", 0, 144), q1, ALU.is_ge, 0.0, -8, 1)
+    pick(A("w1", 0, 144), q1, ALU.is_ge, 0.0, 7, -1)
+    iota(A("sf0", 0, 48), [[0, 4], [32, 12]], 0, 0)
+    iota(A("one", 0, 512), [[0, 512]], 1, 0)
+    pick(A("su", 128, 256), sh("q1", 0), ALU.is_equal, 0.0, 0, 1)
+    pick(A("su", 0, 128), blk, ALU.is_equal, 0.0, -1, 1)
+    pick(A("su", 0, 128), A("su", 0, 128), ALU.not_equal, -1.0, 0, 1)
+    for name, c in (("id512", -512.0), ("id64", -64.0), ("id32", -32.0), ("idh", -0.5)):
+        diag(name, c)
+    add("g", lambda q: q.dma_start(T.w[:, 0:NV], T.h0[:]), COST["gissue"], [{"reg": landed}], [A("w", 0, NV)], kind="dma", sem=sem(), cnt=16,
+        lat=COST["glat"] + NV * 4 * 0.22, follow=line[0])
+    for i in range(16):
+        if i % 4:
+            act(A("bm", 144 * i, 144 * i + 144), q1, scale=A("i16", i, i + 1))
+    act(A("st", 0, 256), A("su", 0, 256), scale=BIG)
+    act(A("blm", 0, 128), blk, scale=-128.0)
+    act(col(6), lane, scale=2.0)
+    act(A("sf", 0, 48), A("sf0", 0, 48), bias=col(6))
+    act(A("fw", 0, 16), A("kr", 0, 16), bias=lane, scale=16.0)
+    act(A("kw", 0, 16), A("fw", 0, 16), bias=0.5)
+    act(A("kw", 16, 32), A("fw", 0, 16), bias=SPARE - 1008.0)
+    act(col(11), lane, bias=128.0, scale=128.0)
+    act(A("kt", 0, K), A("kt", 0, K), bias=col(11))
+    act(col(12), A("i16", 0, 1), bias=BIG - 256.0 + EDGE, scale=-2.0 * BIG)
+    ms(A("sc", 15, 16), 0.0)
+    for name in ("uv0", "uv"):
+        ms(A(name, ZC, SPARE), 0.5)
+    ms(A("us", ZC, SPARE), 0.0)
+    ms(A("cin", 16, 60, 20), 256.0)
+    ms(A("hs", 0, 1), 0.0)
+    fill[0] = False
+
+    def lists(t):
         o = P(4, 0, 48) if t == 0 else P(7, 0, 48)
-        prs = []
-        for i in range(16):
-            src = 4 * (i % 4) + t
-            for part in (0, 192):
-                prs.append((sh("bm", i, 144 * src), A("shl", part + i // 4, part + 192, 4)))
-        mm(o, prs)
+        mm(o, [(sh("bm", i, 144 * (4 * (i % 4) + t)), A("shl", i // 4, 192, 4)) for i in range(16)])
         if t == 0:
             ts(A("sl", 576, 624), o, 2.0, ALU.mult)
         act(A("sdf", 48 * t, 48 * t + 48), o, scale=2.0)
+
+    fill[0] = True
     cp(A("sdf", 192, 384), A("sdi", 0, 192))
-    for b in range(4):
-        act(A("w", BL * b, BL * b + BL), A("h", BL * b, BL * b + BL), scale=0.125)
+    send(A("w", 0, 512), [(prv, A("w", NV, NW))], [nxt], [A("w", NV, NW)], 2048, "k", True)
     fill[0] = False
 
-    send(A("h", 0, 512), [(prv, A("gl0", 0, 512))], [nxt], [A("gl0", 0, 512)], 1024, "k", True)
-
     def prefill(t):
-        for name, mat, c0 in (("a", idb, 0), ("b", id256, BL)):
-            cut = 512 - c0 % 512
-            for lo, hi in ((0, cut), (cut, BL)):
-                mm(A("ps", c0 + lo, c0 + hi), [(mat, A(name, 4 * lo + t, 4 * hi, 4))])
+        for name, mat, bank in (("a", idb, 0), ("b", id256, 2)):
+            for c in range(2):
+                mm(P(bank + c, 0, 384), [(mat, A(name, 1536 * c + t, 1536 * c + 1536, 4))])
+        for c in range(2):
+            if t > 0 and c in OPT["direct"][t]:
+                act(A("xs", 384 * c, 384 * c + 384), A("a", 1536 * c + t, 1536 * c + 1536, 4), bias=0.5, scale=1.0 / 256)
+
+    def rows(t):
         for q in range(4):
             i = 4 * q + t
-            own = OPT["nn"] == "V"
-            if not own and q % 2 == 0:
-                mm(P(3 if q < 2 else 6, 0, 384), [(idb, A("zz", 0, 384))], True, False)
-            mm(rowsof(q), [(sh("bm", l, 144 * i), A("dhl", c0, c0 + 192)) for l, c0 in ((0, 0), (1, 384), (8, 192), (9, 576))], own, own)
+            if q % 2 == 0:
+                mm(P(6 + q // 2, 0, 384), [(idb, A("zz", 0, 384))], True, False)
+            mm(rowsof(q), [(sh("bm", l, 144 * i), A("dhl", c0, c0 + 192)) for l, c0 in ((0, 0), (1, 384), (8, 192), (9, 576))], False, False)
 
     def rowsof(q):
-        return P(3 if q < 2 else 6, 192 * (q % 2), 192 * (q % 2) + 192)
+        return P(6 + q // 2, 192 * (q % 2), 192 * (q % 2) + 192)
 
     def collapse(t):
         for c in range(2):
@@ -390,25 +383,25 @@ def build(T, topo, core):
             c1, c2, d, dm = A("c1", lo, hi), A("c2", lo, hi), P(4 + c, 128, 512), A("dm", BL * t + lo, BL * t + hi)
             if t == 0:
                 off = A("sl", 576 + 24 * c, 600 + 24 * c)
-                if OPT["x0"] == "V":
+                if OPT["x0"][c] == "V":
                     tt(A("dd", lo, hi), G(A(UV[0], 0, K), off), cls("a"), ALU.subtract)
                     act(c2, A("dd", lo, hi), ACT.Abs, bias=-128.0)
                 else:
                     act(A("xs", lo, hi), G(A(UV[0], 0, K), off), bias=-128.0)
-                    mm(d, [(idb, cls("a")), (idn, A("xs", lo, hi))])
+                    mm(d, [(idb, cls("a"))], True, False)
+                    mm(d, [(idn, A("xs", lo, hi))], False)
                     act(c2, d, ACT.Abs)
             else:
-                s = 2.0 ** (t - 10)
                 o = 192 * (t - 1) + 48 * t + 24 * c
-                lin(OPT["xs"][c], cls("x"), G(A(UV[t], 0, K), A("sl", o, o + 24)), bias=-0.5 * s, scale=s)
-                if (t, c) in OPT["direct"]:
+                lin(OPT["xs"][t - 1][c], cls("x"), G(A(UV[t], 0, K), A("sl", o, o + 24)), bias=-2.0 ** t, scale=2.0 ** (t + 1))
+                if c in OPT["direct"][t]:
                     ops[-1]["fill"] = True
-                    tt(A("dd", lo, hi), G(A(UV[t], 0, K), A("sl", o, o + 24)), cls("a"), ALU.subtract)
-                    act(c2, A("dd", lo, hi), ACT.Abs, bias=-0.5)
+                    tt(A("dd", lo, hi), G(A(UV[t], 0, K), A("sl", o, o + 24)), A("xs", lo, hi), ALU.subtract)
+                    act(c2, A("dd", lo, hi), ACT.Abs, scale=256.0)
                 else:
-                    mm(d, [(id512 if t == 1 else id256, cls("a"))], True, False)
-                    mm(d, [(idn, cls("x"))], False)
-                    act(c2, d, ACT.Abs, scale=1.0 / s)
+                    mm(d, [(idb, cls("a"))], True, False)
+                    mm(d, [(A("id64" if t == 1 else "id32", 0, 128), cls("x"))], False)
+                    act(c2, d, ACT.Abs)
             if OPT["cmp"][t] == "V":
                 ts(c1, c2, A("thf", t, t + 1), ALU.is_le)
             else:
@@ -420,17 +413,12 @@ def build(T, topo, core):
                 ops[-1]["follow"] = table
             else:
                 ts(dm, d, thr, ALU.is_ge)
-            tt(cls("ah"), A("ps", lo, hi), dm, ALU.mult)
-            tt(cls("bh"), A("ps", BL + lo, BL + hi), dm, ALU.mult)
+            tt(cls("ah"), P(c, 0, 384), dm, ALU.mult)
+            tt(cls("bh"), P(2 + c, 0, 384), dm, ALU.mult)
         for q in range(4):
-            dq = A("dm", BL * t + q, BL * t + BL, 4)
-            if OPT["nn"] == "V":
-                tt(A("nnd", 4 * q + t, NV, 16), rowsof(q), dq, ALU.mult)
-            else:
-                mm(rowsof(q), [(A("idk", 0, 128), dq)], False, q % 2 == 1)
-        if OPT["nn"] == "S":
-            for q in range(4):
-                act(A("nnd", 4 * q + t, NV, 16), rowsof(q), ACT.Relu, bias=A("cf", 8, 9))
+            mm(rowsof(q), [(idk, A("dm", BL * t + q, BL * t + BL, 4))], False, q % 2 == 1)
+        for q in range(4):
+            act(A("nnd", 4 * q + t, NV, 16), rowsof(q), ACT.Relu, bias=col(8))
 
     marks = {}
 
@@ -443,8 +431,9 @@ def build(T, topo, core):
         src, dst = (UV[t], "uw") if k == 0 else ("uw", UV[t + 1])
         ub, vb = A(src, lo, hi), A(src, VO + lo, VO + hi)
         un, vn = A(dst, lo, hi), A(dst, VO + lo, VO + hi)
-        raw, last, end = t == 0 and k == 0, k == 1, t == 2 and k == 1
+        end = t == 2 and k == 1
         how = OPT["hop"][t][2 * k + c]
+        unit = id256 if t == 0 and k == 0 else idb
 
         def mark(name):
             marks[name, k, c] = len(ops) - 1
@@ -456,239 +445,219 @@ def build(T, topo, core):
         lin(OPT["gn"][2 * k + c], gn, G(A("nnd", 0, NZ), off))
         f = A("ff", 32 * c + 32, 32 * c + 64)
         wb = 4 + c
-        pm, pd, pn = P(wb, 32 - 32 * c, 64 - 32 * c), P(wb, 64, 96), P(wb, 32 * c, 32 * c + 32)
-        less = []
-        if raw:
-            mm(pv, [(idb, vb)])
-            ub, vb = A("uv0", lo, hi), A("uv0", VO + lo, VO + hi)
-            lin(OPT["raw"][c], ub, A(src, lo, hi), bias=-127.5)
-            lin(OPT["raw"][2 + c], vb, A(src, VO + lo, VO + hi), bias=-127.5)
-        else:
-            mm(pv, [(idb, vb), (idb, hc)])
-        mm(pa, [(idb, hc)], True, False)
-        mm(pb, [(idb, hc)], True, False)
+        pm, pn = P(wb, 32 - 32 * c, 64 - 32 * c), P(wb, 32 * c, 32 * c + 32)
+        mm(pv, [(unit, vb)])
+        mm(pa, [(idb, A("zz", 0, 512))], True, False)
+        mm(pb, [(idb, A("zz", 0, 512))], True, False)
         tt(pa, pv, ga, ALU.mult)
         mark("m1")
-        if not OPT["pd"]:
-            wrap(pd, "wd", "gg", 512 + lo, 512 + hi)
-        elif c == 1:
+        if c == 1:
             wrap(P(5, 64, 128), "wd", "gg", 512, 1536)
-        mm(pa, [(idb, ub)] + less, False)
+        mm(pa, [(unit, ub)], False)
         tt(pb, pa, gb, ALU.mult)
         mark("m2")
-        mm(pb, [(idb, vb), (idh, gb)] + less, False)
-        if OPT["qu"][t][2 * k + c] == "V":
-            ts(mqu, pa, MAGIC, ALU.add, -MAGIC, ALU.add)
-        else:
-            act(A("mqt", lo, hi), pa, bias=MAGIC)
-            act(mqu, A("mqt", lo, hi), bias=-MAGIC)
+        mm(pb, [(unit, vb)], False)
+        ts(mqu, pa, -HALF, ALU.add)
         mark("qu")
         if how == "V":
             tt(pa, pa, mqu, ALU.subtract)
-            if end:
-                act(A("us", lo, hi), pa, bias=-0.5 * 2.0 ** -7, scale=2.0 ** -7)
-            else:
-                act(un, pa)
+            act(un, pa)
         else:
             tt(un, pa, mqu, ALU.subtract)
-            if end:
-                ts(A("us", lo, hi), un, -0.5, ALU.add, 2.0 ** -7, ALU.mult)
-        ts(mqv, pb, MAGIC, ALU.add, -MAGIC, ALU.add)
+        if end:
+            lin(OPT["us"][c], A("us", lo, hi), un, bias=-8.0, scale=16.0)
+        if k == 1 and "u" in OPT["early"][t]:
+            ru = A("ru", 2 * K * t + lo, 2 * K * t + hi)
+            send(A("us", lo, hi) if end else un, [(nxt, ru)], [prv], [ru], 1024, "l")
+        ts(mqv, pb, -HALF, ALU.add)
         mark("qv")
         tt(vn, pb, mqv, ALU.subtract)
         mark("vn")
+        if k == 1 and "v" in OPT["early"][t]:
+            ru = A("ru", 2 * K * t + K + lo, 2 * K * t + K + hi)
+            send(vn, [(nxt, ru)], [prv], [ru], 1024, "l")
         if how == "V":
             tt(ge, pa, vn, ALU.is_ge)
         else:
             mm(pa, [(idb, un)], True, False)
             mm(pa, [(idn, vn)], False)
-            act(ge, pa, ACT.Sign, bias=0.5)
-        if end:
-            mm(pb, [(idb, vn), (idb, A("hh", 0, 512))])
-            tt(A("zt", lo, hi), pb, A("us", lo, hi), ALU.mult)
-            act(A("sig", lo, hi), A("zt", lo, hi), ACT.Sigmoid, scale=2.0 ** -6)
+            act(ge, pa, ACT.Sign, bias=1.0 / 512)
         yield
-        if OPT["pd"]:
-            pd = P(5, 64 + 32 * c, 96 + 32 * c)
+        pd = P(5, 64 + 32 * c, 96 + 32 * c)
         mm(P(wb, 0, 64), [(idf, A("ff", 64 * c, 64 * c + 64))], True, False)
-        mm(P(wb, 0, 64), [(sh("q1", i), A("gg", 2 * lo + i, 2 * lo + K, 16)) for i in range(16)], False, True)
+        wrap(P(wb, 0, 64), "q1", "gg", 2 * lo, 2 * lo + K, False)
         sg, t2 = A("sg", 32 * c, 32 * c + 32), A("t2", 32 * c, 32 * c + 32)
-        thr = 8.5 if how == "V" else 1.0
-        if OPT["sg"] == "V":
-            ts(sg, pn, thr, ALU.is_ge, -0.5, ALU.add)
-        else:
-            act(sg, pn, ACT.Sign, bias=-thr)
+        act(sg, pn, ACT.Sign, bias=8.5 if how == "V" else 1.0, scale=-1.0)
         tt(t2, pd, sg, ALU.mult)
-        tt(f, pm, t2, ALU.add)
+        if k == 1:
+            tt(A("on", 32 * c, 32 * c + 32), pm, t2, ALU.is_ge)
+        tt(f, pm, t2, ALU.subtract)
         if k == 0:
-            ts(off, f, float(NV), ALU.min)
+            ts(off, f, EDGE, ALU.add, float(NV), ALU.min)
 
     def moves(t):
-        f, on, sc = A("ff", 32, 96), A("on", 0, 64), A("sc", 0, 64)
-        if OPT["on"] == "V":
-            ts(on, f, 3071.5, ALU.is_ge)
-        else:
-            act(on, f, ACT.Sigmoid, bias=-3071.5 * 512, scale=512.0)
-        add("v", lambda q: q.tensor_tensor_scan(sc["ap"], on["ap"], on["ap"], 0.0, ALU.add, ALU.max), COST["fix"] + 64 * cy, [on], [sc])
-        nv = OPT["accv"][t]
-        mm(P(4, 0, 64), [(blk, sc)])
-        mm(P(0, 0, 64), [(blk, sc)])
-        rk = P(2, 0, 64)
-        mm(P(5, 64, 128), [(blk, sc), (A("un", 0, 128), on)])
-        mm(rk, [(blk, sc), (A("un4", 0, 128), on)])
-        slot = lambda r: A("cin", 16 * t + 4 * r, 16 * t + 4 * r + 1)
-        ts(slot(rank), P(0, 63, 64), 256.0, ALU.min)
-        incl = A("cc", 64, 128)
-        lin(OPT["incl"], incl, P(5, 64, 128))
+        f, on, sc, sx = A("ff", 32, 96), A("on", 0, 64), A("sc", 16, 80), A("sc", 15, 79)
+        scan(sc, on, on, 0.0, ALU.add, ALU.max)
+        slot = lambda r: A("cin", 20 * t + 4 * r, 20 * t + 4 * r + 1)
+        mm(P(4, 0, 1), [(blk, A("sc", 79, 80))])
+        act(slot(rank), P(4, 0, 1))
+        nv = 16 - OPT["accs"][t]
+        shares = [(b, lo, hi) for b, lo, hi in ((0, 0, 8), (3, nv, 16), (2, 8, nv)) if lo < hi]
+        for b, lo, hi in shares:
+            mm(P(b, 0, 64 * (hi - lo)), [(idb, A("kt", 64 * lo, 64 * hi))], True, False)
+            mms([(P(b, 64 * j, 64 * j + 64), A("blm", 0, 128), sc, False, j == hi - lo - 1) for j in range(hi - lo)])
         others = [r for r in range(n) if r != rank]
         send(slot(rank), [(T.cores[r], slot(rank)) for r in others], [T.cores[r] for r in others], [slot(r) for r in others], 4, "l")
-        for c in range(16):
-            jk, acc = A("junk", 64 * c, 64 * c + 64), A("acc", c, c + 1)
-            if c < nv:
-                ts(jk, P(0, 0, 64), A("kw", c, c + 1), ALU.is_le)
-                add("v", lambda q, jk=jk, acc=acc: q.tensor_reduce(acc["ap"], jk["ap"], AxisListType.X, ALU.add), COST["fix"] + 64 * cy, [jk], [acc])
+        mm(P(5, 64, 128), [(blk, sx), (A("tri", 0, 128), on)])
+        incl = A("cc", 0, 64)
+        act(incl, P(5, 64, 128))
+        for b, lo, hi in shares:
+            if b == 3:
+                for j in range(lo, hi):
+                    act(A("sk", 64 * j, 64 * j + 63), P(b, 64 * (j - lo), 64 * (j - lo) + 63), ACT.Sigmoid, bias=-64.0, acc=A("sk", 64 * j + 63, 64 * j + 64))
             else:
-                act(jk, P(4, 0, 64), ACT.Sign, bias=A("kw", c, c + 1), scale=-1.0, acc=acc, extra=20.0)
-        cu = A("cu", 0, 16)
-        if nv:
-            cp(A("cu", 0, nv), A("acc", 0, nv))
-            act(A("cx", 0, nv), A("acc", 0, nv), scale=16.0)
-        ts(A("cu", nv, 16), A("acc", nv, 16), 0.5, ALU.mult, 32.0, ALU.add)
-        act(A("cx", nv, 16), A("acc", nv, 16), bias=512.0, scale=8.0)
-        tt(A("le", 0, 256), G(A("cc", 64, 136), cu), A("kr", 0, 256), ALU.is_le)
-        mm(P(5, 0, 16), [(idf, A("cx", 0, 16))], True, False)
-        mm(P(5, 0, 16), [(sh("q1", i), A("le", i, 256, 16)) for i in range(16)], False, True)
+                scan(A("sk", 64 * lo, 64 * hi), A("jt", 0, 64 * (hi - lo)), P(b, 0, 64 * (hi - lo)), 0.0, ALU.min, ALU.max)
+        ek, cu = A("sk", 63, K, 64), A("cu", 0, 16)
+        ts(cu, ek, 63.0, ALU.min)
+        act(A("rr", 0, 16), ek, ACT.Relu, bias=1008.0, scale=-16.0)
+        le = A("le", 0, 256)
+        tt(le, G(incl, cu), A("kr", 0, 256), ALU.is_le)
+        at = P(5, 0, 16)
+        mm(at, [(idn, A("rr", 0, 16))], True, False)
+        wrap(at, "q1", "le", 0, 256, False)
         atu = A("atu", 0, 16)
-        cp(atu, P(5, 0, 16))
+        ts(atu, at, 1008.0, ALU.add, K - 1.0, ALU.min)
         uv = UV[t + 1]
         utab = A(uv if t < 2 else "us", 0, VO)
-        act(A("snd", 0, 256), G(utab, atu))
-        if t < 2:
-            lin(OPT["sv"], A("snd", 512, 768), G(A(uv, VO, 2 * VO), atu))
-        else:
-            lin(OPT["sv"], A("snd", 512, 768), G(A(uv, VO, 2 * VO), atu), bias=-0.5 * 2.0 ** -6, scale=2.0 ** -6)
-        act(A("fc", 0, 64), f, bias=-3328.0)
-        act(A("fk", 0, 64), f, bias=256.0, scale=-1.0)
+        early, r0 = OPT["early"][t], 768 * t
+        out = {x: A("snd", 256 * i, 256 * i + 256) for i, x in enumerate(OPT["parts"][t])}
+        got = {x: A("rcv", r0 + 256 * i, r0 + 256 * i + 256) for i, x in enumerate(OPT["parts"][t])}
+        ra = A("ra", 16 * t, 16 * t + 16)
+        if early:
+            send(atu, [(nxt, ra)], [prv], [ra], 32, "l")
+        vs = {} if t < 2 else {"bias": -0.25, "scale": 0.5}
+        if "u" not in early:
+            lin(OPT["su"], out["u"], G(A(uv if t < 2 else "us", 0, K), atu))
+        if "v" not in early:
+            lin(OPT["sv"], out["v"], G(A(uv, VO, VO + K), atu), **vs)
+        act(A("fc", 0, 64), f, bias=(EDGE - 3328.0) / BIG, scale=1.0 / BIG)
         eq = P(4, 256, 512)
-        mm(eq, [(A("lz", 0, 128), A("one", 0, 256))], True, False)
-        mm(eq, [(A("st", 0, 128), A("le", 0, 256))], False)
-        act(A("eq", 0, 256), G(A("fc", 0, 72), cu))
-        tt(A("snd", 256, 512), eq, A("eq", 0, 256), ALU.mult)
-        r0 = 768 * t
+        mm(eq, [(A("st", 128, 256), A("one", 0, 256))], True, False)
+        mm(eq, [(A("st", 0, 128), le)], False)
+        act(A("eq", 0, 256), G(A("fc", 0, 64), cu))
+        tt(out["f"], eq, A("eq", 0, 256), ALU.mult)
         cuts = OPT["cuts"][t]
         for lo, hi in zip(cuts, cuts[1:]):
             send(A("snd", lo, hi), [(nxt, A("rcv", r0 + lo, r0 + hi))], [prv], [A("rcv", r0 + lo, r0 + hi)], 2 * (hi - lo), "l")
+        if "u" in early:
+            lin(OPT["su"], got["u"], G(A("ru", 2 * K * t, 2 * K * t + K), ra))
+        if "v" in early:
+            lin(OPT["sv"], got["v"], G(A("ru", 2 * K * t + K, 2 * K * t + 2 * K), ra), **vs)
+        rk = P(4, 64, 128)
+        mm(rk, [(blk, sx), (A("tr4", 0, 128), on), (idk, A("one", 0, 64))])
+        wrap(P(4, 128, 132), "q1", "sc", 16, 80)
+        ts(A("ro", 0, 4), P(4, 128, 132), 256.0, ALU.min)
+        act(A("fk", 0, 64), incl, bias=col(12), scale=4096.0)
         m = A("mm", 4 * t, 4 * t + 1)
-        cin = A("cin", 16 * t, 16 * t + 13, 4)
+        cin = A("cin", 20 * t, 20 * t + 17, 4)
         add("v", lambda q: q.tensor_reduce(m["ap"], cin["ap"], AxisListType.X, ALU.min), COST["fix"] + 64 * cy, [cin], [m])
-        shift = A("mm", 4 * t + 1, 4 * t + 2)
-        if t == 0:
-            shift = m
-        else:
-            act(shift, m, bias=A("mm", 4 * t - 4 + min(t - 1, 1), 4 * t - 3 + min(t - 1, 1)))
-        ts(A("e1", 0, 16), A("kw", 16, 32), m, ALU.subtract, 2048.0, ALU.mult)
-        tt(A("e2", 0, 16), A("e1", 0, 16), A("kw", 32, 48), ALU.min)
-        tt(A("e3", 0, 16), P(5, 0, 16), A("e2", 0, 16), ALU.max)
+        shift, back = A("mm", 4 * t + 1, 4 * t + 2), A("mm", 4 * t + 2, 4 * t + 3)
+        act(shift, m, bias=A("mm", 4 * t - 3, 4 * t - 2) if t else 0.25 - K)
+        ts(A("e1", 0, 16), A("kw", 0, 16), m, ALU.subtract, 2048.0, ALU.mult)
+        tt(A("e2", 0, 16), A("e1", 0, 16), A("kw", 16, 32), ALU.min)
+        tt(A("e3", 0, 16), at, A("e2", 0, 16), ALU.max)
         asu = A("asu", 0, 16)
-        cp(asu, A("e3", 0, 16))
+        ts(asu, A("e3", 0, 16), 1008.0, ALU.add)
         lo = 0 if t < 2 else 192
-        si = A("si", 0, 192)
-        ts(si, A("sdf", lo, lo + 192), shift, ALU.add)
-        ts(si, si, 1023, ALU.bitwise_and)
+        si, sdf = P(1, 0, 192), A("sdf", lo, lo + 192)
+        act(A("si", 0, 192), sdf, ACT.Sign, bias=shift)
+        act(back, shift, bias=512.0)
+        mm(si, [(idf, sdf)], True, False)
         if OPT["pre3"][t]:
-            for lo, hi, o in [(144, 192, 24)] if t == 2 else [(48 * c + 36, 48 * c + 48, 12 * c) for c in range(t + 1)]:
-                tt(A("si", lo, hi), A("si", lo, hi), A("md", o, o + hi - lo), ALU.max)
-        cp(A("sl", 192 * t, 192 * t + 192), si)
-        lv = A("lv", 0, 64)
-        ts(lv, rk, 4096.0, ALU.add, m, ALU.is_le)
+            parts = [(144, 192, 24)] if t == 2 else [(48 * c + 36, 48 * c + 48, 12 * c) for c in range(t + 1)]
+            mms([(P(1, lo, hi), idb, A("md", o, o + hi - lo), False, False) for lo, hi, o in parts])
+        mm(si, [(A("id512", 0, 128), A("si", 0, 192))], False)
+        ts(A("sl", 192 * t, 192 * t + 192), si, back, ALU.add, float(ZC), ALU.min)
+        if t == 2:
+            for c in range(2):
+                lo, hi, pz = 512 * c, 512 * c + 512, P(2 * c, 0, 512)
+                mm(pz, [(idh, A("one", 0, 512)), (idb, A(uv, VO + lo, VO + hi))])
+                tt(A("zt", lo, hi), pz, A("us", lo, hi), ALU.mult)
+                act(A("sig", lo, hi), A("zt", lo, hi), ACT.Sigmoid, scale=0.5)
+        ts(A("lv", 0, 64), rk, m, ALU.is_ge, -8.0 * BIG, ALU.mult)
+        tt(A("fl", 0, 64), A("lv", 0, 64), A("fk", 0, 64), ALU.add)
         if t < 2:
             prefill(t + 1)
-        cp(G(utab, asu), A("rcv", r0, r0 + 256))
+        cp(G(utab, asu), got["u"])
         if t == 2:
             yield
-        faces = A("rcv", r0 + 256, r0 + 512)
-        if OPT["gf"][t] == "V":
-            cp(G(A("gf", 0, VO), asu), faces)
-        else:
-            ts(A("ro", 0, 64), incl, -1.0, ALU.add, 255.0, ALU.min)
-            for c in range(2):
-                act(A("gf", 512 * c, 512 * c + 512), G(faces, A("ro", 32 * c, 32 * c + 32)))
+        hold = P(7 if t < 2 else 1, 256, 512)
+        mm(hold, [(idk, A("kr", 1, 257)), (A("st", 0, 128), le)], True, False)
+        mm(hold, [(blk, got["f"])], False)
+        scan(A("hs", 1, 257), hold, A("zz", 0, 256), -4.0 * BIG, ALU.max, ALU.add)
         if t < 2:
-            cp(G(A(uv, VO, 2 * VO), asu), A("rcv", r0 + 512, r0 + 768))
+            rows(t + 1)
+            cp(G(A(uv, VO, 2 * VO), asu), got["v"])
         else:
             o, z = G(A("sig", 0, VO), asu), A("zt", 0, 256)
-            mm(P(5, 0, 256), [(idb, A("rcv", r0 + 512, r0 + 768))])
-            tt(z, P(5, 0, 256), A("rcv", r0, r0 + 256), ALU.mult)
+            mm(P(3, 256, 512), [(idb, got["v"])])
+            tt(z, P(3, 256, 512), got["u"], ALU.mult)
             add("s", lambda q: q.activation(o["ap"], z["ap"], ACT.Sigmoid), COST["fix"] + 256 * COST["sca"] * cy, [z], [o])
-            act(P(5, 0, 512), A("sig", 512, K))
-        pf = (P(3, 384, 448) if OPT["nn"] == "V" else P(7, 384, 448)) if t < 2 else P(4, 256, 320)
-        mm(pf, [(idf, A("fk", 0, 64))], True, False)
-        mm(pf, [(sh("q1", i), A("gf", i, K, 16)) for i in range(16)], False, True)
-        tt(A("t2", 0, 64), pf, lv, ALU.mult)
-        tt(f, A("t2", 0, 64), f, ALU.add)
-        if t < 2:
-            ts(A("fu", 0, 64), f, float(NV), ALU.min)
-        else:
-            cp(A("fu", 0, 64), f)
+            act(A("sa", 0, 512), A("sig", 0, 512), scale=0.125)
+        tt(A("t2", 0, 64), G(A("hs", 0, 257), A("ro", 0, 4)), A("fl", 0, 64), ALU.subtract)
+        tt(f, A("t2", 0, 64), f, ALU.min)
+        ts(A("fu", 0, 64), f, EDGE, ALU.add, float(NV if t < 2 else NW), ALU.min)
 
     def follower_lists(t):
         for j, mat in ((0, "w0"), (1, "w1")):
             o = P(7, 64 * j, 64 * j + 48)
-            mm(o, [(sh(mat, i), A("nnd", 4 * i + t, NV, 64)) for i in range(16)] + [(idf, A("sf", 0, 48))])
-            ts(A("nl", 144 * j + 48 * t, 144 * j + 48 * t + 48), o, float(t), ALU.add)
+            mm(o, [(idf, A("sf", 0, 48))], True, False)
+            mm(o, [(sh(mat, i), A("nnd", 4 * i + t, NV, 64)) for i in range(16)], False)
+            ts(A("nl", 144 * j + 48 * t, 144 * j + 48 * t + 48), o, 2.0, ALU.mult, float(t), ALU.add)
         if t < 2 and any(OPT["pre3"][t:2]):
             o = P(7, 128, 140)
             wrap(o, "q1", "dm", BL * t + 576, BL * t + BL)
-            act(A("md", 12 * t, 12 * t + 12), o, scale=ZC / 16.0)
+            act(A("md", 12 * t, 12 * t + 12), o, scale=256.0)
         if t < 2 and OPT["pre3"][t]:
             ghosts(t)
             correct(t, 3)
         if t == 2 and OPT["pre3"][t]:
             o = P(7, 128, 176)
             mm(o, [(sh("q1", i), A("dm", BL * (i % 4) + 576 + i // 4, BL * (i % 4) + BL, 4)) for i in range(16) if i % 4 < 3])
-            act(A("md", 24, 72), o, scale=ZC / 16.0)
+            act(A("md", 24, 72), o, scale=256.0)
 
     def ghosts(t):
-        if t == 0:
-            act(A("w", NV, NW), A("gl0", 0, 512), scale=0.25)
-        else:
-            act(A("w", NV, NW), A("gl", 512 * t - 512, 512 * t), scale=2.0)
-            for c in range(t if OPT["gs"] else 0):
+        if t > 0:
+            copy(A("w", NV, NW), A("gl", 512 * t - 512, 512 * t), 2048)
+            for c in range(t):
                 o = 128 * (t - 1 + c)
-                lin(OPT["gs"][c], A("w", NV + c, NW, 4), A("gr", o, o + 128), scale=2.0)
+                if OPT["gr"] == "g":
+                    line[0] = None
+                    pick(A("w", NV + c, NW, 4), A("gr", o, o + 128), ALU.is_ge, 0.0, 128, 1)
+                else:
+                    lin(OPT["gr"], A("w", NV + c, NW, 4), A("gr", o, o + 128))
 
     def live(b):
         for c in range(2):
             how = OPT["xl"][b][c]
             lo, hi = BL * b + 384 * c, BL * b + 384 * c + 384
-            g = G(A("us", 0, VO), A("sl", 384 + lo // 16, 384 + hi // 16))
+            g = G(A("us", 0, SPARE), A("sl", 384 + lo // 16, 384 + hi // 16))
             if how == "V":
                 tt(A("w", lo, hi), g, A("w", lo, hi), ALU.add)
                 continue
             act(A("x", lo, hi), g)
-            if how == "A":
-                o = P(6 + b % 2, 0, 384) if OPT["oh"] == "D" or OPT["early"] else P(3 + b % 2, 128, 512)
-                mm(o, [(idf, A("w", lo, hi))], True, False)
-                mm(o, [(idb, A("x", lo, hi))], False, True)
-                act(A("w", lo, hi), o)
+            if OPT["xl"][b] != "DD":
+                dadd(A("w", lo, hi), A("x", lo, hi))
         if OPT["xl"][b] == "DD":
             dadd(A("w", BL * b, BL * b + BL), A("x", BL * b, BL * b + BL))
 
     yh = {"ap": T.yh[:], "reg": [("yh", 0, BL, 1)], "n": BL}
 
     def total(b):
-        src = A("w", BL * b, BL * b + BL)
-        if OPT["oh"] == "D":
-            if b == 3:
-                store(yh, src, "y", 3072)
-            else:
-                dadd(yh, src)
-        elif b > 0 or OPT["oh"] == "P":
-            for bank, lo, hi in ((7, 512, BL), (6, 0, 512)):
-                mm(P(bank, 0, hi - lo), [(idf, A("w", BL * b + lo, BL * b + hi))], b == 3, b == (0 if OPT["oh"] == "P" else 1))
+        for j, c in enumerate(OPT["sums"]):
+            mm(P(6 + j // 2, 192 * (j % 2), 192 * (j % 2) + 192), [(idf, A("w", BL * b + c, BL * b + BL, 4))], b == 3 and j % 2 == 0, b == 0 and j % 2 == 1)
 
     def heights(t):
-        s = 2.0 ** (t - 9)
         if not OPT["pre3"][t]:
             ghosts(t)
         parts = OPT["xparts"][t]
@@ -697,109 +666,108 @@ def build(T, topo, core):
             for c in range(4):
                 if c != t + 1:
                     o = 192 * t + 48 * c + m * k
-                    lin(OPT["xc"][t][c], A("x", 64 * m * k + c, 64 * m * (k + 1), 4), G(A(UV[t + 1], 0, VO), A("sl", o, o + m)), bias=-0.5 * s, scale=s)
+                    lin(OPT["xc"][t][c], A("x", 64 * m * k + c, 64 * m * (k + 1), 4), G(A(UV[t + 1], 0, SPARE), A("sl", o, o + m)),
+                        bias=-2.0 ** (t + 1), scale=2.0 ** (t + 2))
         cuts = OPT["dcuts"][t]
         for hi, lo in zip(cuts, cuts[1:]):
             dadd(A("w", BL * lo, BL * hi), A("x", BL * lo, BL * hi))
         gl = A("gl", 512 * t, 512 * t + 512)
-        if OPT["gs"]:
-            send(A("w", 0, 512), [(prv, gl)], [nxt], [gl], 2048, "k")
+        send(A("w", 0, 512), [(prv, gl)], [nxt], [gl], 2048, "k", True)
         for b in range(2 if OPT["pre3"][t] else 3, -1, -1):
             correct(t, b)
-        if OPT["gs"]:
-            gr = A("gr", 128 * t, 256 * t + 128)
-            send(A("gs", 128 * t, 256 * t + 128), [(prv, gr)], [nxt], [gr], 512 * (t + 1), "k")
-        else:
-            send(A("w", 0, 512), [(prv, gl)], [nxt], [gl], 2048, "k")
+        gr = A("gr", 128 * t, 256 * t + 128)
+        send(A("gs", 128 * t, 256 * t + 128), [(prv, gr)], [nxt], [gr], 512 * (t + 1), "k", True)
 
-    def factors():
-        for b in range(3, -1, -1):
-            for c in range(3):
-                i = 192 * (3 * (3 - b) + c)
-                cut = min(192, 512 - i % 512)
-                for lo, hi in ((0, cut), (cut, 192)):
-                    if lo < hi:
-                        d0 = BL * c + 192 * b
-                        mm(A("ps", i + lo, i + hi), [(id256, A("ah", BL * b + 4 * lo + c, BL * b + 4 * hi, 4)), (idn, A("dm", d0 + lo, d0 + hi)), (idb, A("one", lo, hi))])
+    def factors(b):
+        for c in range(3):
+            d0 = BL * c + 192 * b
+            mm(P(2 - 2 * (b % 2) + c // 2, 192 * (c % 2), 192 * (c % 2) + 192),
+               [(id256, A("ah", BL * b + c, BL * b + BL, 4)), (idn, A("dm", d0, d0 + 192)), (idb, A("one", 0, 192))])
+
+    def last(b):
+        win = A("w", BL * b, NW)
+        for c in OPT["turn"]:
+            o = 48 * c + 12 * b
+            act(A("h1", 192 * c, 192 * c + 192), G(win, A("nl", o, o + 12)))
+            tt(A("p2", 192 * c, 192 * c + 192), G(win, A("nl", 144 + o, 156 + o)), A("bh", BL * b + c, BL * b + BL, 4), ALU.mult)
+        done = []
+        for j, cs in enumerate(((0, 1), (2,))):
+            how, bank, lo, k = OPT["last"][b][j], 2 - 2 * (b % 2) + j, 192 * cs[0], 192 * len(cs)
+            out = P(4 + j if how == "P" else bank, 0, k)
+            if how == "P":
+                mm(out, [(idb, A("zz", 0, k))], True, False)
+            for x, y in [(0, k)] if how != "B" else [(192 * i, 192 * i + 192) for i in range(len(cs))]:
+                tt(P(4 + j if how == "P" else bank, x, y), P(bank, x, y), A("h1", lo + x, lo + y), ALU.mult)
+            if how == "P":
+                mm(out, [(idf, A("p2", lo, lo + k))], False)
+            done += [(how, c, P(4 + j if how == "P" else bank, 192 * i, 192 * i + 192)) for i, c in enumerate(cs)]
+        for how, c, x in done:
+            o = A("w", BL * b + c, BL * b + BL, 4)
+            if how == "P":
+                act(o, x)
+            else:
+                tt(o, x, A("p2", 192 * c, 192 * c + 192), ALU.add)
 
     def correct(t, b):
-        if True:
-            win = A("w", BL * b, NW)
-            m = 128 if b == 0 and t < 2 else 192
-            adds, work = [], []
-            hows = OPT["corr"][t][b]
-            for c in range(t + 1):
-                lo, hi = BL * b + c, BL * b + 4 * m
-                l0 = A("nl", 48 * c + 12 * b, 48 * c + 12 * b + m // 16)
-                l1 = A("nl", 144 + 48 * c + 12 * b, 144 + 48 * c + 12 * b + m // 16)
-                h1, p2 = (A(x, m * c, m * c + m) for x in ("h1", "p2"))
-                if t == 2 and OPT["early"]:
-                    i = 192 * (3 * (3 - b) + c)
-                    pa = pr = A("ps", i, i + 192)
-                elif t == 2:
-                    pa, pr = P(c // 2, m * (c % 2), m * (c % 2) + m), P(2 + c, 0, m)
-                elif "P" in hows or "M" in hows or b == 0 and OPT["gs"]:
-                    pa, pr = P(6, m * c, m * c + m), P(7, m * c, m * c + m)
-                else:
-                    pa, pr = P(6 + c, 0, m), None
-                d0 = BL * c + 192 * b
-                if t < 2 or not OPT["early"]:
-                    mm(pa, [(id256, A("ah", lo, hi, 4)), (idn, A("dm", d0, d0 + m)), (idb, A("one", 0, m))])
-                act(h1, G(win, l0))
-                tt(p2, G(win, l1), A("bh", lo, hi, 4), ALU.mult)
-                work.append((hows[c], A("w", lo, hi, 4), pa, pr, h1, p2))
-            k = m * (t + 1)
-            if t < 2 and b == 0 and OPT["gs"]:
-                tt(P(6, 0, k), P(6, 0, k), A("h1", 0, k), ALU.mult)
-                tt(A("gs", 128 * t, 128 * t + k), P(6, 0, k), A("p2", 0, k), ALU.add)
-            elif t < 2 and "M" in hows:
-                tt(P(6, 0, k), P(6, 0, k), A("h1", 0, k), ALU.mult)
-                for how, o, pa, pr, h1, p2 in work:
-                    tt(o, pa, p2, ALU.add)
-            elif t < 2 and "P" in hows:
-                mm(P(7, 0, k), [(idb, A("hc", 0, k))], True, False)
-                tt(P(7, 0, k), P(6, 0, k), A("h1", 0, k), ALU.mult)
-                mm(P(7, 0, k), [(idf, A("p2", 0, k))], False)
-                for how, o, pa, pr, h1, p2 in work:
-                    act(o, pr)
-            else:
-                for how, o, pa, pr, h1, p2 in work:
-                    if how == "P":
-                        mm(pr, [(idb, A("hc", 0, m))], True, False)
-                        tt(pr, pa, h1, ALU.mult)
-                        mm(pr, [(idf, p2)], False)
-                    elif t == 2:
-                        tt(pr, pa, h1, ALU.mult)
-                    else:
-                        tt(pa, pa, h1, ALU.mult)
-                        pr = pa
-                    adds.append((how, o, pr, p2))
-                for how, o, pr, p2 in adds:
-                    if how == "P":
-                        act(o, pr)
-                    else:
-                        tt(o, pr, p2, ALU.add)
+        win = A("w", BL * b, NW)
+        m = 128 if b == 0 and t < 2 else 192
+        hows = OPT["corr"][t][b]
+        k = m * (t + 1)
+        i0 = 512 * 6
+        work = []
+        for c in range(t + 1):
+            lo, hi = BL * b + c, BL * b + 4 * m
+            l0 = A("nl", 48 * c + 12 * b, 48 * c + 12 * b + m // 16)
+            l1 = A("nl", 144 + 48 * c + 12 * b, 144 + 48 * c + 12 * b + m // 16)
+            h1, p2 = (A(x, m * c, m * c + m) for x in ("h1", "p2"))
+            pa = A("ps", i0 + m * c, i0 + m * c + m)
+            d0 = BL * c + 192 * b
+            if t < 2:
+                mm(pa, [(id256, A("ah", lo, hi, 4)), (idn, A("dm", d0, d0 + m)), (idb, A("one", 0, m))])
+            act(h1, G(win, l0))
+            tt(p2, G(win, l1), A("bh", lo, hi, 4), ALU.mult)
+            work.append((hows[c], A("w", lo, hi, 4), pa, h1, p2))
+        both = A("ps", i0, i0 + k)
+        if t < 2 and b == 0:
+            tt(both, both, A("h1", 0, k), ALU.mult)
+            tt(A("gs", 128 * t, 128 * t + k), both, A("p2", 0, k), ALU.add)
+        elif "M" in hows:
+            tt(both, both, A("h1", 0, k), ALU.mult)
+            for how, o, pa, h1, p2 in work:
+                tt(o, pa, p2, ALU.add)
+        elif t < 2 and "P" in hows:
+            mm(P(7, 0, k), [(idb, A("zz", 0, k))], True, False)
+            tt(P(7, 0, k), both, A("h1", 0, k), ALU.mult)
+            mm(P(7, 0, k), [(idf, A("p2", 0, k))], False)
+            for c, (how, o, pa, h1, p2) in enumerate(work):
+                act(o, P(7, m * c, m * c + m))
+        else:
+            for how, o, pa, h1, p2 in work:
+                tt(pa, pa, h1, ALU.mult)
+            for how, o, pa, h1, p2 in work:
+                tt(o, pa, p2, ALU.add)
 
     def outputs():
         win = A("w", 0, NW)
-        act(A("hb", 0, 512), G(win, A("fu", 32, 64)))
-        tt(A("pa", 0, 512), G(win, A("fu", 0, 32)), A("sig", 0, 512), ALU.mult)
-        z = P(5, 0, 512)
+        act(A("hb", 0, 512), G(win, A("fu", 32, 64)), scale=0.125)
+        tt(A("pa", 0, 512), G(win, A("fu", 0, 32)), A("sa", 0, 512), ALU.mult)
+        z = P(0, 0, 512)
         tt(z, z, A("hb", 0, 512), ALU.mult)
         tt(A("ow", 0, 512), z, A("pa", 0, 512), ALU.add)
-        if OPT["oh"] == "P":
-            act(A("oh", 512, BL), P(7, 0, 256))
-            act(A("oh", 0, 512), P(6, 0, 512))
-        elif OPT["oh"] == "V":
-            tt(A("oh", 0, BL), P(6, 0, BL), A("w", 0, BL), ALU.add)
-        store({"ap": T.yw[:], "reg": [("yw", 0, 512, 1)]}, A("ow", 0, 512), "y", 2048)
-        if OPT["oh"] != "D":
-            store(yh, A("oh", 0, BL), "y", 3072)
+        for j, c in enumerate(OPT["sums"]):
+            act(A("oh", c, BL, 4), P(6 + j // 2, 192 * (j % 2), 192 * (j % 2) + 192), scale=0.125)
+        copy({"ap": T.yw[:], "reg": [("yw", 0, 512, 1)]}, A("ow", 0, 512), 2048)
+        copy(yh, A("oh", 0, BL), 3072)
 
+    lists(0)
     prefill(0)
+    rows(0)
     for t in range(3):
         collapse(t)
         fill[0] = True
+        if t == 0:
+            for c in range(1, 4):
+                lists(c)
         if t > 0:
             heights(t - 1)
         follower_lists(t)
@@ -812,16 +780,22 @@ def build(T, topo, core):
         rest = moves(t)
         next(rest, None)
     ghosts(2)
-    if OPT["early"]:
-        factors()
+    factors(3)
+    factors(2)
     if OPT["pre3"][2]:
-        correct(2, 3)
+        last(3)
+        factors(1)
     for b in range(3, -1, -1):
         live(b)
-    next(rest, None)
     for b in range(3, -1, -1):
+        if b == OPT["rest"]:
+            next(rest, None)
         if b < 3 or not OPT["pre3"][2]:
-            correct(2, b)
+            last(b)
+            if b > 1:
+                factors(b - 2)
+        if b == 1:
+            act(P(0, 0, 512), A("sig", 512, K))
         total(b)
     outputs()
     return ops

@@ -6,13 +6,14 @@ from concourse.mybir import AluOpType, AxisListType, ActivationFunctionType
 F32, BF, I32, U16 = "float32", "bfloat16", "int32", "uint16"
 NV, NW, BL, K = 3072, 3584, 768, 1024
 NZ = NV + 32
+WZ = NW + 8
 ZC = K
 SPARE = K + 16
 VO = SPARE + 256
 UV = ("uv", "uv0", "uv", "uv0")
 BIG = 2.0 ** 21
 EDGE = NV - 0.5
-HALF = 127.5 / 256
+HALF = 127.7 / 256
 
 
 def _sb(n, d):
@@ -21,20 +22,21 @@ def _sb(n, d):
 
 SCRATCH = {
     "ps": ("psum", [128, 4096], F32),
-    "a": _sb(NV, BF), "b": _sb(NV, BF), "zz": _sb(NZ // 4, BF),
+    "a": _sb(NV, BF), "b": _sb(NZ, BF), "zz": _sb(NZ // 4, BF),
     "uv": _sb(2 * VO, BF), "uv0": _sb(2 * VO, BF), "uw": _sb(2 * VO, BF), "us": _sb(VO, BF),
     "md": _sb(72, BF), "id512": _sb(128, BF), "gs": _sb(384, F32), "gr": _sb(384, F32), "gl": _sb(1024, F32),
     "mqu": _sb(K, I32), "mqv": _sb(K, I32), "one": _sb(512, BF),
     "nab": _sb(384, I32), "sdi": _sb(192, I32), "pfi": _sb(64, I32), "thi": _sb(4, I32),
+    "idm": _sb(128, BF), "idq": _sb(128, BF), "wz": _sb(144, BF),
     "ci": _sb(4, I32), "cf": _sb(24, F32), "cb": _sb(8, BF), "kr": _sb(272, BF), "r16": _sb(128, BF),
     "q1": _sb(144, BF), "wd": _sb(144, BF), "w0": _sb(144, BF), "w1": _sb(144, BF),
     "blk": _sb(128, BF), "blm": _sb(128, BF), "idb": _sb(128, BF), "idn": _sb(128, BF), "idh": _sb(128, BF), "id256": _sb(128, BF),
     "idk": _sb(128, BF), "id64": _sb(128, BF), "id32": _sb(128, BF), "idf": _sb(128, F32),
     "tri": _sb(128, BF), "tr4": _sb(128, BF), "st": _sb(256, BF), "su": _sb(256, BF),
     "i16": _sb(16, F32), "bm": _sb(16 * 144, BF),
-    "kw": _sb(32, F32), "fw": _sb(16, F32), "sf0": _sb(48, F32), "sf": _sb(48, F32), "kt": _sb(K, BF), "jt": _sb(512, BF),
+    "kw": _sb(32, F32), "fw": _sb(16, F32), "sf0": _sb(96, F32), "sf": _sb(96, F32), "zc": _sb(96, F32), "nf": _sb(96, F32), "kt": _sb(K, BF), "jt": _sb(512, BF),
     "thf": _sb(8, F32), "shl": _sb(192, "float16"), "dhl": _sb(768, BF),
-    "nnd": _sb(NZ, BF), "ah": _sb(NZ, BF), "bh": _sb(NZ, BF), "dm": _sb(3 * BL, BF),
+    "nnd": _sb(NZ, BF), "ah": _sb(NZ, BF), "dm": _sb(BL, BF),
     "sdf": _sb(384, F32), "si": _sb(192, BF), "sl": _sb(624, U16),
     "dd": _sb(BL, F32), "xs": _sb(BL, BF), "c1": _sb(BL, BF), "c2": _sb(BL, BF),
     "ff": _sb(128, F32), "fu": _sb(64, U16), "sg": _sb(64, F32), "t2": _sb(64, F32),
@@ -45,7 +47,7 @@ SCRATCH = {
     "e1": _sb(16, F32), "e2": _sb(16, F32), "e3": _sb(16, F32),
     "cin": _sb(60, F32), "mm": _sb(12, F32), "lv": _sb(64, F32), "fk": _sb(64, F32), "fl": _sb(64, F32),
     "snd": _sb(768, BF), "rcv": _sb(3 * 768, BF), "ru": _sb(6 * K, BF), "ra": _sb(48, U16),
-    "w": _sb(NW, F32), "x": _sb(NV, BF),
+    "w": _sb(WZ, F32), "x": _sb(NV, BF),
     "nl": _sb(6 * 48, U16), "h1": _sb(3 * 192, F32), "p2": _sb(3 * 192, F32),
     "zt": _sb(K + 16, F32), "sig": _sb(VO, F32), "sa": _sb(512, F32), "pa": _sb(512, F32), "hb": _sb(512, F32),
     "oh": _sb(BL, F32), "ow": _sb(512, F32),
@@ -53,20 +55,28 @@ SCRATCH = {
 SEMAPHORES = ["cv", "cs", "cp", "cg"] + ["d%d" % i for i in range(48)] + ["l%d" % i for i in range(32)] + ["r%d" % i for i in range(32)]
 COUNTER = {"v": "cv", "s": "cs", "p": "cp", "g": "cg"}
 
-COST = {"cyc": 0.95, "pe": 0.49, "mm": 3.0, "gat": 1.55, "sca": 3.8, "fix": 60.0, "lat": 120.0, "own": 120.0, "remote": 1800.0, "rows": 800.0, "link": 1.4, "rissue": 900.0,
-        "gissue": 900.0, "glat": 3000.0}
+SLOW = {"remote": 2600.0, "rows": 1200.0, "rissue": 1300.0, "gissue": 1300.0, "glat": 4000.0, "lat": 160.0, "own": 160.0, "once": 2500.0}
+FAST = {"remote": 1300.0, "rows": 500.0, "rissue": 600.0, "gissue": 600.0, "glat": 2400.0, "lat": 80.0, "own": 80.0}
+CASES = [{"cyc": 0.85}, {"cyc": 1.2, "gat": 1.2, "sca": 2.5}, {"cyc": 1.05, "gat": 2.0, "sca": 5.5},
+         dict(SLOW, cyc=1.0, gat=1.3, sca=4.5), dict(FAST, cyc=1.1, gat=1.8, sca=2.0)]
+COST = {"cyc": 1.0, "pe": 0.52, "mm": 3.0, "gat": 1.55, "sca": 3.8, "fix": 60.0, "lat": 120.0, "own": 120.0, "remote": 1800.0, "rows": 800.0, "link": 1.4, "rissue": 900.0,
+        "gissue": 900.0, "glat": 3000.0, "drow": 100.0, "issue": 60.0, "once": 1000.0}
 OPT = {
     "corr": [["M"] * 4, ["MM"] * 4, ["BBB"] * 4], "cmp": "VVV",
-    "hop": ["SVSV", "SVSV", "SSSS"],
-    "ga": "SSSS", "gb": "SSSS", "gn": "SSSS",
+    "hop": ["SWSW", "SWSW", "SSSW"],
+    "apart": [(1, 0), (1, 0), (1, 0)],
+    "inturn": 1, "share": "", "fold": 0.0, "store": "s",
     "stag": [(("m2", 0, 1), ("vn", 0, 0)), (("m2", 1, 1), ("vn", 1, 0))],
-    "early": ["u", "u", "u"], "parts": ["uvf", "uvf", "uvf"], "accs": [4, 4, 4], "last": ["MB", "MP", "MP", "MP"], "turn": (0, 1, 2), "sums": (3, 0, 1, 2), "rest": 2,
+    "early": ["u", "u", "u"], "parts": ["uvf", "uvf", "uvf"], "accs": [4, 4, 4], "last": ["MMM", "MMP", "MMP", "MMP"], "turn": (0, 1, 2), "sums": (3, 0, 1, 2), "rest": 2,
     "cuts": [(256, 512, 768), (256, 512, 768), (256, 768)], "dcuts": [(4, 2, 0), (4, 2, 0)],
-    "loads": ["b", "na", "nb", "pf", "v", "bh", "nnd"], "direct": [(), (), ()],
-    "xparts": [2, 2], "x0": "VV", "xs": ["VS", "SS"], "xc": ["SSSS", "SSSS"], "gr": "S", "us": "SS",
+    "loads": [("sd", "y"), ("u", "s"), ("a0", "y"), ("a1", "s"), ("th", "y"), ("b", "y"), ("na", "y"), ("nb", "y"), ("pf", "y"), ("v", "y"),
+              (0, "s"), (1, "s"), (2, "y"), (3, "y")],
+    "zeros": {"ah": "g"}, "direct": [(), (), ()],
+    "xparts": [2, 2], "x0": "VV", "xs": ["VS", "VS"], "xc": ["SSSS", "SSSS"], "gr": "S", "us": "SS",
     "xl": ["DD", "DD", "VV", "VV"], "pre3": [1, 1, 0], "dead": "SS", "oh": "P", "sv": "S", "su": "S", "bm0": "VSVS",
-    "sweeps": 8, "wide": 24000.0, "tries": 300, "near": 0.5, "cool": 100.0,
-    "aim": 0.85, "reach": 2000.0, "every": 10, "passes": 9000, "noise": 4000.0, "span": 10000.0, "later": [0.0, 5e3, 1e4, 2e4, 4e4, 1e6], "seed": 1, "pull": 3.0, "warm": 250.0}
+    "starts": 5, "rounds": (3, 26), "part": 100, "steps": 400, "heat": 0.002, "give": 0.001, "mean": 0.5, "short": 0.5,
+    "sweeps": 2, "wide": 24000.0, "tries": 300, "near": 0.5, "cool": 100.0,
+    "aim": 0.85, "reach": 2000.0, "every": 10, "passes": 2500, "noise": 4000.0, "span": 10000.0, "later": [0.0, 5e3, 1e4, 2e4, 4e4, 1e6], "seed": 1, "pull": 3.0, "warm": 250.0}
 
 
 def build(T, topo, core):
@@ -155,8 +165,8 @@ def build(T, topo, core):
             for o, l, r, a, z in items:
                 last = q.matmul(o["ap"], l["ap"], r["ap"], a, z)
             return last
-        dur = 30.0 + sum(COST["mm"] + max(64, r["n"]) * (4 if r["d"] == F32 else 1) * COST["pe"] for o, l, r, a, z in items)
-        add("p", fn, dur, [x for it in items for x in it[1:3]], [it[0] for it in items])
+        dur = 30.0 + sum(COST["mm"] + max(64, r["n"]) * (4 if r["d"] == F32 else 1) * COST["pe"] * cy for o, l, r, a, z in items)
+        add("p", fn, dur, [x for it in items for x in it[1:3]], [it[0] for it in items], adds=not items[0][3])
 
     def mm(out, pairs, start=True, stop=True):
         mms([(out, l, r, start and j == 0, stop and j == len(pairs) - 1) for j, (l, r) in enumerate(pairs)])
@@ -182,25 +192,35 @@ def build(T, topo, core):
     def diag(name, c):
         pick(A(name, 0, 128), A("zz", 0, 128), ALU.not_equal, c, 0, 1)
 
-    nd, nr, bus = [0], [0], [0.0, 0]
+    nd, nr, bus, used = [0], [0], {"busy": 0.0}, set()
 
     def sem():
         nd[0] += 1
         return "d%d" % (nd[0] - 1)
 
-    def load(dst, src, nbytes):
-        bus[0] += nbytes * 0.22 - 60.0
-        j = add("y", lambda q: q.dma_start(dst["ap"], src), 60.0, [], [dst], kind="dma", sem=sem(), cnt=16, lat=1900.0 + max(bus[0], 0.0))
-        if j > 0:
-            ops[j]["follow"] = bus[1]
-        bus[1] = j
+    def load(queue, dst, src, nbytes):
+        bus["busy"] += nbytes * 0.22 + COST["drow"]
+        before = bus.get(queue, [])
+        j = add(queue, lambda q: q.dma_start(dst["ap"], src), COST["issue"], [], [dst], kind="dma", sem=sem(), cnt=16,
+                lat=1700.0 + bus["busy"] - COST["issue"] * len(before))
+        if before:
+            ops[j]["follow"] = before[-1]
+        bus[queue] = before + [j]
 
-    def copy(dst, src, nbytes):
-        add("y", lambda q: q.dma_start(dst["ap"], src["ap"]), 60.0, [src], [dst], kind="dma", sem=sem(), cnt=16, lat=1900.0 + nbytes * 0.22)
+    def copy(dst, src, nbytes, queue="y"):
+        add(queue, lambda q: q.dma_start(dst["ap"], src["ap"]), 60.0, [src], [dst], kind="dma", sem=sem(), cnt=16, lat=1900.0 + nbytes * 0.22,
+            lead=1500.0)
+        share(dst, nbytes * 0.22)
+
+    def share(dst, busy):
+        j = len(ops) - 1
+        for x in OPT["share"]:
+            add(x, None, 400.0 + busy, [], [dst], kind="recv", sem=ops[j]["sem"], cnt=16, after=j, lat=0.0)
 
     def dadd(dst, src):
         add("g", lambda q: q.dma_start(dst["ap"], src["ap"], accum_op=ALU.add), COST["gissue"], [src, dst], [dst], kind="dma", sem=sem(), cnt=16,
-            lat=COST["glat"] + dst["n"] * 4 * 0.3)
+            lat=COST["glat"] + dst["n"] * 4 * 0.3, lead=COST["glat"] - 900.0)
+        share(dst, 500.0 + dst["n"] * 4 * 0.3)
 
     def engines(a, b, wide=False):
         far = -1
@@ -224,10 +244,13 @@ def build(T, topo, core):
                 trs.append(RemoteDMATransfer(dst_ids=[DstId(rid=topo.addr(c)[0], pnc=topo.addr(c)[1]) for c, _ in to], dma_engine_mask=m, remote_sem=T.sem[rs],
                                              srcs=[src["ap"]] * (2 if twice else 1), dsts=[d["ap"] for _, d in to], alu_op=1 if twice else 0))
             return q.remote_dma_fused(trs, local_sem=T.sem[ls])
-        rows = COST["rows"] * min(len(dsts), 2) + nbytes * COST["link"]
+        rows = COST["rows"] * min(len(dsts), 2) + nbytes * COST["link"] * (1 + twice * OPT["fold"])
         left = sum(bin(m).count("1") for m in masks)
-        j = add("g", fn, COST["rissue"], [src], [], kind="send", sem=ls, cnt=left, lat=COST["remote"] + rows, lead=COST["remote"])
-        add(lane, None, rows, [], lands, kind="recv", sem=rs, cnt=sum(bin(engines(c, core)).count("1") for c in froms), after=j, lat=0.0)
+        new = COST["once"] * (lane not in used)
+        used.add(lane)
+        j = add("g", fn, COST["rissue"] + new, [src], [], kind="send", sem=ls, cnt=left, lat=COST["remote"] + rows + new, lead=COST["remote"] + new)
+        for x in lane:
+            add(x, None, rows, [], lands, kind="recv", sem=rs, cnt=sum(bin(engines(c, core)).count("1") for c in froms), after=j, lat=0.0)
 
     nxt, prv = T.cores[(rank + 1) % n], T.cores[(rank - 1) % n]
 
@@ -237,22 +260,19 @@ def build(T, topo, core):
     def wrap(out, mat, src, lo, hi, start=True):
         mm(out, [(sh(mat, i), A(src, lo + i, hi, 16)) for i in range(16)], start)
 
-    load(A("sdi", 0, 192), T.sd[:], 768)
-    load(A("uv", 0, K), T.u0[:], 2048)
-    for c in range(2):
-        load(A("a", 1536 * c, 1536 * c + 1536), T.ta[:, 1536 * c:1536 * c + 1536], 3072)
-    load(A("thi", 0, 3), T.th[:], 200)
+    inputs = {"sd": (A("sdi", 0, 192), T.sd[:], 768), "u": (A("uv", 0, K), T.u0[:], 2048), "th": (A("thi", 0, 3), T.th[:], 12),
+              "a0": (A("a", 0, 1536), T.ta[:, 0:1536], 3072), "a1": (A("a", 1536, NV), T.ta[:, 1536:NV], 3072), "a": (A("a", 0, NV), T.ta[:], 6144),
+              "na": (A("nab", 0, 192), T.na[:], 768), "nb": (A("nab", 192, 384), T.nb[:], 768), "pf": (A("pfi", 0, 64), T.pf[:], 256),
+              "v": (A("uv", VO, VO + K), T.v0[:], 2048), "b": (A("b", 0, NV), T.tb[:], 6144)}
     zz = A("zz", 0, NZ // 4)
-    ms(zz, 0.0)
-    later = {"na": (A("nab", 0, 192), T.na, 768), "nb": (A("nab", 192, 384), T.nb, 768), "pf": (A("pfi", 0, 64), T.pf, 256),
-             "v": (A("uv", VO, VO + K), T.v0, 2048), "b": (A("b", 0, NV), T.tb, 6144)}
-    for name in OPT["loads"]:
-        if name in later:
-            load(later[name][0], later[name][1][:], later[name][2])
+    for name, queue in OPT["loads"]:
+        if name in inputs:
+            load(queue, *inputs[name])
         else:
-            for c in range(4):
-                load(A(name, c * NZ // 4, (c + 1) * NZ // 4), zz["ap"], NZ // 2)
-                ops[-1]["rd"] = zz["reg"]
+            if name == 0:
+                ms(zz, 0.0)
+            load(queue, A("nnd", name * NZ // 4, (name + 1) * NZ // 4), zz["ap"], NZ // 2)
+            ops[-1]["rd"] = zz["reg"]
     landed = [("landed", 0, 1, 1)]
     ops[-1]["wr"] = ops[-1]["wr"] + landed
 
@@ -276,13 +296,20 @@ def build(T, topo, core):
     ts(blk, A("r16", 0, 128), g16, ALU.is_equal)
     ts(idb, A("kr", 0, 128), pc, ALU.is_equal)
     act(id256, idb, scale=1.0 / 256)
-    for name in ("ah", "bh", "nnd"):
-        if name not in OPT["loads"]:
+    for name, how in OPT["zeros"].items():
+        if how == "g":
             for c in range(1, 4):
                 iota(A(name, c, NV, 4), [[0, BL]], 0, 0)
             ms(A(name, NV, NZ), 0.0)
-    diag("idk", 4096.0)
-    diag("idn", -1.0)
+        else:
+            for c in range(1, 4):
+                ms(A(name, c, NV, 4), 0.0)
+            ms(A(name, NV, NZ), 0.0)
+        if name == "ah":
+            diag("idq", -2048.0)
+            diag("idn", -1.0)
+    ms(A("b", NV, NZ), 0.0)
+    diag("idm", 256.0)
     act(idf, idb)
     low = A("cb", 0, 1)
     act(low, lane, ACT.Sigmoid, bias=7.5 * 512, scale=-512.0, extra=1300.0)
@@ -298,12 +325,12 @@ def build(T, topo, core):
 
     cp(A("shl", 0, 192), A("sdi", 0, 192))
     act(col(7), lane, bias=-4112.5)
-    act(P(5, 0, 192), A("kr", 0, 192), bias=col(7), scale=16.0)
+    act(P(7, 0, 192), A("kr", 0, 192), bias=col(7), scale=16.0)
     tt(A("cf", 9, 11), A("i16", 0, 2), A("i16", 8, 10), ALU.add)
-    act(col(9), col(9), bias=-4096.0, scale=-4128.0)
+    act(col(9), col(9), bias=-2048.0, scale=-4128.0)
     act(col(8), col(10), bias=col(9), scale=15.5)
     for j in range(2):
-        tt(P(6, 192 * j, 192 * j + 192), A("nab", 192 * j, 192 * j + 192), P(5, 0, 192), ALU.subtract)
+        tt(P(6, 192 * j, 192 * j + 192), A("nab", 192 * j, 192 * j + 192), P(7, 0, 192), ALU.subtract)
     act(A("dhl", 0, 384), P(6, 0, 384))
     tt(A("dhl", 384, 768), P(6, 0, 384), A("dhl", 0, 384), ALU.subtract)
     ts(A("ff", 32, 96), A("pfi", 0, 64), -EDGE, ALU.add)
@@ -316,22 +343,26 @@ def build(T, topo, core):
     pick(A("tr4", 0, 128), A("tri", 0, 128), ALU.not_equal, -4096.0, 0, 1)
     pick(A("w0", 0, 144), q1, ALU.is_ge, 0.0, -8, 1)
     pick(A("w1", 0, 144), q1, ALU.is_ge, 0.0, 7, -1)
-    iota(A("sf0", 0, 48), [[0, 4], [32, 12]], 0, 0)
+    act(A("wz", 0, 144), q1, scale=64.0)
+    iota(A("sf0", 0, 96), [[1024, 2], [0, 4], [32, 12]], 0, 0)
+    iota(A("zc", 0, 96), [[NW // 2 - 4096, 2], [-BL // 2, 4], [0, 12]], 4096, 0)
+    diag("idk", 4096.0)
     iota(A("one", 0, 512), [[0, 512]], 1, 0)
+    line[0] = add("g", lambda q: q.dma_start(T.w[:, 0:NV], T.h0[:]), COST["gissue"] + COST["once"], [{"reg": landed}], [A("w", 0, NV)], kind="dma", sem=sem(),
+                  cnt=16, lat=COST["glat"] + NV * 4 * 0.22, follow=line[0])
     pick(A("su", 128, 256), sh("q1", 0), ALU.is_equal, 0.0, 0, 1)
     pick(A("su", 0, 128), blk, ALU.is_equal, 0.0, -1, 1)
     pick(A("su", 0, 128), A("su", 0, 128), ALU.not_equal, -1.0, 0, 1)
     for name, c in (("id512", -512.0), ("id64", -64.0), ("id32", -32.0), ("idh", -0.5)):
         diag(name, c)
-    add("g", lambda q: q.dma_start(T.w[:, 0:NV], T.h0[:]), COST["gissue"], [{"reg": landed}], [A("w", 0, NV)], kind="dma", sem=sem(), cnt=16,
-        lat=COST["glat"] + NV * 4 * 0.22, follow=line[0])
     for i in range(16):
         if i % 4:
             act(A("bm", 144 * i, 144 * i + 144), q1, scale=A("i16", i, i + 1))
     act(A("st", 0, 256), A("su", 0, 256), scale=BIG)
     act(A("blm", 0, 128), blk, scale=-128.0)
     act(col(6), lane, scale=2.0)
-    act(A("sf", 0, 48), A("sf0", 0, 48), bias=col(6))
+    act(A("sf", 0, 96), A("sf0", 0, 96), bias=col(6))
+    ms(A("w", NW, WZ), 0.0)
     act(A("fw", 0, 16), A("kr", 0, 16), bias=lane, scale=16.0)
     act(A("kw", 0, 16), A("fw", 0, 16), bias=0.5)
     act(A("kw", 16, 32), A("fw", 0, 16), bias=SPARE - 1008.0)
@@ -356,22 +387,21 @@ def build(T, topo, core):
     fill[0] = True
     cp(A("sdf", 192, 384), A("sdi", 0, 192))
     send(A("w", 0, 512), [(prv, A("w", NV, NW))], [nxt], [A("w", NV, NW)], 2048, "k", True)
+    ghosted = len(ops) - 2
     fill[0] = False
 
-    def prefill(t):
-        for name, mat, bank in (("a", idb, 0), ("b", id256, 2)):
-            for c in range(2):
-                mm(P(bank + c, 0, 384), [(mat, A(name, 1536 * c + t, 1536 * c + 1536, 4))])
-        for c in range(2):
+    def prefill(t, banks=(0, 1, 2, 3)):
+        for bank in banks:
+            c = bank % 2
+            mm(P(bank, 0, 384), [(id256, A("ab"[bank // 2], 1536 * c + t, 1536 * c + 1536, 4))])
+        for c in range(2 * (0 in banks)):
             if t > 0 and c in OPT["direct"][t]:
                 act(A("xs", 384 * c, 384 * c + 384), A("a", 1536 * c + t, 1536 * c + 1536, 4), bias=0.5, scale=1.0 / 256)
 
     def rows(t):
         for q in range(4):
             i = 4 * q + t
-            if q % 2 == 0:
-                mm(P(6 + q // 2, 0, 384), [(idb, A("zz", 0, 384))], True, False)
-            mm(rowsof(q), [(sh("bm", l, 144 * i), A("dhl", c0, c0 + 192)) for l, c0 in ((0, 0), (1, 384), (8, 192), (9, 576))], False, False)
+            mm(rowsof(q), [(sh("bm", l, 144 * i), A("dhl", c0, c0 + 192)) for l, c0 in ((0, 0), (1, 384), (8, 192), (9, 576))], q % 2 == 0, False)
 
     def rowsof(q):
         return P(6 + q // 2, 192 * (q % 2), 192 * (q % 2) + 192)
@@ -380,12 +410,13 @@ def build(T, topo, core):
         for c in range(2):
             lo, hi = 384 * c, 384 * c + 384
             cls = lambda name: A(name, 4 * lo + t, 4 * hi, 4)
-            c1, c2, d, dm = A("c1", lo, hi), A("c2", lo, hi), P(4 + c, 128, 512), A("dm", BL * t + lo, BL * t + hi)
+            c1, c2, d, dm = A("c1", lo, hi), A("c2", lo, hi), P(4 + c, 128, 512), A("dm", lo, hi)
             if t == 0:
                 off = A("sl", 576 + 24 * c, 600 + 24 * c)
                 if OPT["x0"][c] == "V":
                     tt(A("dd", lo, hi), G(A(UV[0], 0, K), off), cls("a"), ALU.subtract)
                     act(c2, A("dd", lo, hi), ACT.Abs, bias=-128.0)
+                    ops[-1]["follow"] = table
                 else:
                     act(A("xs", lo, hi), G(A(UV[0], 0, K), off), bias=-128.0)
                     mm(d, [(idb, cls("a"))], True, False)
@@ -408,15 +439,11 @@ def build(T, topo, core):
                 act(c1, c2, ACT.Sign, bias=A("thf", 4 + t, 5 + t), scale=-1.0)
             thr = 8.5 if OPT["cmp"][t] == "V" else 1.0
             mm(d, [(blk, c1)])
-            if OPT["dead"][c] == "S":
-                act(dm, d, ACT.Sigmoid, bias=-512.0 * thr, scale=512.0)
-                ops[-1]["follow"] = table
-            else:
-                ts(dm, d, thr, ALU.is_ge)
-            tt(cls("ah"), P(c, 0, 384), dm, ALU.mult)
-            tt(cls("bh"), P(2 + c, 0, 384), dm, ALU.mult)
+            act(dm, d, ACT.Sign, bias=thr, scale=-1.0)
+            tt(cls("ah"), P(c, 0, 384), dm, ALU.max)
+            tt(cls("b"), P(2 + c, 0, 384), dm, ALU.max)
         for q in range(4):
-            mm(rowsof(q), [(idk, A("dm", BL * t + q, BL * t + BL, 4))], False, q % 2 == 1)
+            mm(rowsof(q), [(A("idq", 0, 128), A("dm", q, BL, 4))], False, q % 2 == 1)
         for q in range(4):
             act(A("nnd", 4 * q + t, NV, 16), rowsof(q), ACT.Relu, bias=col(8))
 
@@ -433,25 +460,29 @@ def build(T, topo, core):
         un, vn = A(dst, lo, hi), A(dst, VO + lo, VO + hi)
         end = t == 2 and k == 1
         how = OPT["hop"][t][2 * k + c]
-        unit = id256 if t == 0 and k == 0 else idb
+        first = t == 0 and k == 0
+        unit = id256 if first else idb
 
         def mark(name):
             marks[name, k, c] = len(ops) - 1
             for late, early in OPT["stag"]:
                 if late == (name, k, c) and early in marks:
                     ops[-1]["follow"] = marks[early]
-        lin(OPT["ga"][2 * k + c], ga, G(A("ah", 0, NZ), off))
-        lin(OPT["gb"][2 * k + c], gb, G(A("bh", 0, NZ), off), scale=256.0)
-        lin(OPT["gn"][2 * k + c], gn, G(A("nnd", 0, NZ), off))
+        act(ga, G(A("ah", 0, NZ), off))
+        act(gb, G(A("b", 0, NZ), off), scale=256.0)
+        act(gn, G(A("nnd", 0, NZ), off))
         f = A("ff", 32 * c + 32, 32 * c + 64)
         wb = 4 + c
         pm, pn = P(wb, 32 - 32 * c, 64 - 32 * c), P(wb, 32 * c, 32 * c + 32)
-        mm(pv, [(unit, vb)])
+        mm(pv, [(idb if first else A("idm", 0, 128), vb)])
         mm(pa, [(idb, A("zz", 0, 512))], True, False)
         mm(pb, [(idb, A("zz", 0, 512))], True, False)
         tt(pa, pv, ga, ALU.mult)
         mark("m1")
-        if c == 1:
+        apart = OPT["apart"][t][k]
+        if apart:
+            wrap(P(wb, 64 + 32 * c, 96 + 32 * c), "wd", "gg", 512 + lo, 512 + hi)
+        elif c == 1:
             wrap(P(5, 64, 128), "wd", "gg", 512, 1536)
         mm(pa, [(unit, ub)], False)
         tt(pb, pa, gb, ALU.mult)
@@ -471,23 +502,26 @@ def build(T, topo, core):
             send(A("us", lo, hi) if end else un, [(nxt, ru)], [prv], [ru], 1024, "l")
         ts(mqv, pb, -HALF, ALU.add)
         mark("qv")
-        tt(vn, pb, mqv, ALU.subtract)
+        tt(pb if how == "W" else vn, pb, mqv, ALU.subtract)
         mark("vn")
+        if how == "W":
+            tt(ge, pb, un, ALU.is_le)
+            act(vn, pb)
         if k == 1 and "v" in OPT["early"][t]:
             ru = A("ru", 2 * K * t + K + lo, 2 * K * t + K + hi)
             send(vn, [(nxt, ru)], [prv], [ru], 1024, "l")
         if how == "V":
             tt(ge, pa, vn, ALU.is_ge)
-        else:
+        elif how == "S":
             mm(pa, [(idb, un)], True, False)
             mm(pa, [(idn, vn)], False)
             act(ge, pa, ACT.Sign, bias=1.0 / 512)
         yield
-        pd = P(5, 64 + 32 * c, 96 + 32 * c)
+        pd = P(wb if apart else 5, 64 + 32 * c, 96 + 32 * c)
         mm(P(wb, 0, 64), [(idf, A("ff", 64 * c, 64 * c + 64))], True, False)
         wrap(P(wb, 0, 64), "q1", "gg", 2 * lo, 2 * lo + K, False)
         sg, t2 = A("sg", 32 * c, 32 * c + 32), A("t2", 32 * c, 32 * c + 32)
-        act(sg, pn, ACT.Sign, bias=8.5 if how == "V" else 1.0, scale=-1.0)
+        act(sg, pn, ACT.Sign, bias=1.0 if how == "S" else 8.5, scale=-1.0)
         tt(t2, pd, sg, ALU.mult)
         if k == 1:
             tt(A("on", 32 * c, 32 * c + 32), pm, t2, ALU.is_ge)
@@ -508,6 +542,7 @@ def build(T, topo, core):
             mms([(P(b, 64 * j, 64 * j + 64), A("blm", 0, 128), sc, False, j == hi - lo - 1) for j in range(hi - lo)])
         others = [r for r in range(n) if r != rank]
         send(slot(rank), [(T.cores[r], slot(rank)) for r in others], [T.cores[r] for r in others], [slot(r) for r in others], 4, "l")
+        ops[-2]["follow"] = ghosted
         mm(P(5, 64, 128), [(blk, sx), (A("tri", 0, 128), on)])
         incl = A("cc", 0, 64)
         act(incl, P(5, 64, 128))
@@ -535,6 +570,7 @@ def build(T, topo, core):
         ra = A("ra", 16 * t, 16 * t + 16)
         if early:
             send(atu, [(nxt, ra)], [prv], [ra], 32, "l")
+            listed = len(ops) - 2
         vs = {} if t < 2 else {"bias": -0.25, "scale": 0.5}
         if "u" not in early:
             lin(OPT["su"], out["u"], G(A(uv if t < 2 else "us", 0, K), atu))
@@ -549,6 +585,8 @@ def build(T, topo, core):
         cuts = OPT["cuts"][t]
         for lo, hi in zip(cuts, cuts[1:]):
             send(A("snd", lo, hi), [(nxt, A("rcv", r0 + lo, r0 + hi))], [prv], [A("rcv", r0 + lo, r0 + hi)], 2 * (hi - lo), "l")
+            if OPT["inturn"]:
+                ops[-2]["follow"] = len(ops) - 4 if lo > cuts[0] else listed
         if "u" in early:
             lin(OPT["su"], got["u"], G(A("ru", 2 * K * t, 2 * K * t + K), ra))
         if "v" in early:
@@ -591,7 +629,7 @@ def build(T, topo, core):
         cp(G(utab, asu), got["u"])
         if t == 2:
             yield
-        hold = P(7 if t < 2 else 1, 256, 512)
+        hold = P(7 if t < 2 else 4, 256, 512)
         mm(hold, [(idk, A("kr", 1, 257)), (A("st", 0, 128), le)], True, False)
         mm(hold, [(blk, got["f"])], False)
         scan(A("hs", 1, 257), hold, A("zz", 0, 256), -4.0 * BIG, ALU.max, ALU.add)
@@ -600,8 +638,8 @@ def build(T, topo, core):
             cp(G(A(uv, VO, 2 * VO), asu), got["v"])
         else:
             o, z = G(A("sig", 0, VO), asu), A("zt", 0, 256)
-            mm(P(3, 256, 512), [(idb, got["v"])])
-            tt(z, P(3, 256, 512), got["u"], ALU.mult)
+            mm(P(4, 0, 256), [(idb, got["v"])])
+            tt(z, P(4, 0, 256), got["u"], ALU.mult)
             add("s", lambda q: q.activation(o["ap"], z["ap"], ACT.Sigmoid), COST["fix"] + 256 * COST["sca"] * cy, [z], [o])
             act(A("sa", 0, 512), A("sig", 0, 512), scale=0.125)
         tt(A("t2", 0, 64), G(A("hs", 0, 257), A("ro", 0, 4)), A("fl", 0, 64), ALU.subtract)
@@ -609,33 +647,26 @@ def build(T, topo, core):
         ts(A("fu", 0, 64), f, EDGE, ALU.add, float(NV if t < 2 else NW), ALU.min)
 
     def follower_lists(t):
+        mm(P(7, 0, 96), [(idf, A("sf", 0, 96))], True, False)
+        mm(P(7, 48, 96), [(sh("wz", i), A("dm", i, BL, 16)) for i in range(16)], False, False)
         for j, mat in ((0, "w0"), (1, "w1")):
-            o = P(7, 64 * j, 64 * j + 48)
-            mm(o, [(idf, A("sf", 0, 48))], True, False)
-            mm(o, [(sh(mat, i), A("nnd", 4 * i + t, NV, 64)) for i in range(16)], False)
-            ts(A("nl", 144 * j + 48 * t, 144 * j + 48 * t + 48), o, 2.0, ALU.mult, float(t), ALU.add)
+            mm(P(7, 48 * j, 48 * j + 48), [(sh(mat, i), A("nnd", 4 * i + t, NV, 64)) for i in range(16)], False, j == 1)
+        tt(A("nf", 0, 96), P(7, 0, 96), A("zc", 0, 96), ALU.min)
+        ts(A("nl", 96 * t, 96 * t + 96), A("nf", 0, 96), 2.0, ALU.mult, float(t), ALU.add)
         if t < 2 and any(OPT["pre3"][t:2]):
             o = P(7, 128, 140)
-            wrap(o, "q1", "dm", BL * t + 576, BL * t + BL)
-            act(A("md", 12 * t, 12 * t + 12), o, scale=256.0)
-        if t < 2 and OPT["pre3"][t]:
+            wrap(o, "q1", "dm", 576, BL)
+            act(A("md", 12 * t, 12 * t + 12), o, bias=2048.0, scale=-128.0)
+        if t < 2:
             ghosts(t)
             correct(t, 3)
-        if t == 2 and OPT["pre3"][t]:
-            o = P(7, 128, 176)
-            mm(o, [(sh("q1", i), A("dm", BL * (i % 4) + 576 + i // 4, BL * (i % 4) + BL, 4)) for i in range(16) if i % 4 < 3])
-            act(A("md", 24, 72), o, scale=256.0)
 
     def ghosts(t):
         if t > 0:
             copy(A("w", NV, NW), A("gl", 512 * t - 512, 512 * t), 2048)
-            for c in range(t):
-                o = 128 * (t - 1 + c)
-                if OPT["gr"] == "g":
-                    line[0] = None
-                    pick(A("w", NV + c, NW, 4), A("gr", o, o + 128), ALU.is_ge, 0.0, 128, 1)
-                else:
-                    lin(OPT["gr"], A("w", NV + c, NW, 4), A("gr", o, o + 128))
+        for c in range(t):
+            o = 128 * (t - 1 + c)
+            lin(OPT["gr"], A("w", NV + c, NW, 4), A("gr", o, o + 128), scale=2.0)
 
     def live(b):
         for c in range(2):
@@ -646,7 +677,10 @@ def build(T, topo, core):
                 tt(A("w", lo, hi), g, A("w", lo, hi), ALU.add)
                 continue
             act(A("x", lo, hi), g)
-            if OPT["xl"][b] != "DD":
+            if how == "A":
+                mm(P(4 + c, 0, 384), [(idb, A("x", lo, hi))])
+                tt(A("w", lo, hi), P(4 + c, 0, 384), A("w", lo, hi), ALU.add)
+            elif OPT["xl"][b] != "DD":
                 dadd(A("w", lo, hi), A("x", lo, hi))
         if OPT["xl"][b] == "DD":
             dadd(A("w", BL * b, BL * b + BL), A("x", BL * b, BL * b + BL))
@@ -658,8 +692,6 @@ def build(T, topo, core):
             mm(P(6 + j // 2, 192 * (j % 2), 192 * (j % 2) + 192), [(idf, A("w", BL * b + c, BL * b + BL, 4))], b == 3 and j % 2 == 0, b == 0 and j % 2 == 1)
 
     def heights(t):
-        if not OPT["pre3"][t]:
-            ghosts(t)
         parts = OPT["xparts"][t]
         for k in range(parts - 1, -1, -1):
             m = 48 // parts
@@ -676,31 +708,30 @@ def build(T, topo, core):
         for b in range(2 if OPT["pre3"][t] else 3, -1, -1):
             correct(t, b)
         gr = A("gr", 128 * t, 256 * t + 128)
-        send(A("gs", 128 * t, 256 * t + 128), [(prv, gr)], [nxt], [gr], 512 * (t + 1), "k", True)
+        send(A("gs", 128 * t, 256 * t + 128), [(prv, gr)], [nxt], [gr], 512 * (t + 1), "k")
 
     def factors(b):
         for c in range(3):
-            d0 = BL * c + 192 * b
-            mm(P(2 - 2 * (b % 2) + c // 2, 192 * (c % 2), 192 * (c % 2) + 192),
-               [(id256, A("ah", BL * b + c, BL * b + BL, 4)), (idn, A("dm", d0, d0 + 192)), (idb, A("one", 0, 192))])
+            mm(P(2 - 2 * (b % 2) + c // 2, 192 * (c % 2), 192 * (c % 2) + 192), [(idb, A("b", BL * b + c, BL * b + BL, 4))])
 
     def last(b):
-        win = A("w", BL * b, NW)
+        win = A("w", BL * b, WZ)
         for c in OPT["turn"]:
-            o = 48 * c + 12 * b
-            act(A("h1", 192 * c, 192 * c + 192), G(win, A("nl", o, o + 12)))
-            tt(A("p2", 192 * c, 192 * c + 192), G(win, A("nl", 144 + o, 156 + o)), A("bh", BL * b + c, BL * b + BL, 4), ALU.mult)
-        done = []
-        for j, cs in enumerate(((0, 1), (2,))):
-            how, bank, lo, k = OPT["last"][b][j], 2 - 2 * (b % 2) + j, 192 * cs[0], 192 * len(cs)
-            out = P(4 + j if how == "P" else bank, 0, k)
+            o = 96 * c + 12 * b
+            act(A("h1", 192 * c, 192 * c + 192), G(win, A("nl", 48 + o, 60 + o)))
+            tt(A("p2", 192 * c, 192 * c + 192), G(win, A("nl", o, o + 12)), A("ah", BL * b + c, BL * b + BL, 4), ALU.mult)
+        done, hows = [], OPT["last"][b]
+        for cs in ((0, 1), (2,)) if hows[:2] == "MM" else ((2,), (1,), (0,)):
+            how, k = hows[cs[0]], 192 * len(cs)
+            lo = 192 * cs[0]
+            factor = P(2 - 2 * (b % 2) + cs[0] // 2, lo % 384, lo % 384 + k)
+            out = P(3 + cs[0], 0, k) if how == "P" else factor
             if how == "P":
                 mm(out, [(idb, A("zz", 0, k))], True, False)
-            for x, y in [(0, k)] if how != "B" else [(192 * i, 192 * i + 192) for i in range(len(cs))]:
-                tt(P(4 + j if how == "P" else bank, x, y), P(bank, x, y), A("h1", lo + x, lo + y), ALU.mult)
+            tt(out, factor, A("h1", lo, lo + k), ALU.mult)
             if how == "P":
                 mm(out, [(idf, A("p2", lo, lo + k))], False)
-            done += [(how, c, P(4 + j if how == "P" else bank, 192 * i, 192 * i + 192)) for i, c in enumerate(cs)]
+            done += [(how, c, A("ps", out["reg"][0][1] + 192 * i, out["reg"][0][1] + 192 * i + 192)) for i, c in enumerate(cs)]
         for how, c, x in done:
             o = A("w", BL * b + c, BL * b + BL, 4)
             if how == "P":
@@ -709,7 +740,7 @@ def build(T, topo, core):
                 tt(o, x, A("p2", 192 * c, 192 * c + 192), ALU.add)
 
     def correct(t, b):
-        win = A("w", BL * b, NW)
+        win = A("w", BL * b, WZ)
         m = 128 if b == 0 and t < 2 else 192
         hows = OPT["corr"][t][b]
         k = m * (t + 1)
@@ -717,15 +748,13 @@ def build(T, topo, core):
         work = []
         for c in range(t + 1):
             lo, hi = BL * b + c, BL * b + 4 * m
-            l0 = A("nl", 48 * c + 12 * b, 48 * c + 12 * b + m // 16)
-            l1 = A("nl", 144 + 48 * c + 12 * b, 144 + 48 * c + 12 * b + m // 16)
+            l0 = A("nl", 96 * c + 12 * b, 96 * c + 12 * b + m // 16)
+            l1 = A("nl", 48 + 96 * c + 12 * b, 48 + 96 * c + 12 * b + m // 16)
             h1, p2 = (A(x, m * c, m * c + m) for x in ("h1", "p2"))
             pa = A("ps", i0 + m * c, i0 + m * c + m)
-            d0 = BL * c + 192 * b
-            if t < 2:
-                mm(pa, [(id256, A("ah", lo, hi, 4)), (idn, A("dm", d0, d0 + m)), (idb, A("one", 0, m))])
-            act(h1, G(win, l0))
-            tt(p2, G(win, l1), A("bh", lo, hi, 4), ALU.mult)
+            mm(pa, [(idb, A("b", lo, hi, 4))])
+            act(h1, G(win, l1))
+            tt(p2, G(win, l0), A("ah", lo, hi, 4), ALU.mult)
             work.append((hows[c], A("w", lo, hi, 4), pa, h1, p2))
         both = A("ps", i0, i0 + k)
         if t < 2 and b == 0:
@@ -757,7 +786,7 @@ def build(T, topo, core):
         for j, c in enumerate(OPT["sums"]):
             act(A("oh", c, BL, 4), P(6 + j // 2, 192 * (j % 2), 192 * (j % 2) + 192), scale=0.125)
         copy({"ap": T.yw[:], "reg": [("yw", 0, 512, 1)]}, A("ow", 0, 512), 2048)
-        copy(yh, A("oh", 0, BL), 3072)
+        copy(yh, A("oh", 0, BL), 3072, OPT["store"])
 
     lists(0)
     prefill(0)
@@ -818,7 +847,7 @@ def depend(ops):
                     if lo // 512 <= (hi2 - 1) // 512 and lo2 // 512 <= (hi - 1) // 512:
                         wait.add(i)
                 elif lo < hi2 and lo2 < hi and (wr or wr2) and (lo - lo2) % math.gcd(st, st2) == 0:
-                    wait.add(i)
+                    (order if same and op.get("adds") else wait).add(i)
                 elif name == "ps" and op["eng"] == "p" and lo // 512 == lo2 // 512:
                     order.add(i)
         for (name, lo, hi, st), wr in acc:
@@ -892,7 +921,7 @@ def place(eng, dur, pred, succ, pri, rel):
     return start
 
 
-def schedule(ops):
+def schedule(ops, rng):
     n = len(ops)
     pred = graph(ops)
     succ = [{} for _ in range(n)]
@@ -904,7 +933,6 @@ def schedule(ops):
     chain = [0.0] * n
     for j in range(n - 1, -1, -1):
         chain[j] = dur[j] + max([chain[s] + d for s, d in succ[j].items()] + [tail[j]])
-    rng = numpy.random.default_rng(OPT["seed"])
     seeds = [[chain[j] - (x if ops[j]["fill"] else 0.0) for j in range(n)] for x in OPT["later"]]
     main = [j for j in range(n) if not ops[j]["fill"]]
     start = anneal(eng, dur, pred, succ, [0.0] * n, tail, seeds, main, OPT["passes"], OPT["pull"], OPT["warm"], rng)
@@ -995,6 +1023,136 @@ def anneal(eng, dur, pred, succ, zero, tail, seeds, main, passes, pull, warm, rn
     return best[1]
 
 
+def steady(eng, cases, start, rng, rounds):
+    n, many = len(eng), range(len(cases))
+    seq = sorted(range(n), key=lambda j: (start[j], j))
+    into = [[[(i, d + dur[i]) for i, d in p.items()] for p in pred] for dur, pred, tail in cases]
+    out = [[[] for _ in range(n)] for _ in cases]
+    for c in many:
+        for j in range(n):
+            for i, d in cases[c][1][j].items():
+                out[c][i].append((j, d))
+    pred0, succ0 = cases[0][1], [[j for j, d in x] for x in out[0]]
+    first, wide, steps, pull = [], OPT["part"], OPT["steps"], OPT["mean"] / n
+
+    def links(part):
+        before, last = {}, {}
+        for j in part:
+            before[j] = last.get(eng[j], -1)
+            last[eng[j]] = j
+        return before
+
+    def times(c, part, before, old=None, lo=0):
+        dur, rel, end, edges = sets[c]
+        head, best = (dict(old[1]), old[3][:lo + 1]) if old else ({}, [(0.0, -1)])
+        last, at = best[-1]
+        for j in part[lo:]:
+            t = rel[j]
+            i = before[j]
+            if i >= 0:
+                x = head[i] + dur[i]
+                if x > t:
+                    t = x
+            for i, d in edges[j]:
+                x = head[i] + d
+                if x > t:
+                    t = x
+            head[j] = t
+            t += end[j]
+            if t > last:
+                last, at = t, j
+            best.append((last, at))
+        return last + pull * sum(head.values()), head, at, best
+
+    def queued(c, now, before):
+        dur, rel, end, edges = sets[c]
+        _, head, j, _ = now[c]
+        pairs = []
+        while head[j] > rel[j]:
+            by = [i for i, d in edges[j] if head[i] + d > head[j] - 1e-3]
+            if not by and before[j] not in pred0[j]:
+                pairs.append((before[j], j))
+            j = by[0] if by else before[j]
+        return pairs
+
+    for turn in range(rounds + 1):
+        heat = OPT["heat"] * (1.0 - turn / max(rounds, 1))
+        heads, frees, rests = [[0.0] * n for _ in many], [{} for _ in many], [[0.0] * n for _ in many]
+        for c in many:
+            (dur, pred, tail), rest, behind = cases[c], rests[c], {}
+            for j in reversed(seq):
+                rest[j] = behind[eng[j]] = dur[j] + max([rest[i] + d for i, d in out[c][j]] + [tail[j], behind.get(eng[j], 0.0)])
+        if turn == rounds:
+            return sum(math.log(max(rest)) for rest in rests), seq
+        done = 0
+        for lo in range(-int(rng.integers(wide // 2)), n - wide // 2, wide // 2):
+            lo, hi = max(lo, 0), min(lo + wide, n)
+            part, sets = seq[lo:hi], []
+            inside, then = set(part), {eng[j]: j for j in reversed(seq[hi:])}
+            for c in many:
+                (dur, pred, tail), head, free, rest = cases[c], heads[c], frees[c], rests[c]
+                for j in seq[done:lo]:
+                    head[j] = max([head[i] + d for i, d in into[c][j]] + [free.get(eng[j], 0.0)])
+                    free[eng[j]] = head[j] + dur[j]
+                rel = {j: max([head[i] + d for i, d in into[c][j] if i not in inside] + [free.get(eng[j], 0.0)]) for j in part}
+                end = {j: dur[j] + max([rest[i] + d for i, d in out[c][j] if i not in inside] + [tail[j], rest[then[eng[j]]] if eng[j] in then else 0.0])
+                       for j in part}
+                sets.append((dur, rel, end, {j: [(i, d) for i, d in into[c][j] if i in inside] for j in part}))
+            done = lo
+            before = links(part)
+            now = [times(c, part, before) for c in many]
+            first = first or [x[0] for x in now]
+            cur = sum(x[0] / f for x, f in zip(now, first))
+            best, pairs = (cur, part), [None] * len(cases)
+            for c, u, w, far, z in zip(rng.integers(len(cases), size=steps).tolist(), rng.random(steps).tolist(), rng.random(steps).tolist(),
+                                       rng.geometric(OPT["short"], steps).tolist(), rng.exponential(1.0, steps).tolist()):
+                if pairs[c] is None:
+                    pairs[c] = queued(c, now, before)
+                if not pairs[c]:
+                    continue
+                a, b = pairs[c][int(u * len(pairs[c]))]
+                ahead, y = w < 0.5, part.index(b)
+                for _ in range(far - 1):
+                    if ahead:
+                        a = before[a] if before[a] >= 0 else a
+                    else:
+                        y = next((k for k in range(y + 1, len(part)) if eng[part[k]] == eng[b]), y)
+                b, x = part[y], part.index(a)
+                mid, take = part[x:y + 1], {b if ahead else a}
+                for j in reversed(mid) if ahead else mid:
+                    if not take.isdisjoint(succ0[j] if ahead else pred0[j]):
+                        take.add(j)
+                if a in take and b in take:
+                    continue
+                new = part[:x] + [j for j in mid if (j in take) == ahead] + [j for j in mid if (j in take) != ahead] + part[y + 1:]
+                after = links(new)
+                one = times(c, new, after, now[c], x)
+                if (one[0] - now[c][0]) / first[c] > heat * z + OPT["give"]:
+                    continue
+                res = [one if k == c else times(k, new, after, now[k], x) for k in many]
+                x = sum(r[0] / f for r, f in zip(res, first))
+                if x <= cur + heat * z:
+                    part, before, now, cur, pairs = new, after, res, x, [None] * len(cases)
+                    if x < best[0]:
+                        best = (x, part)
+            seq[lo:hi] = best[1]
+
+
+def plan(ops, T, topo, core):
+    keep, cases = dict(COST), []
+    for case in CASES:
+        COST.update(case)
+        like = build(T, topo, core)
+        for o, p in zip(like, ops):
+            o["wait"], o["order"] = p["wait"], p["order"]
+        cases.append(([o["dur"] + 1e-3 for o in like], graph(like), [o.get("lat", 0.0) for o in like]))
+        COST.update(keep)
+    eng, rng = [o["eng"] for o in ops], numpy.random.default_rng(OPT["seed"])
+    seq = min(steady(eng, cases, schedule(ops, rng)[1], rng, OPT["rounds"][0]) for _ in range(OPT["starts"]))[1]
+    seq = steady(eng, cases, {j: k for k, j in enumerate(seq)}, rng, OPT["rounds"][1])[1]
+    return {j: k for k, j in enumerate(seq)}
+
+
 PLAN = {}
 
 
@@ -1004,8 +1162,9 @@ def rank_program(g, core, T, topo):
     ops = build(T, topo, core)
     depend(ops)
     if "order" not in PLAN:
-        PLAN["order"] = schedule(ops)
-    order, start, _ = PLAN["order"]
+        PLAN["order"] = plan(ops, T, topo, core)
+    start = PLAN["order"]
+    order = {e: sorted((j for j in start if ops[j]["eng"] == e), key=start.get) for e in "vspgy"}
     queue = {"v": g.vector, "s": g.scalar, "p": g.tensor, "g": g, "y": g.sync}
     total = {}
     for e in "vspg":
@@ -1043,5 +1202,7 @@ def rank_program(g, core, T, topo):
                 ins.then_inc(T.sem[op["sem"]], 1)
             elif op["kind"] == "dma":
                 ins.then_inc(T.sem[op["sem"]], 16)
-    for s in sorted(total):
-        g.wait_ge(T.sem[s], total[s])
+    done = {op["sem"]: start[j] for j, op in sorted(enumerate(ops), key=lambda x: start[x[0]])}
+    for s in sorted(total, key=done.get):
+        if known["g"].get(s, 0) < total[s]:
+            g.wait_ge(T.sem[s], total[s])

import math
import numpy
from concourse.bass import DstId, RemoteDMATransfer
from concourse.mybir import AluOpType, AxisListType, ActivationFunctionType

F32, BF, I32, U16 = "float32", "bfloat16", "int32", "uint16"
NV, NW, BL, K = 3072, 3584, 768, 1024
NZ = NV + 32
WZ = NW + 8
ZC = K
SPARE = K + 16
VO = SPARE + 256
UV = ("uv", "uv0", "uv", "uv0")
BIG = 2.0 ** 21
EDGE = NV - 0.5
HALF = 127.7 / 256


def _sb(n, d):
    return ("sbuf", [128, n], d)


SCRATCH = {
    "ps": ("psum", [128, 4096], F32),
    "a": _sb(NV, BF), "b": _sb(NZ, BF), "zz": _sb(NZ // 4, BF),
    "uv": _sb(2 * VO, BF), "uv0": _sb(2 * VO, BF), "uw": _sb(2 * VO, BF), "us": _sb(VO, BF),
    "md": _sb(72, BF), "id512": _sb(128, BF), "gs": _sb(384, F32), "gr": _sb(384, F32), "gl": _sb(1024, F32),
    "mqu": _sb(K, I32), "mqv": _sb(K, I32), "one": _sb(512, BF),
    "nab": _sb(384, I32), "sdi": _sb(192, I32), "pfi": _sb(64, I32), "thi": _sb(4, I32),
    "idm": _sb(128, BF), "idq": _sb(128, BF), "wz": _sb(144, BF),
    "ci": _sb(4, I32), "cf": _sb(24, F32), "cb": _sb(8, BF), "kr": _sb(272, BF), "r16": _sb(128, BF),
    "q1": _sb(144, BF), "wd": _sb(144, BF), "w0": _sb(144, BF), "w1": _sb(144, BF),
    "blk": _sb(128, BF), "blm": _sb(128, BF), "idb": _sb(128, BF), "idn": _sb(128, BF), "idh": _sb(128, BF), "id256": _sb(128, BF),
    "idk": _sb(128, BF), "id64": _sb(128, BF), "id32": _sb(128, BF), "idf": _sb(128, F32),
    "tri": _sb(128, BF), "tr4": _sb(128, BF), "st": _sb(256, BF), "su": _sb(256, BF),
    "i16": _sb(16, F32), "bm": _sb(16 * 144, BF),
    "kw": _sb(32, F32), "fw": _sb(16, F32), "sf0": _sb(96, F32), "sf": _sb(96, F32), "zc": _sb(96, F32), "nf": _sb(96, F32), "kt": _sb(K, BF), "jt": _sb(512, BF),
    "thf": _sb(8, F32), "shl": _sb(192, "float16"), "dhl": _sb(768, BF),
    "nnd": _sb(NZ, BF), "ah": _sb(NZ, BF), "dm": _sb(BL, BF),
    "sdf": _sb(384, F32), "si": _sb(192, BF), "sl": _sb(624, U16),
    "dd": _sb(BL, F32), "xs": _sb(BL, BF), "c1": _sb(BL, BF), "c2": _sb(BL, BF),
    "ff": _sb(128, F32), "fu": _sb(64, U16), "sg": _sb(64, F32), "t2": _sb(64, F32),
    "ga": _sb(K, BF), "gb": _sb(K, BF), "gg": _sb(2 * K, BF),
    "on": _sb(64, BF), "sc": _sb(80, BF), "cc": _sb(64, F32), "fc": _sb(64, F32),
    "sk": _sb(K, F32), "ek": _sb(16, F32), "rr": _sb(16, BF), "cu": _sb(16, U16), "ro": _sb(4, U16), "hs": _sb(272, F32),
    "le": _sb(256, BF), "eq": _sb(256, BF), "atu": _sb(16, U16), "asu": _sb(16, U16),
    "e1": _sb(16, F32), "e2": _sb(16, F32), "e3": _sb(16, F32),
    "cin": _sb(60, F32), "mm": _sb(12, F32), "lv": _sb(64, F32), "fk": _sb(64, F32), "fl": _sb(64, F32),
    "snd": _sb(768, BF), "rcv": _sb(3 * 768, BF), "ru": _sb(6 * K, BF), "ra": _sb(48, U16),
    "w": _sb(WZ, F32), "x": _sb(NV, BF),
    "nl": _sb(6 * 48, U16), "h1": _sb(3 * 192, F32), "p2": _sb(3 * 192, F32),
    "zt": _sb(K + 16, F32), "sig": _sb(VO, F32), "sa": _sb(512, F32), "pa": _sb(512, F32), "hb": _sb(512, F32),
    "oh": _sb(BL, F32), "ow": _sb(512, F32),
}
SEMAPHORES = ["cv", "cs", "cp", "cg"] + ["d%d" % i for i in range(48)] + ["l%d" % i for i in range(32)] + ["r%d" % i for i in range(32)]
COUNTER = {"v": "cv", "s": "cs", "p": "cp", "g": "cg"}

SLOW = {"remote": 2600.0, "rows": 1200.0, "rissue": 1300.0, "gissue": 1300.0, "glat": 4000.0, "lat": 160.0, "own": 160.0, "once": 2500.0}
FAST = {"remote": 1300.0, "rows": 500.0, "rissue": 600.0, "gissue": 600.0, "glat": 2400.0, "lat": 80.0, "own": 80.0}
CASES = [{"cyc": 0.85}, {"cyc": 1.2, "gat": 1.2, "sca": 2.5}, {"cyc": 1.05, "gat": 2.0, "sca": 5.5},
         dict(SLOW, cyc=1.0, gat=1.3, sca=4.5), dict(FAST, cyc=1.1, gat=1.8, sca=2.0)]
COST = {"cyc": 1.0, "pe": 0.52, "mm": 3.0, "gat": 1.55, "sca": 3.8, "fix": 60.0, "lat": 120.0, "own": 120.0, "remote": 1800.0, "rows": 800.0, "link": 1.4, "rissue": 900.0,
        "gissue": 900.0, "glat": 3000.0, "drow": 100.0, "issue": 60.0, "once": 1000.0}
OPT = {
    "corr": [["M"] * 4, ["MM"] * 4, ["BBB"] * 4], "cmp": "VVV",
    "hop": ["SWSW", "SWSW", "SSSW"],
    "apart": [(1, 0), (1, 0), (1, 0)],
    "inturn": 1, "share": "", "fold": 0.0, "store": "s",
    "stag": [(("m2", 0, 1), ("vn", 0, 0)), (("m2", 1, 1), ("vn", 1, 0))],
    "early": ["u", "u", "u"], "parts": ["uvf", "uvf", "uvf"], "accs": [4, 4, 4], "last": ["MMM", "MMP", "MMP", "MMP"], "turn": (0, 1, 2), "sums": (3, 0, 1, 2), "rest": 2,
    "cuts": [(256, 512, 768), (256, 512, 768), (256, 768)], "dcuts": [(4, 2, 0), (4, 2, 0)],
    "loads": [("sd", "y"), ("u", "s"), ("a0", "y"), ("a1", "s"), ("th", "y"), ("b", "y"), ("na", "y"), ("nb", "y"), ("pf", "y"), ("v", "y"),
              (0, "s"), (1, "s"), (2, "y"), (3, "y")],
    "zeros": {"ah": "g"}, "direct": [(), (), ()],
    "xparts": [2, 2], "x0": "VV", "xs": ["VS", "VS"], "xc": ["SSSS", "SSSS"], "gr": "S", "us": "SS",
    "xl": ["DD", "DD", "VV", "VV"], "pre3": [1, 1, 0], "dead": "SS", "oh": "P", "sv": "S", "su": "S", "bm0": "VSVS",
    "starts": 5, "rounds": (3, 26), "part": 100, "steps": 400, "heat": 0.002, "give": 0.001, "mean": 0.5, "short": 0.5,
    "sweeps": 2, "wide": 24000.0, "tries": 300, "near": 0.5, "cool": 100.0,
    "aim": 0.85, "reach": 2000.0, "every": 10, "passes": 2500, "noise": 4000.0, "span": 10000.0, "later": [0.0, 5e3, 1e4, 2e4, 4e4, 1e6], "seed": 1, "pull": 3.0, "warm": 250.0}


def build(T, topo, core):
    ALU, ACT = AluOpType, ActivationFunctionType
    ops = []
    fill = [False]
    rank = T.rank_of(core)
    n = len(T.cores)
    cy = COST["cyc"]

    def A(name, lo, hi, step=1):
        ap = T[name][:, lo:hi] if step == 1 else T[name][:, lo:hi:step]
        return {"ap": ap, "reg": [(name, lo, hi, step)], "n": (hi - lo + step - 1) // step, "d": SCRATCH[name][2], "ps": name == "ps", "ind": False}

    def P(bank, lo, hi):
        return A("ps", 512 * bank + lo, 512 * bank + hi)

    def G(win, off):
        return {"ap": win["ap"].indirect(off["ap"]), "reg": win["reg"], "oreg": off["reg"], "n": 16 * off["n"], "d": win["d"], "ps": False, "ind": True}

    def add(eng, fn, dur, rd, wr, **kw):
        r, w = [], []
        for x in rd:
            if isinstance(x, dict):
                r += x["reg"] + x.get("oreg", [])
        for x in wr:
            w += x["reg"]
            r += x.get("oreg", [])
        op = {"eng": eng, "fn": fn, "dur": dur * COST.get(eng, 1.0), "rd": r, "wr": w, "kind": "c", "fill": fill[0]}
        op.update(kw)
        ops.append(op)
        return len(ops) - 1

    def ap(x):
        return x["ap"] if isinstance(x, dict) else x

    def vcost(out, ins, two=False):
        m = out["n"]
        if out["ind"]:
            c = COST["sca"]
        elif ins[0]["ind"]:
            c = COST["gat"]
        elif two:
            c = 1.0 if any(x["ps"] for x in ins) else 2.0
        else:
            c = 0.5 if all(x["d"] in (BF, U16) for x in ins + [out]) else 1.0
        return COST["fix"] + max(64, m * c) * cy

    def tt(out, i0, i1, op):
        add("v", lambda q: q.tensor_tensor(out["ap"], i0["ap"], i1["ap"], op), vcost(out, [i0, i1], True), [i0, i1], [out])

    def ts(out, i0, s1, op0, s2=None, op1=None):
        if op1 is None:
            fn = lambda q: q.tensor_scalar(out["ap"], i0["ap"], ap(s1), None, op0)
        else:
            fn = lambda q: q.tensor_scalar(out["ap"], i0["ap"], ap(s1), ap(s2), op0, op1)
        add("v", fn, vcost(out, [i0]), [i0, s1, s2], [out])

    def cp(out, i0):
        add("v", lambda q: q.tensor_copy(out["ap"], i0["ap"]), vcost(out, [i0]), [i0], [out])

    def ms(out, val):
        add("v", lambda q: q.memset(out["ap"], val), vcost(out, [out]), [], [out])

    def scan(out, d0, d1, first, op0, op1):
        add("v", lambda q: q.tensor_tensor_scan(out["ap"], d0["ap"], d1["ap"], ap(first), op0, op1), vcost(out, [d0, d1]), [d0, d1, first], [out])

    def act(out, i0, func=None, bias=0.0, scale=1.0, extra=0.0, acc=None):
        f = ACT.Identity if func is None else func
        c = COST["gat"] if i0["ind"] else 1.0
        more = {"accum_out": acc["ap"]} if acc else {}
        add("s", lambda q: q.activation(out["ap"], i0["ap"], f, bias=ap(bias), scale=ap(scale), **more),
            COST["fix"] + extra + (20.0 if acc else 0.0) + max(64, i0["n"] * c) * cy, [i0, bias, scale], [out] + ([acc] if acc else []))

    def lin(how, out, i0, bias=0.0, scale=1.0):
        if how == "S":
            act(out, i0, bias=bias, scale=scale)
        elif bias == 0.0 and scale == 1.0:
            cp(out, i0)
        else:
            ts(out, i0, scale, ALU.mult, bias, ALU.add)

    def mms(items):
        def fn(q):
            last = None
            for o, l, r, a, z in items:
                last = q.matmul(o["ap"], l["ap"], r["ap"], a, z)
            return last
        dur = 30.0 + sum(COST["mm"] + max(64, r["n"]) * (4 if r["d"] == F32 else 1) * COST["pe"] * cy for o, l, r, a, z in items)
        add("p", fn, dur, [x for it in items for x in it[1:3]], [it[0] for it in items], adds=not items[0][3])

    def mm(out, pairs, start=True, stop=True):
        mms([(out, l, r, start and j == 0, stop and j == len(pairs) - 1) for j, (l, r) in enumerate(pairs)])

    line = [None]

    def gp(fn, dur, rd, out):
        j = add("g", fn, dur, rd, [out])
        if line[0] is not None:
            ops[j]["follow"] = line[0]
        line[0] = j

    def iota(out, pattern, base, cm):
        if out["d"] == I32:
            fn = lambda q: q.iota(out["ap"], pattern, base, cm)
        else:
            fn = lambda q: q.iota(out["ap"], pattern, base, cm, allow_small_or_imprecise_dtypes=True)
        gp(fn, 130.0 + 2 * out["n"] * cy, [], out)

    def pick(out, i0, test, other, base, sign):
        gp(lambda q: q.affine_select(out["ap"], i0["ap"], [[sign, out["n"]]], test, other, base, -sign), 170.0 + 2 * out["n"] * cy, [i0], out)

    def diag(name, c):
        pick(A(name, 0, 128), A("zz", 0, 128), ALU.not_equal, c, 0, 1)

    nd, nr, bus, used = [0], [0], {"busy": 0.0}, set()

    def sem():
        nd[0] += 1
        return "d%d" % (nd[0] - 1)

    def load(queue, dst, src, nbytes):
        bus["busy"] += nbytes * 0.22 + COST["drow"]
        before = bus.get(queue, [])
        j = add(queue, lambda q: q.dma_start(dst["ap"], src), COST["issue"], [], [dst], kind="dma", sem=sem(), cnt=16,
                lat=1700.0 + bus["busy"] - COST["issue"] * len(before))
        if before:
            ops[j]["follow"] = before[-1]
        bus[queue] = before + [j]

    def copy(dst, src, nbytes, queue="y"):
        add(queue, lambda q: q.dma_start(dst["ap"], src["ap"]), 60.0, [src], [dst], kind="dma", sem=sem(), cnt=16, lat=1900.0 + nbytes * 0.22,
            lead=1500.0)
        share(dst, nbytes * 0.22)

    def share(dst, busy):
        j = len(ops) - 1
        for x in OPT["share"]:
            add(x, None, 400.0 + busy, [], [dst], kind="recv", sem=ops[j]["sem"], cnt=16, after=j, lat=0.0)

    def dadd(dst, src):
        add("g", lambda q: q.dma_start(dst["ap"], src["ap"], accum_op=ALU.add), COST["gissue"], [src, dst], [dst], kind="dma", sem=sem(), cnt=16,
            lat=COST["glat"] + dst["n"] * 4 * 0.3, lead=COST["glat"] - 900.0)
        share(dst, 500.0 + dst["n"] * 4 * 0.3)

    def engines(a, b, wide=False):
        far = -1
        for c in T.cores:
            if c != a:
                far &= topo.mask(a, c)
        return topo.mask(a, b) if wide else (topo.mask(a, b) & ~far) or far

    def send(src, dsts, froms, lands, nbytes, lane, twice=False):
        ls, rs = "l%d" % nr[0], "r%d" % nr[0]
        nr[0] += 1
        masks = sorted({engines(core, c) for c, _ in dsts})

        def fn(q):
            if len(dsts) == 1 and not twice:
                rid, pid, _ = topo.addr(dsts[0][0])
                return q.remote_dma(dsts[0][1]["ap"], src["ap"], T.sem[rs], T.sem[ls], pid, rid, masks[0])
            trs = []
            for m in masks:
                to = [(c, d) for c, d in dsts if engines(core, c) == m]
                trs.append(RemoteDMATransfer(dst_ids=[DstId(rid=topo.addr(c)[0], pnc=topo.addr(c)[1]) for c, _ in to], dma_engine_mask=m, remote_sem=T.sem[rs],
                                             srcs=[src["ap"]] * (2 if twice else 1), dsts=[d["ap"] for _, d in to], alu_op=1 if twice else 0))
            return q.remote_dma_fused(trs, local_sem=T.sem[ls])
        rows = COST["rows"] * min(len(dsts), 2) + nbytes * COST["link"] * (1 + twice * OPT["fold"])
        left = sum(bin(m).count("1") for m in masks)
        new = COST["once"] * (lane not in used)
        used.add(lane)
        j = add("g", fn, COST["rissue"] + new, [src], [], kind="send", sem=ls, cnt=left, lat=COST["remote"] + rows + new, lead=COST["remote"] + new)
        for x in lane:
            add(x, None, rows, [], lands, kind="recv", sem=rs, cnt=sum(bin(engines(c, core)).count("1") for c in froms), after=j, lat=0.0)

    nxt, prv = T.cores[(rank + 1) % n], T.cores[(rank - 1) % n]

    def sh(name, i, base=0):
        return A(name, base + 15 - i, base + 143 - i)

    def wrap(out, mat, src, lo, hi, start=True):
        mm(out, [(sh(mat, i), A(src, lo + i, hi, 16)) for i in range(16)], start)

    inputs = {"sd": (A("sdi", 0, 192), T.sd[:], 768), "u": (A("uv", 0, K), T.u0[:], 2048), "th": (A("thi", 0, 3), T.th[:], 12),
              "a0": (A("a", 0, 1536), T.ta[:, 0:1536], 3072), "a1": (A("a", 1536, NV), T.ta[:, 1536:NV], 3072), "a": (A("a", 0, NV), T.ta[:], 6144),
              "na": (A("nab", 0, 192), T.na[:], 768), "nb": (A("nab", 192, 384), T.nb[:], 768), "pf": (A("pfi", 0, 64), T.pf[:], 256),
              "v": (A("uv", VO, VO + K), T.v0[:], 2048), "b": (A("b", 0, NV), T.tb[:], 6144)}
    zz = A("zz", 0, NZ // 4)
    for name, queue in OPT["loads"]:
        if name in inputs:
            load(queue, *inputs[name])
        else:
            if name == 0:
                ms(zz, 0.0)
            load(queue, A("nnd", name * NZ // 4, (name + 1) * NZ // 4), zz["ap"], NZ // 2)
            ops[-1]["rd"] = zz["reg"]
    landed = [("landed", 0, 1, 1)]
    ops[-1]["wr"] = ops[-1]["wr"] + landed

    iota(A("ci", 0, 1), [[0, 1]], 0, 1)
    iota(A("kr", 0, 272), [[1, 272]], 0, 0)
    iota(A("r16", 0, 128), [[16, 8], [0, 16]], 0, 0)
    ts(A("ci", 1, 2), A("ci", 0, 1), 15, ALU.bitwise_and)
    ts(A("ci", 2, 3), A("ci", 0, 1), 112, ALU.bitwise_and)
    cp(A("cf", 0, 3), A("ci", 0, 3))
    col = lambda i: A("cf", i, i + 1)
    pc, lane, g16 = col(0), col(1), col(2)
    q1 = A("q1", 0, 144)
    ts(q1, A("kr", 0, 144), -15.0, ALU.add, g16, ALU.is_equal)
    ts(A("i16", 0, 16), A("kr", 0, 16), lane, ALU.is_equal, 0.5, ALU.mult)
    for q in range(4):
        if OPT["bm0"][q] == "V":
            ts(A("bm", 576 * q, 576 * q + 144), q1, A("i16", 4 * q, 4 * q + 1), ALU.mult)
        else:
            act(A("bm", 576 * q, 576 * q + 144), q1, scale=A("i16", 4 * q, 4 * q + 1))
    idb, idf, idn, idh, idk, id256, blk = (A(x, 0, 128) for x in ("idb", "idf", "idn", "idh", "idk", "id256", "blk"))
    ts(blk, A("r16", 0, 128), g16, ALU.is_equal)
    ts(idb, A("kr", 0, 128), pc, ALU.is_equal)
    act(id256, idb, scale=1.0 / 256)
    for name, how in OPT["zeros"].items():
        if how == "g":
            for c in range(1, 4):
                iota(A(name, c, NV, 4), [[0, BL]], 0, 0)
            ms(A(name, NV, NZ), 0.0)
        else:
            for c in range(1, 4):
                ms(A(name, c, NV, 4), 0.0)
            ms(A(name, NV, NZ), 0.0)
        if name == "ah":
            diag("idq", -2048.0)
            diag("idn", -1.0)
    ms(A("b", NV, NZ), 0.0)
    diag("idm", 256.0)
    act(idf, idb)
    low = A("cb", 0, 1)
    act(low, lane, ACT.Sigmoid, bias=7.5 * 512, scale=-512.0, extra=1300.0)
    table = len(ops) - 1
    act(col(5), low, bias=-1.0, scale=2.0)
    act(A("wd", 0, 144), q1, scale=col(5))
    ms(A("ff", 0, 32), 0.0)
    ms(A("ff", 96, 128), 0.0)
    if "V" in OPT["cmp"]:
        cp(A("thf", 0, 3), A("thi", 0, 3))
    if "S" in OPT["cmp"]:
        ts(A("thf", 4, 7), A("thi", 0, 3), 0.5, ALU.add)

    cp(A("shl", 0, 192), A("sdi", 0, 192))
    act(col(7), lane, bias=-4112.5)
    act(P(7, 0, 192), A("kr", 0, 192), bias=col(7), scale=16.0)
    tt(A("cf", 9, 11), A("i16", 0, 2), A("i16", 8, 10), ALU.add)
    act(col(9), col(9), bias=-2048.0, scale=-4128.0)
    act(col(8), col(10), bias=col(9), scale=15.5)
    for j in range(2):
        tt(P(6, 192 * j, 192 * j + 192), A("nab", 192 * j, 192 * j + 192), P(7, 0, 192), ALU.subtract)
    act(A("dhl", 0, 384), P(6, 0, 384))
    tt(A("dhl", 384, 768), P(6, 0, 384), A("dhl", 0, 384), ALU.subtract)
    ts(A("ff", 32, 96), A("pfi", 0, 64), -EDGE, ALU.add)
    ts(A("fu", 0, 64), A("pfi", 0, 64), float(NV), ALU.min)

    fill[0] = True
    iota(A("kt", 0, K), [[2048, 16], [0, 64]], 0, 0)
    iota(A("jt", 0, 512), [[0, 8], [1, 64]], 0, 0)
    pick(A("tri", 0, 128), blk, ALU.is_ge, 0.0, 0, 1)
    pick(A("tr4", 0, 128), A("tri", 0, 128), ALU.not_equal, -4096.0, 0, 1)
    pick(A("w0", 0, 144), q1, ALU.is_ge, 0.0, -8, 1)
    pick(A("w1", 0, 144), q1, ALU.is_ge, 0.0, 7, -1)
    act(A("wz", 0, 144), q1, scale=64.0)
    iota(A("sf0", 0, 96), [[1024, 2], [0, 4], [32, 12]], 0, 0)
    iota(A("zc", 0, 96), [[NW // 2 - 4096, 2], [-BL // 2, 4], [0, 12]], 4096, 0)
    diag("idk", 4096.0)
    iota(A("one", 0, 512), [[0, 512]], 1, 0)
    line[0] = add("g", lambda q: q.dma_start(T.w[:, 0:NV], T.h0[:]), COST["gissue"] + COST["once"], [{"reg": landed}], [A("w", 0, NV)], kind="dma", sem=sem(),
                  cnt=16, lat=COST["glat"] + NV * 4 * 0.22, follow=line[0])
    pick(A("su", 128, 256), sh("q1", 0), ALU.is_equal, 0.0, 0, 1)
    pick(A("su", 0, 128), blk, ALU.is_equal, 0.0, -1, 1)
    pick(A("su", 0, 128), A("su", 0, 128), ALU.not_equal, -1.0, 0, 1)
    for name, c in (("id512", -512.0), ("id64", -64.0), ("id32", -32.0), ("idh", -0.5)):
        diag(name, c)
    for i in range(16):
        if i % 4:
            act(A("bm", 144 * i, 144 * i + 144), q1, scale=A("i16", i, i + 1))
    act(A("st", 0, 256), A("su", 0, 256), scale=BIG)
    act(A("blm", 0, 128), blk, scale=-128.0)
    act(col(6), lane, scale=2.0)
    act(A("sf", 0, 96), A("sf0", 0, 96), bias=col(6))
    ms(A("w", NW, WZ), 0.0)
    act(A("fw", 0, 16), A("kr", 0, 16), bias=lane, scale=16.0)
    act(A("kw", 0, 16), A("fw", 0, 16), bias=0.5)
    act(A("kw", 16, 32), A("fw", 0, 16), bias=SPARE - 1008.0)
    act(col(11), lane, bias=128.0, scale=128.0)
    act(A("kt", 0, K), A("kt", 0, K), bias=col(11))
    act(col(12), A("i16", 0, 1), bias=BIG - 256.0 + EDGE, scale=-2.0 * BIG)
    ms(A("sc", 15, 16), 0.0)
    for name in ("uv0", "uv"):
        ms(A(name, ZC, SPARE), 0.5)
    ms(A("us", ZC, SPARE), 0.0)
    ms(A("cin", 16, 60, 20), 256.0)
    ms(A("hs", 0, 1), 0.0)
    fill[0] = False

    def lists(t):
        o = P(4, 0, 48) if t == 0 else P(7, 0, 48)
        mm(o, [(sh("bm", i, 144 * (4 * (i % 4) + t)), A("shl", i // 4, 192, 4)) for i in range(16)])
        if t == 0:
            ts(A("sl", 576, 624), o, 2.0, ALU.mult)
        act(A("sdf", 48 * t, 48 * t + 48), o, scale=2.0)

    fill[0] = True
    cp(A("sdf", 192, 384), A("sdi", 0, 192))
    send(A("w", 0, 512), [(prv, A("w", NV, NW))], [nxt], [A("w", NV, NW)], 2048, "k", True)
    ghosted = len(ops) - 2
    fill[0] = False

    def prefill(t, banks=(0, 1, 2, 3)):
        for bank in banks:
            c = bank % 2
            mm(P(bank, 0, 384), [(id256, A("ab"[bank // 2], 1536 * c + t, 1536 * c + 1536, 4))])
        for c in range(2 * (0 in banks)):
            if t > 0 and c in OPT["direct"][t]:
                act(A("xs", 384 * c, 384 * c + 384), A("a", 1536 * c + t, 1536 * c + 1536, 4), bias=0.5, scale=1.0 / 256)

    def rows(t):
        for q in range(4):
            i = 4 * q + t
            mm(rowsof(q), [(sh("bm", l, 144 * i), A("dhl", c0, c0 + 192)) for l, c0 in ((0, 0), (1, 384), (8, 192), (9, 576))], q % 2 == 0, False)

    def rowsof(q):
        return P(6 + q // 2, 192 * (q % 2), 192 * (q % 2) + 192)

    def collapse(t):
        for c in range(2):
            lo, hi = 384 * c, 384 * c + 384
            cls = lambda name: A(name, 4 * lo + t, 4 * hi, 4)
            c1, c2, d, dm = A("c1", lo, hi), A("c2", lo, hi), P(4 + c, 128, 512), A("dm", lo, hi)
            if t == 0:
                off = A("sl", 576 + 24 * c, 600 + 24 * c)
                if OPT["x0"][c] == "V":
                    tt(A("dd", lo, hi), G(A(UV[0], 0, K), off), cls("a"), ALU.subtract)
                    act(c2, A("dd", lo, hi), ACT.Abs, bias=-128.0)
                    ops[-1]["follow"] = table
                else:
                    act(A("xs", lo, hi), G(A(UV[0], 0, K), off), bias=-128.0)
                    mm(d, [(idb, cls("a"))], True, False)
                    mm(d, [(idn, A("xs", lo, hi))], False)
                    act(c2, d, ACT.Abs)
            else:
                o = 192 * (t - 1) + 48 * t + 24 * c
                lin(OPT["xs"][t - 1][c], cls("x"), G(A(UV[t], 0, K), A("sl", o, o + 24)), bias=-2.0 ** t, scale=2.0 ** (t + 1))
                if c in OPT["direct"][t]:
                    ops[-1]["fill"] = True
                    tt(A("dd", lo, hi), G(A(UV[t], 0, K), A("sl", o, o + 24)), A("xs", lo, hi), ALU.subtract)
                    act(c2, A("dd", lo, hi), ACT.Abs, scale=256.0)
                else:
                    mm(d, [(idb, cls("a"))], True, False)
                    mm(d, [(A("id64" if t == 1 else "id32", 0, 128), cls("x"))], False)
                    act(c2, d, ACT.Abs)
            if OPT["cmp"][t] == "V":
                ts(c1, c2, A("thf", t, t + 1), ALU.is_le)
            else:
                act(c1, c2, ACT.Sign, bias=A("thf", 4 + t, 5 + t), scale=-1.0)
            thr = 8.5 if OPT["cmp"][t] == "V" else 1.0
            mm(d, [(blk, c1)])
            act(dm, d, ACT.Sign, bias=thr, scale=-1.0)
            tt(cls("ah"), P(c, 0, 384), dm, ALU.max)
            tt(cls("b"), P(2 + c, 0, 384), dm, ALU.max)
        for q in range(4):
            mm(rowsof(q), [(A("idq", 0, 128), A("dm", q, BL, 4))], False, q % 2 == 1)
        for q in range(4):
            act(A("nnd", 4 * q + t, NV, 16), rowsof(q), ACT.Relu, bias=col(8))

    marks = {}

    def hop(t, k, c):
        lo, hi = 512 * c, 512 * c + 512
        off = A("fu", 32 * c, 32 * c + 32)
        gn, ge = A("gg", 512 + lo, 512 + hi), A("gg", 3 * lo, 3 * lo + 512)
        pa, pb, pv = P(2 * c, 0, 512), P(2 * c + 1, 0, 512), P(4 + c, 0, 512)
        ga, gb, mqu, mqv = (A(x, lo, hi) for x in ("ga", "gb", "mqu", "mqv"))
        src, dst = (UV[t], "uw") if k == 0 else ("uw", UV[t + 1])
        ub, vb = A(src, lo, hi), A(src, VO + lo, VO + hi)
        un, vn = A(dst, lo, hi), A(dst, VO + lo, VO + hi)
        end = t == 2 and k == 1
        how = OPT["hop"][t][2 * k + c]
        first = t == 0 and k == 0
        unit = id256 if first else idb

        def mark(name):
            marks[name, k, c] = len(ops) - 1
            for late, early in OPT["stag"]:
                if late == (name, k, c) and early in marks:
                    ops[-1]["follow"] = marks[early]
        act(ga, G(A("ah", 0, NZ), off))
        act(gb, G(A("b", 0, NZ), off), scale=256.0)
        act(gn, G(A("nnd", 0, NZ), off))
        f = A("ff", 32 * c + 32, 32 * c + 64)
        wb = 4 + c
        pm, pn = P(wb, 32 - 32 * c, 64 - 32 * c), P(wb, 32 * c, 32 * c + 32)
        mm(pv, [(idb if first else A("idm", 0, 128), vb)])
        mm(pa, [(idb, A("zz", 0, 512))], True, False)
        mm(pb, [(idb, A("zz", 0, 512))], True, False)
        tt(pa, pv, ga, ALU.mult)
        mark("m1")
        apart = OPT["apart"][t][k]
        if apart:
            wrap(P(wb, 64 + 32 * c, 96 + 32 * c), "wd", "gg", 512 + lo, 512 + hi)
        elif c == 1:
            wrap(P(5, 64, 128), "wd", "gg", 512, 1536)
        mm(pa, [(unit, ub)], False)
        tt(pb, pa, gb, ALU.mult)
        mark("m2")
        mm(pb, [(unit, vb)], False)
        ts(mqu, pa, -HALF, ALU.add)
        mark("qu")
        if how == "V":
            tt(pa, pa, mqu, ALU.subtract)
            act(un, pa)
        else:
            tt(un, pa, mqu, ALU.subtract)
        if end:
            lin(OPT["us"][c], A("us", lo, hi), un, bias=-8.0, scale=16.0)
        if k == 1 and "u" in OPT["early"][t]:
            ru = A("ru", 2 * K * t + lo, 2 * K * t + hi)
            send(A("us", lo, hi) if end else un, [(nxt, ru)], [prv], [ru], 1024, "l")
        ts(mqv, pb, -HALF, ALU.add)
        mark("qv")
        tt(pb if how == "W" else vn, pb, mqv, ALU.subtract)
        mark("vn")
        if how == "W":
            tt(ge, pb, un, ALU.is_le)
            act(vn, pb)
        if k == 1 and "v" in OPT["early"][t]:
            ru = A("ru", 2 * K * t + K + lo, 2 * K * t + K + hi)
            send(vn, [(nxt, ru)], [prv], [ru], 1024, "l")
        if how == "V":
            tt(ge, pa, vn, ALU.is_ge)
        elif how == "S":
            mm(pa, [(idb, un)], True, False)
            mm(pa, [(idn, vn)], False)
            act(ge, pa, ACT.Sign, bias=1.0 / 512)
        yield
        pd = P(wb if apart else 5, 64 + 32 * c, 96 + 32 * c)
        mm(P(wb, 0, 64), [(idf, A("ff", 64 * c, 64 * c + 64))], True, False)
        wrap(P(wb, 0, 64), "q1", "gg", 2 * lo, 2 * lo + K, False)
        sg, t2 = A("sg", 32 * c, 32 * c + 32), A("t2", 32 * c, 32 * c + 32)
        act(sg, pn, ACT.Sign, bias=1.0 if how == "S" else 8.5, scale=-1.0)
        tt(t2, pd, sg, ALU.mult)
        if k == 1:
            tt(A("on", 32 * c, 32 * c + 32), pm, t2, ALU.is_ge)
        tt(f, pm, t2, ALU.subtract)
        if k == 0:
            ts(off, f, EDGE, ALU.add, float(NV), ALU.min)

    def moves(t):
        f, on, sc, sx = A("ff", 32, 96), A("on", 0, 64), A("sc", 16, 80), A("sc", 15, 79)
        scan(sc, on, on, 0.0, ALU.add, ALU.max)
        slot = lambda r: A("cin", 20 * t + 4 * r, 20 * t + 4 * r + 1)
        mm(P(4, 0, 1), [(blk, A("sc", 79, 80))])
        act(slot(rank), P(4, 0, 1))
        nv = 16 - OPT["accs"][t]
        shares = [(b, lo, hi) for b, lo, hi in ((0, 0, 8), (3, nv, 16), (2, 8, nv)) if lo < hi]
        for b, lo, hi in shares:
            mm(P(b, 0, 64 * (hi - lo)), [(idb, A("kt", 64 * lo, 64 * hi))], True, False)
            mms([(P(b, 64 * j, 64 * j + 64), A("blm", 0, 128), sc, False, j == hi - lo - 1) for j in range(hi - lo)])
        others = [r for r in range(n) if r != rank]
        send(slot(rank), [(T.cores[r], slot(rank)) for r in others], [T.cores[r] for r in others], [slot(r) for r in others], 4, "l")
        ops[-2]["follow"] = ghosted
        mm(P(5, 64, 128), [(blk, sx), (A("tri", 0, 128), on)])
        incl = A("cc", 0, 64)
        act(incl, P(5, 64, 128))
        for b, lo, hi in shares:
            if b == 3:
                for j in range(lo, hi):
                    act(A("sk", 64 * j, 64 * j + 63), P(b, 64 * (j - lo), 64 * (j - lo) + 63), ACT.Sigmoid, bias=-64.0, acc=A("sk", 64 * j + 63, 64 * j + 64))
            else:
                scan(A("sk", 64 * lo, 64 * hi), A("jt", 0, 64 * (hi - lo)), P(b, 0, 64 * (hi - lo)), 0.0, ALU.min, ALU.max)
        ek, cu = A("sk", 63, K, 64), A("cu", 0, 16)
        ts(cu, ek, 63.0, ALU.min)
        act(A("rr", 0, 16), ek, ACT.Relu, bias=1008.0, scale=-16.0)
        le = A("le", 0, 256)
        tt(le, G(incl, cu), A("kr", 0, 256), ALU.is_le)
        at = P(5, 0, 16)
        mm(at, [(idn, A("rr", 0, 16))], True, False)
        wrap(at, "q1", "le", 0, 256, False)
        atu = A("atu", 0, 16)
        ts(atu, at, 1008.0, ALU.add, K - 1.0, ALU.min)
        uv = UV[t + 1]
        utab = A(uv if t < 2 else "us", 0, VO)
        early, r0 = OPT["early"][t], 768 * t
        out = {x: A("snd", 256 * i, 256 * i + 256) for i, x in enumerate(OPT["parts"][t])}
        got = {x: A("rcv", r0 + 256 * i, r0 + 256 * i + 256) for i, x in enumerate(OPT["parts"][t])}
        ra = A("ra", 16 * t, 16 * t + 16)
        if early:
            send(atu, [(nxt, ra)], [prv], [ra], 32, "l")
            listed = len(ops) - 2
        vs = {} if t < 2 else {"bias": -0.25, "scale": 0.5}
        if "u" not in early:
            lin(OPT["su"], out["u"], G(A(uv if t < 2 else "us", 0, K), atu))
        if "v" not in early:
            lin(OPT["sv"], out["v"], G(A(uv, VO, VO + K), atu), **vs)
        act(A("fc", 0, 64), f, bias=(EDGE - 3328.0) / BIG, scale=1.0 / BIG)
        eq = P(4, 256, 512)
        mm(eq, [(A("st", 128, 256), A("one", 0, 256))], True, False)
        mm(eq, [(A("st", 0, 128), le)], False)
        act(A("eq", 0, 256), G(A("fc", 0, 64), cu))
        tt(out["f"], eq, A("eq", 0, 256), ALU.mult)
        cuts = OPT["cuts"][t]
        for lo, hi in zip(cuts, cuts[1:]):
            send(A("snd", lo, hi), [(nxt, A("rcv", r0 + lo, r0 + hi))], [prv], [A("rcv", r0 + lo, r0 + hi)], 2 * (hi - lo), "l")
            if OPT["inturn"]:
                ops[-2]["follow"] = len(ops) - 4 if lo > cuts[0] else listed
        if "u" in early:
            lin(OPT["su"], got["u"], G(A("ru", 2 * K * t, 2 * K * t + K), ra))
        if "v" in early:
            lin(OPT["sv"], got["v"], G(A("ru", 2 * K * t + K, 2 * K * t + 2 * K), ra), **vs)
        rk = P(4, 64, 128)
        mm(rk, [(blk, sx), (A("tr4", 0, 128), on), (idk, A("one", 0, 64))])
        wrap(P(4, 128, 132), "q1", "sc", 16, 80)
        ts(A("ro", 0, 4), P(4, 128, 132), 256.0, ALU.min)
        act(A("fk", 0, 64), incl, bias=col(12), scale=4096.0)
        m = A("mm", 4 * t, 4 * t + 1)
        cin = A("cin", 20 * t, 20 * t + 17, 4)
        add("v", lambda q: q.tensor_reduce(m["ap"], cin["ap"], AxisListType.X, ALU.min), COST["fix"] + 64 * cy, [cin], [m])
        shift, back = A("mm", 4 * t + 1, 4 * t + 2), A("mm", 4 * t + 2, 4 * t + 3)
        act(shift, m, bias=A("mm", 4 * t - 3, 4 * t - 2) if t else 0.25 - K)
        ts(A("e1", 0, 16), A("kw", 0, 16), m, ALU.subtract, 2048.0, ALU.mult)
        tt(A("e2", 0, 16), A("e1", 0, 16), A("kw", 16, 32), ALU.min)
        tt(A("e3", 0, 16), at, A("e2", 0, 16), ALU.max)
        asu = A("asu", 0, 16)
        ts(asu, A("e3", 0, 16), 1008.0, ALU.add)
        lo = 0 if t < 2 else 192
        si, sdf = P(1, 0, 192), A("sdf", lo, lo + 192)
        act(A("si", 0, 192), sdf, ACT.Sign, bias=shift)
        act(back, shift, bias=512.0)
        mm(si, [(idf, sdf)], True, False)
        if OPT["pre3"][t]:
            parts = [(144, 192, 24)] if t == 2 else [(48 * c + 36, 48 * c + 48, 12 * c) for c in range(t + 1)]
            mms([(P(1, lo, hi), idb, A("md", o, o + hi - lo), False, False) for lo, hi, o in parts])
        mm(si, [(A("id512", 0, 128), A("si", 0, 192))], False)
        ts(A("sl", 192 * t, 192 * t + 192), si, back, ALU.add, float(ZC), ALU.min)
        if t == 2:
            for c in range(2):
                lo, hi, pz = 512 * c, 512 * c + 512, P(2 * c, 0, 512)
                mm(pz, [(idh, A("one", 0, 512)), (idb, A(uv, VO + lo, VO + hi))])
                tt(A("zt", lo, hi), pz, A("us", lo, hi), ALU.mult)
                act(A("sig", lo, hi), A("zt", lo, hi), ACT.Sigmoid, scale=0.5)
        ts(A("lv", 0, 64), rk, m, ALU.is_ge, -8.0 * BIG, ALU.mult)
        tt(A("fl", 0, 64), A("lv", 0, 64), A("fk", 0, 64), ALU.add)
        if t < 2:
            prefill(t + 1)
        cp(G(utab, asu), got["u"])
        if t == 2:
            yield
        hold = P(7 if t < 2 else 4, 256, 512)
        mm(hold, [(idk, A("kr", 1, 257)), (A("st", 0, 128), le)], True, False)
        mm(hold, [(blk, got["f"])], False)
        scan(A("hs", 1, 257), hold, A("zz", 0, 256), -4.0 * BIG, ALU.max, ALU.add)
        if t < 2:
            rows(t + 1)
            cp(G(A(uv, VO, 2 * VO), asu), got["v"])
        else:
            o, z = G(A("sig", 0, VO), asu), A("zt", 0, 256)
            mm(P(4, 0, 256), [(idb, got["v"])])
            tt(z, P(4, 0, 256), got["u"], ALU.mult)
            add("s", lambda q: q.activation(o["ap"], z["ap"], ACT.Sigmoid), COST["fix"] + 256 * COST["sca"] * cy, [z], [o])
            act(A("sa", 0, 512), A("sig", 0, 512), scale=0.125)
        tt(A("t2", 0, 64), G(A("hs", 0, 257), A("ro", 0, 4)), A("fl", 0, 64), ALU.subtract)
        tt(f, A("t2", 0, 64), f, ALU.min)
        ts(A("fu", 0, 64), f, EDGE, ALU.add, float(NV if t < 2 else NW), ALU.min)

    def follower_lists(t):
        mm(P(7, 0, 96), [(idf, A("sf", 0, 96))], True, False)
        mm(P(7, 48, 96), [(sh("wz", i), A("dm", i, BL, 16)) for i in range(16)], False, False)
        for j, mat in ((0, "w0"), (1, "w1")):
            mm(P(7, 48 * j, 48 * j + 48), [(sh(mat, i), A("nnd", 4 * i + t, NV, 64)) for i in range(16)], False, j == 1)
        tt(A("nf", 0, 96), P(7, 0, 96), A("zc", 0, 96), ALU.min)
        ts(A("nl", 96 * t, 96 * t + 96), A("nf", 0, 96), 2.0, ALU.mult, float(t), ALU.add)
        if t < 2 and any(OPT["pre3"][t:2]):
            o = P(7, 128, 140)
            wrap(o, "q1", "dm", 576, BL)
            act(A("md", 12 * t, 12 * t + 12), o, bias=2048.0, scale=-128.0)
        if t < 2:
            ghosts(t)
            correct(t, 3)

    def ghosts(t):
        if t > 0:
            copy(A("w", NV, NW), A("gl", 512 * t - 512, 512 * t), 2048)
        for c in range(t):
            o = 128 * (t - 1 + c)
            lin(OPT["gr"], A("w", NV + c, NW, 4), A("gr", o, o + 128), scale=2.0)

    def live(b):
        for c in range(2):
            how = OPT["xl"][b][c]
            lo, hi = BL * b + 384 * c, BL * b + 384 * c + 384
            g = G(A("us", 0, SPARE), A("sl", 384 + lo // 16, 384 + hi // 16))
            if how == "V":
                tt(A("w", lo, hi), g, A("w", lo, hi), ALU.add)
                continue
            act(A("x", lo, hi), g)
            if how == "A":
                mm(P(4 + c, 0, 384), [(idb, A("x", lo, hi))])
                tt(A("w", lo, hi), P(4 + c, 0, 384), A("w", lo, hi), ALU.add)
            elif OPT["xl"][b] != "DD":
                dadd(A("w", lo, hi), A("x", lo, hi))
        if OPT["xl"][b] == "DD":
            dadd(A("w", BL * b, BL * b + BL), A("x", BL * b, BL * b + BL))

    yh = {"ap": T.yh[:], "reg": [("yh", 0, BL, 1)], "n": BL}

    def total(b):
        for j, c in enumerate(OPT["sums"]):
            mm(P(6 + j // 2, 192 * (j % 2), 192 * (j % 2) + 192), [(idf, A("w", BL * b + c, BL * b + BL, 4))], b == 3 and j % 2 == 0, b == 0 and j % 2 == 1)

    def heights(t):
        parts = OPT["xparts"][t]
        for k in range(parts - 1, -1, -1):
            m = 48 // parts
            for c in range(4):
                if c != t + 1:
                    o = 192 * t + 48 * c + m * k
                    lin(OPT["xc"][t][c], A("x", 64 * m * k + c, 64 * m * (k + 1), 4), G(A(UV[t + 1], 0, SPARE), A("sl", o, o + m)),
                        bias=-2.0 ** (t + 1), scale=2.0 ** (t + 2))
        cuts = OPT["dcuts"][t]
        for hi, lo in zip(cuts, cuts[1:]):
            dadd(A("w", BL * lo, BL * hi), A("x", BL * lo, BL * hi))
        gl = A("gl", 512 * t, 512 * t + 512)
        send(A("w", 0, 512), [(prv, gl)], [nxt], [gl], 2048, "k", True)
        for b in range(2 if OPT["pre3"][t] else 3, -1, -1):
            correct(t, b)
        gr = A("gr", 128 * t, 256 * t + 128)
        send(A("gs", 128 * t, 256 * t + 128), [(prv, gr)], [nxt], [gr], 512 * (t + 1), "k")

    def factors(b):
        for c in range(3):
            mm(P(2 - 2 * (b % 2) + c // 2, 192 * (c % 2), 192 * (c % 2) + 192), [(idb, A("b", BL * b + c, BL * b + BL, 4))])

    def last(b):
        win = A("w", BL * b, WZ)
        for c in OPT["turn"]:
            o = 96 * c + 12 * b
            act(A("h1", 192 * c, 192 * c + 192), G(win, A("nl", 48 + o, 60 + o)))
            tt(A("p2", 192 * c, 192 * c + 192), G(win, A("nl", o, o + 12)), A("ah", BL * b + c, BL * b + BL, 4), ALU.mult)
        done, hows = [], OPT["last"][b]
        for cs in ((0, 1), (2,)) if hows[:2] == "MM" else ((2,), (1,), (0,)):
            how, k = hows[cs[0]], 192 * len(cs)
            lo = 192 * cs[0]
            factor = P(2 - 2 * (b % 2) + cs[0] // 2, lo % 384, lo % 384 + k)
            out = P(3 + cs[0], 0, k) if how == "P" else factor
            if how == "P":
                mm(out, [(idb, A("zz", 0, k))], True, False)
            tt(out, factor, A("h1", lo, lo + k), ALU.mult)
            if how == "P":
                mm(out, [(idf, A("p2", lo, lo + k))], False)
            done += [(how, c, A("ps", out["reg"][0][1] + 192 * i, out["reg"][0][1] + 192 * i + 192)) for i, c in enumerate(cs)]
        for how, c, x in done:
            o = A("w", BL * b + c, BL * b + BL, 4)
            if how == "P":
                act(o, x)
            else:
                tt(o, x, A("p2", 192 * c, 192 * c + 192), ALU.add)

    def correct(t, b):
        win = A("w", BL * b, WZ)
        m = 128 if b == 0 and t < 2 else 192
        hows = OPT["corr"][t][b]
        k = m * (t + 1)
        i0 = 512 * 6
        work = []
        for c in range(t + 1):
            lo, hi = BL * b + c, BL * b + 4 * m
            l0 = A("nl", 96 * c + 12 * b, 96 * c + 12 * b + m // 16)
            l1 = A("nl", 48 + 96 * c + 12 * b, 48 + 96 * c + 12 * b + m // 16)
            h1, p2 = (A(x, m * c, m * c + m) for x in ("h1", "p2"))
            pa = A("ps", i0 + m * c, i0 + m * c + m)
            mm(pa, [(idb, A("b", lo, hi, 4))])
            act(h1, G(win, l1))
            tt(p2, G(win, l0), A("ah", lo, hi, 4), ALU.mult)
            work.append((hows[c], A("w", lo, hi, 4), pa, h1, p2))
        both = A("ps", i0, i0 + k)
        if t < 2 and b == 0:
            tt(both, both, A("h1", 0, k), ALU.mult)
            tt(A("gs", 128 * t, 128 * t + k), both, A("p2", 0, k), ALU.add)
        elif "M" in hows:
            tt(both, both, A("h1", 0, k), ALU.mult)
            for how, o, pa, h1, p2 in work:
                tt(o, pa, p2, ALU.add)
        elif t < 2 and "P" in hows:
            mm(P(7, 0, k), [(idb, A("zz", 0, k))], True, False)
            tt(P(7, 0, k), both, A("h1", 0, k), ALU.mult)
            mm(P(7, 0, k), [(idf, A("p2", 0, k))], False)
            for c, (how, o, pa, h1, p2) in enumerate(work):
                act(o, P(7, m * c, m * c + m))
        else:
            for how, o, pa, h1, p2 in work:
                tt(pa, pa, h1, ALU.mult)
            for how, o, pa, h1, p2 in work:
                tt(o, pa, p2, ALU.add)

    def outputs():
        win = A("w", 0, NW)
        act(A("hb", 0, 512), G(win, A("fu", 32, 64)), scale=0.125)
        tt(A("pa", 0, 512), G(win, A("fu", 0, 32)), A("sa", 0, 512), ALU.mult)
        z = P(0, 0, 512)
        tt(z, z, A("hb", 0, 512), ALU.mult)
        tt(A("ow", 0, 512), z, A("pa", 0, 512), ALU.add)
        for j, c in enumerate(OPT["sums"]):
            act(A("oh", c, BL, 4), P(6 + j // 2, 192 * (j % 2), 192 * (j % 2) + 192), scale=0.125)
        copy({"ap": T.yw[:], "reg": [("yw", 0, 512, 1)]}, A("ow", 0, 512), 2048)
        copy(yh, A("oh", 0, BL), 3072, OPT["store"])

    lists(0)
    prefill(0)
    rows(0)
    for t in range(3):
        collapse(t)
        fill[0] = True
        if t == 0:
            for c in range(1, 4):
                lists(c)
        if t > 0:
            heights(t - 1)
        follower_lists(t)
        fill[0] = False
        for k in range(2):
            halves = [hop(t, k, c) for c in range(2)]
            for _ in range(2):
                for x in halves:
                    next(x, None)
        rest = moves(t)
        next(rest, None)
    ghosts(2)
    factors(3)
    factors(2)
    if OPT["pre3"][2]:
        last(3)
        factors(1)
    for b in range(3, -1, -1):
        live(b)
    for b in range(3, -1, -1):
        if b == OPT["rest"]:
            next(rest, None)
        if b < 3 or not OPT["pre3"][2]:
            last(b)
            if b > 1:
                factors(b - 2)
        if b == 1:
            act(P(0, 0, 512), A("sig", 512, K))
        total(b)
    outputs()
    return ops


def depend(ops):
    hist = {}
    for j, op in enumerate(ops):
        wait, order = set(), set()
        if op["kind"] == "recv":
            order.add(op["after"])
        if "follow" in op:
            order.add(op["follow"])
        acc = [(r, False) for r in op["rd"]] + [(r, True) for r in op["wr"]]
        for (name, lo, hi, st), wr in acc:
            for lo2, hi2, st2, i, wr2 in hist.get(name, []):
                o = ops[i]
                same = o["eng"] == op["eng"] and o["kind"] == "c" and op["kind"] == "c"
                if name == "ps" and not same:
                    if lo // 512 <= (hi2 - 1) // 512 and lo2 // 512 <= (hi - 1) // 512:
                        wait.add(i)
                elif lo < hi2 and lo2 < hi and (wr or wr2) and (lo - lo2) % math.gcd(st, st2) == 0:
                    (order if same and op.get("adds") else wait).add(i)
                elif name == "ps" and op["eng"] == "p" and lo // 512 == lo2 // 512:
                    order.add(i)
        for (name, lo, hi, st), wr in acc:
            hist.setdefault(name, []).append((lo, hi, st, j, wr))
        if op["kind"] == "recv":
            wait = set()
        op["wait"], op["order"] = wait, order - wait


def graph(ops):
    pred = []
    for op in ops:
        p = {i: 0.0 for i in op["order"]}
        if op["kind"] == "recv":
            p[op["after"]] = ops[op["after"]]["lead"]
        for i in op["wait"]:
            near = ops[i]["eng"] == op["eng"]
            p[i] = ops[i].get("lat", 0.0) + (COST["own"] if near else COST["lat"])
        pred.append(p)
    far = []
    for j, p in enumerate(pred):
        reach = {}
        for i in sorted(p, reverse=True):
            if reach.get(i, -1.0) >= p[i]:
                del p[i]
                continue
            reach[i] = p[i]
            for h, x in far[i].items():
                reach[h] = max(reach.get(h, -1.0), x + ops[i]["dur"] + p[i])
        far.append(reach)
    return pred


def place(eng, dur, pred, succ, pri, rel):
    n = len(eng)
    left = [len(p) for p in pred]
    ready = sorted((pri[j], j) for j in range(n) if left[j] == 0)
    start, can = [0.0] * n, list(rel)
    busy = {e: ([], []) for e in "vspgylk"}
    while ready:
        j = ready.pop()[1]
        t, d = can[j], dur[j]
        if eng[j] is not None:
            a, b = busy[eng[j]]
            m = len(a)
            lo, hi = 0, m
            while lo < hi:
                mid = (lo + hi) // 2
                if b[mid] > t:
                    hi = mid
                else:
                    lo = mid + 1
            while lo < m and t + d > a[lo] + 1e-6:
                t = b[lo]
                lo += 1
            a.insert(lo, t)
            b.insert(lo, t + d)
        start[j] = t
        t += d
        for s, x in succ[j].items():
            if can[s] < t + x:
                can[s] = t + x
            left[s] -= 1
            if left[s] == 0:
                x = (pri[s], s)
                if not ready or x >= ready[-1]:
                    ready.append(x)
                else:
                    ready.append(x)
                    ready.sort()
    return start


def schedule(ops, rng):
    n = len(ops)
    pred = graph(ops)
    succ = [{} for _ in range(n)]
    for j in range(n):
        for i, d in pred[j].items():
            succ[i][j] = d
    eng, dur = [o["eng"] for o in ops], [o["dur"] + 1e-3 for o in ops]
    tail = [o.get("lat", 0.0) for o in ops]
    chain = [0.0] * n
    for j in range(n - 1, -1, -1):
        chain[j] = dur[j] + max([chain[s] + d for s, d in succ[j].items()] + [tail[j]])
    seeds = [[chain[j] - (x if ops[j]["fill"] else 0.0) for j in range(n)] for x in OPT["later"]]
    main = [j for j in range(n) if not ops[j]["fill"]]
    start = anneal(eng, dur, pred, succ, [0.0] * n, tail, seeds, main, OPT["passes"], OPT["pull"], OPT["warm"], rng)
    for _ in range(OPT["sweeps"]):
        lo = -float(rng.random()) * OPT["wide"]
        while lo < max(start):
            seq = sorted(range(n), key=lambda j: (start[j], j))
            rest, behind, free = [0.0] * n, {}, {}
            for j in reversed(seq):
                rest[j] = dur[j] + max([rest[s] + d for s, d in succ[j].items()] + [tail[j], behind.get(eng[j], 0.0)])
                if start[j] >= lo + OPT["wide"]:
                    behind[eng[j]] = rest[j]
            part = [j for j in seq if lo <= start[j] < lo + OPT["wide"]]
            for j in seq:
                if start[j] < lo:
                    free[eng[j]] = start[j] + dur[j]
            at = {j: k for k, j in enumerate(part)}
            if len(part) > 1:
                rel = [max([start[i] + dur[i] + d for i, d in pred[j].items() if i not in at] + [free.get(eng[j], 0.0)]) for j in part]
                end = [max([rest[s] + d for s, d in succ[j].items() if s not in at] + [tail[j], behind.get(eng[j], 0.0)]) for j in part]
                new = anneal([eng[j] for j in part], [dur[j] for j in part], [{at[i]: d for i, d in pred[j].items() if i in at} for j in part],
                             [{at[i]: d for i, d in succ[j].items() if i in at} for j in part], rel, end, [[-start[j] for j in part]],
                             [k for k, j in enumerate(part) if not ops[j]["fill"]] or [0], OPT["tries"], OPT["near"], OPT["cool"], rng)
                seq = [j for j in seq if start[j] < lo] + sorted(part, key=lambda j: (new[at[j]], j)) + [j for j in seq if start[j] >= lo + OPT["wide"]]
                free = {}
                for j in seq:
                    start[j] = max([start[i] + dur[i] + d for i, d in pred[j].items()] + [free.get(eng[j], 0.0)])
                    free[eng[j]] = start[j] + dur[j]
            lo += 0.5 * OPT["wide"]
    seq = sorted(range(n), key=lambda j: (start[j], j))
    order = {e: [j for j in seq if eng[j] == e] for e in "vspgylk"}
    return order, start, [start[j] + dur[j] + tail[j] for j in range(n)]


def anneal(eng, dur, pred, succ, zero, tail, seeds, main, passes, pull, warm, rng):
    n = len(eng)
    best = cur = None

    def queued(start):
        ends = {(eng[j], round(start[j] + dur[j])): j for j in range(n)}
        j = max(range(n), key=lambda x: start[x] + dur[x] + tail[x])
        pairs = []
        while j is not None:
            by = [i for i, d in pred[j].items() if abs(start[i] + dur[i] + d - start[j]) < 0.5]
            if by:
                j = by[int(rng.integers(len(by)))]
            else:
                i = ends.get((eng[j], round(start[j])))
                if i is not None:
                    pairs.append((i, j))
                j = i
        return pairs

    for it in range(passes):
        if it >= len(seeds) and cur[2] is None:
            cur[2] = queued(cur[1])
        if it < len(seeds):
            pri = seeds[it]
        elif cur[2] and float(rng.random()) < OPT["aim"]:
            pri = [-x for x in cur[1]]
            for _ in range(int(rng.integers(1, 3))):
                a, b = cur[2][int(rng.integers(len(cur[2])))]
                gain = (cur[1][b] - cur[1][a] + 1.0) * (1.0 + 3.0 * float(rng.random()) ** 2)
                if float(rng.random()) < 0.5:
                    todo, edge, sign = [b], pred, 1.0
                else:
                    todo, edge, sign = [a], succ, -1.0
                seen, t0 = set(todo), cur[1][todo[0]]
                for j in todo:
                    pri[j] += sign * gain
                    for i in edge[j]:
                        if i not in seen and abs(cur[1][i] - t0) < OPT["reach"]:
                            seen.add(i)
                            todo.append(i)
        else:
            shake = (rng.random(n) * OPT["noise"] * float(rng.random()) ** 2).tolist()
            lo = min(cur[1]) + float(rng.random()) * (max(cur[1]) - min(cur[1])) - 0.5 * OPT["span"]
            pri = [(shake[j] if lo <= cur[1][j] < lo + OPT["span"] else 0.0) - cur[1][j] for j in range(n)]
        start = place(eng, dur, pred, succ, pri, zero)
        for _ in range(3 if it < len(seeds) > 1 else int(it % OPT["every"] == 1)):
            back = place(eng, dur, succ, pred, [start[j] + dur[j] for j in range(n)], tail)
            start = place(eng, dur, pred, succ, [back[j] + dur[j] for j in range(n)], zero)
        end = max(start[j] + dur[j] + tail[j] for j in range(n)) + pull * sum(start[j] for j in main) / len(main)
        if best is None or end < best[0]:
            best = (end, start)
        if cur is None or end <= cur[0] + warm * (1.0 - it / passes) * (it >= len(seeds)):
            cur = [end, start, None]
    return best[1]


def steady(eng, cases, start, rng, rounds):
    n, many = len(eng), range(len(cases))
    seq = sorted(range(n), key=lambda j: (start[j], j))
    into = [[[(i, d + dur[i]) for i, d in p.items()] for p in pred] for dur, pred, tail in cases]
    out = [[[] for _ in range(n)] for _ in cases]
    for c in many:
        for j in range(n):
            for i, d in cases[c][1][j].items():
                out[c][i].append((j, d))
    pred0, succ0 = cases[0][1], [[j for j, d in x] for x in out[0]]
    first, wide, steps, pull = [], OPT["part"], OPT["steps"], OPT["mean"] / n

    def links(part):
        before, last = {}, {}
        for j in part:
            before[j] = last.get(eng[j], -1)
            last[eng[j]] = j
        return before

    def times(c, part, before, old=None, lo=0):
        dur, rel, end, edges = sets[c]
        head, best = (dict(old[1]), old[3][:lo + 1]) if old else ({}, [(0.0, -1)])
        last, at = best[-1]
        for j in part[lo:]:
            t = rel[j]
            i = before[j]
            if i >= 0:
                x = head[i] + dur[i]
                if x > t:
                    t = x
            for i, d in edges[j]:
                x = head[i] + d
                if x > t:
                    t = x
            head[j] = t
            t += end[j]
            if t > last:
                last, at = t, j
            best.append((last, at))
        return last + pull * sum(head.values()), head, at, best

    def queued(c, now, before):
        dur, rel, end, edges = sets[c]
        _, head, j, _ = now[c]
        pairs = []
        while head[j] > rel[j]:
            by = [i for i, d in edges[j] if head[i] + d > head[j] - 1e-3]
            if not by and before[j] not in pred0[j]:
                pairs.append((before[j], j))
            j = by[0] if by else before[j]
        return pairs

    for turn in range(rounds + 1):
        heat = OPT["heat"] * (1.0 - turn / max(rounds, 1))
        heads, frees, rests = [[0.0] * n for _ in many], [{} for _ in many], [[0.0] * n for _ in many]
        for c in many:
            (dur, pred, tail), rest, behind = cases[c], rests[c], {}
            for j in reversed(seq):
                rest[j] = behind[eng[j]] = dur[j] + max([rest[i] + d for i, d in out[c][j]] + [tail[j], behind.get(eng[j], 0.0)])
        if turn == rounds:
            return sum(math.log(max(rest)) for rest in rests), seq
        done = 0
        for lo in range(-int(rng.integers(wide // 2)), n - wide // 2, wide // 2):
            lo, hi = max(lo, 0), min(lo + wide, n)
            part, sets = seq[lo:hi], []
            inside, then = set(part), {eng[j]: j for j in reversed(seq[hi:])}
            for c in many:
                (dur, pred, tail), head, free, rest = cases[c], heads[c], frees[c], rests[c]
                for j in seq[done:lo]:
                    head[j] = max([head[i] + d for i, d in into[c][j]] + [free.get(eng[j], 0.0)])
                    free[eng[j]] = head[j] + dur[j]
                rel = {j: max([head[i] + d for i, d in into[c][j] if i not in inside] + [free.get(eng[j], 0.0)]) for j in part}
                end = {j: dur[j] + max([rest[i] + d for i, d in out[c][j] if i not in inside] + [tail[j], rest[then[eng[j]]] if eng[j] in then else 0.0])
                       for j in part}
                sets.append((dur, rel, end, {j: [(i, d) for i, d in into[c][j] if i in inside] for j in part}))
            done = lo
            before = links(part)
            now = [times(c, part, before) for c in many]
            first = first or [x[0] for x in now]
            cur = sum(x[0] / f for x, f in zip(now, first))
            best, pairs = (cur, part), [None] * len(cases)
            for c, u, w, far, z in zip(rng.integers(len(cases), size=steps).tolist(), rng.random(steps).tolist(), rng.random(steps).tolist(),
                                       rng.geometric(OPT["short"], steps).tolist(), rng.exponential(1.0, steps).tolist()):
                if pairs[c] is None:
                    pairs[c] = queued(c, now, before)
                if not pairs[c]:
                    continue
                a, b = pairs[c][int(u * len(pairs[c]))]
                ahead, y = w < 0.5, part.index(b)
                for _ in range(far - 1):
                    if ahead:
                        a = before[a] if before[a] >= 0 else a
                    else:
                        y = next((k for k in range(y + 1, len(part)) if eng[part[k]] == eng[b]), y)
                b, x = part[y], part.index(a)
                mid, take = part[x:y + 1], {b if ahead else a}
                for j in reversed(mid) if ahead else mid:
                    if not take.isdisjoint(succ0[j] if ahead else pred0[j]):
                        take.add(j)
                if a in take and b in take:
                    continue
                new = part[:x] + [j for j in mid if (j in take) == ahead] + [j for j in mid if (j in take) != ahead] + part[y + 1:]
                after = links(new)
                one = times(c, new, after, now[c], x)
                if (one[0] - now[c][0]) / first[c] > heat * z + OPT["give"]:
                    continue
                res = [one if k == c else times(k, new, after, now[k], x) for k in many]
                x = sum(r[0] / f for r, f in zip(res, first))
                if x <= cur + heat * z:
                    part, before, now, cur, pairs = new, after, res, x, [None] * len(cases)
                    if x < best[0]:
                        best = (x, part)
            seq[lo:hi] = best[1]


def plan(ops, T, topo, core):
    keep, cases = dict(COST), []
    for case in CASES:
        COST.update(case)
        like = build(T, topo, core)
        for o, p in zip(like, ops):
            o["wait"], o["order"] = p["wait"], p["order"]
        cases.append(([o["dur"] + 1e-3 for o in like], graph(like), [o.get("lat", 0.0) for o in like]))
        COST.update(keep)
    eng, rng = [o["eng"] for o in ops], numpy.random.default_rng(OPT["seed"])
    seq = min(steady(eng, cases, schedule(ops, rng)[1], rng, OPT["rounds"][0]) for _ in range(OPT["starts"]))[1]
    seq = steady(eng, cases, {j: k for k, j in enumerate(seq)}, rng, OPT["rounds"][1])[1]
    return {j: k for k, j in enumerate(seq)}


PLAN = {}


def rank_program(g, core, T, topo):
    if T.rank_of(core) is None:
        return
    ops = build(T, topo, core)
    depend(ops)
    if "order" not in PLAN:
        PLAN["order"] = plan(ops, T, topo, core)
    start = PLAN["order"]
    order = {e: sorted((j for j in start if ops[j]["eng"] == e), key=start.get) for e in "vspgy"}
    queue = {"v": g.vector, "s": g.scalar, "p": g.tensor, "g": g, "y": g.sync}
    total = {}
    for e in "vspg":
        k = 0
        for j in order[e]:
            if ops[j]["kind"] == "c":
                k += 1
                ops[j]["sem"], ops[j]["cnt"] = COUNTER[e], k
    for op in ops:
        total[op["sem"]] = max(total.get(op["sem"], 0), op["cnt"])
    known = {e: {} for e in "vspgy"}
    for j in sorted(range(len(ops)), key=lambda x: (start[x], x)):
        op = ops[j]
        if op["kind"] == "recv":
            op["clock"] = {}
            continue
        seen = known[op["eng"]]
        op["waits"] = []
        for i in sorted(op["wait"], key=lambda x: -start[x]):
            o = ops[i]
            if seen.get(o["sem"], 0) < o["cnt"]:
                op["waits"].append((o["sem"], o["cnt"]))
                seen[o["sem"]] = o["cnt"]
                for s, c in o["clock"].items():
                    seen[s] = max(seen.get(s, 0), c)
        op["clock"] = dict(seen)
    for e in "yvspg":
        q = queue[e]
        for j in order[e]:
            op = ops[j]
            for s, c in op["waits"]:
                q.wait_ge(T.sem[s], c)
            ins = op["fn"](q)
            if op["kind"] == "c":
                ins.then_inc(T.sem[op["sem"]], 1)
            elif op["kind"] == "dma":
                ins.then_inc(T.sem[op["sem"]], 16)
    done = {op["sem"]: start[j] for j, op in sorted(enumerate(ops), key=lambda x: start[x[0]])}
    for s in sorted(total, key=done.get):
        if known["g"].get(s, 0) < total[s]:
            g.wait_ge(T.sem[s], total[s])
